import numpy as np
import ml_dtypes


def mxq(x, axis, fmt="e4m3"):
    dtype, down = {"e4m3": (ml_dtypes.float8_e4m3fn, 7), "e5m2": (ml_dtypes.float8_e5m2, 14)}[fmt]
    v = np.moveaxis(np.asarray(x, np.float32).astype(ml_dtypes.bfloat16).astype(np.float64), axis, -1)
    blocks = v.reshape(v.shape[:-1] + (-1, 32))
    amax = np.abs(blocks).max(-1, keepdims=True)
    byte = np.maximum(np.where(amax > 0, np.frexp(amax)[1] - 1 + 127, 0) - down, 1)
    scale = np.exp2(byte - 127.0)
    codes = (blocks / scale).astype(np.float32).astype(dtype).astype(np.float64)
    return np.moveaxis((codes * scale).reshape(v.shape), -1, axis)


WIDE = False


def mx_kscale(k):
    if not WIDE:
        return np.ones(k)
    levels = np.array([30, -30])
    if k % 512:
        return np.exp2(np.random.permutation(np.resize(levels, k // 32))).repeat(32)
    a = np.empty((k // 512, 16))
    for p in range(k // 512):
        a[p, :8] = np.random.permutation(np.resize(levels, 8))
        for g in range(8):
            far = levels[np.abs(levels - a[p, g]) >= 10]
            a[p, g + 8] = far[np.random.randint(len(far))]
    return np.exp2(a.ravel()).repeat(32)


def f64(x):
    return np.asarray(x).astype(np.float64)


def striped8(idx):
    return np.concatenate([v.reshape(-1, 16).T for v in idx]).astype(np.uint16)


def unstriped8(offs):
    return np.stack([offs[16 * g:16 * g + 16].T.reshape(-1) for g in range(8)]).astype(np.int64)


E2M1 = np.array([0.0, 0.5, 1.0, 1.5, 2.0, 3.0, 4.0, 6.0, -0.0, -0.5, -1.0, -1.5, -2.0, -3.0, -4.0, -6.0])


def pack_weight(w, fmt):
    k, n = w.shape
    w = f64(np.asarray(w, np.float32).astype(ml_dtypes.bfloat16)).reshape(k // 32, 32, n)
    amax = np.abs(w).max(1)
    if fmt == "e4m3":
        byte = np.frexp(amax)[1] - 1 + 127 - 7
    else:
        mant, ex = np.frexp(amax / 6.0)
        byte = np.where(mant > 0.5, ex, ex - 1) + 127
    byte = np.clip(np.where(amax > 0, byte, 1), 1, 254)
    scaled = (w * np.exp2(127.0 - byte)[:, None, :]).reshape(k, n).astype(np.float32)
    by_word = np.ascontiguousarray(scaled.reshape(k // 512, 128, 4, n).transpose(0, 1, 3, 2))
    if fmt == "e4m3":
        words = by_word.astype(ml_dtypes.float8_e4m3fn).view(np.uint8)
    else:
        c = by_word.astype(ml_dtypes.float4_e2m1fn).view(np.uint8) & 0xF
        words = (c[..., 0::2] | (c[..., 1::2] << 4)).reshape(k // 512, 128, 2 * n)
    return np.ascontiguousarray(words), np.ascontiguousarray(byte.astype(np.uint8).reshape(k // 512, 16, n))


def unpack_weight(words, scales, fmt):
    g, _, n = scales.shape
    words = np.ascontiguousarray(words).reshape(g, 128, n, -1)
    if fmt == "e4m3":
        vals = words.view(ml_dtypes.float8_e4m3fn).astype(np.float64)
    else:
        nib = np.empty((g, 128, n, 4), np.uint8)
        nib[..., 0::2] = words & 0xF
        nib[..., 1::2] = words >> 4
        vals = E2M1[nib]
    vals = vals * np.repeat(np.exp2(scales.astype(np.float64) - 127.0), 8, axis=1)[..., None]
    return vals.transpose(0, 1, 3, 2).reshape(g * 512, n)


K, N, T, J = 512, 512, 2048, 1024


def setup_inputs():
    n = np.random.standard_normal
    s = mx_kscale(K)[:, None]
    m = np.exp(0.5 * n((1, J)))
    p_w = pack_weight(n((K, N)) / np.sqrt(K) / s, "e2m1")
    return {
        "dy": (m * n((K, J)) * s).astype(np.float32),
        "w_words": p_w[0],
        "w_scales": p_w[1],
        "d": (0.5 + 0.3 * n((N, J))).astype(np.float32),
        "wgo": np.repeat(np.random.uniform(0.5, 2.0, (8, J)), 16, axis=0).astype(np.float32),
        "offs": striped8(np.stack([np.random.permutation(T)[:J] for _ in range(8)])),
    }


def reference(dy, w_words, w_scales, d, wgo, offs):
    idx = unstriped8(offs)
    dy_q_ = mxq(f64(dy), 0, "e5m2")
    dy_r_ = mxq(f64(dy) - dy_q_, 0, "e4m3")
    w_ = unpack_weight(w_words, w_scales, "e2m1")
    dx = w_.T @ dy_q_ + w_.T @ dy_r_
    out = np.zeros((N, T))
    rows = np.arange(N)
    out[rows[:, None], idx[rows % 128 // 16]] = f64(wgo)[rows % 128] * (dx * f64(d))
    return out

@@ -1,0 +1,238 @@
+from contextlib import ExitStack
+
+import concourse.mybir as mybir
+
+K, N, T, J = 512, 512, 2048, 1024
+FLOPS = 3 * 2 * K * N * J
+
+F32 = mybir.dt.float32
+BF16 = mybir.dt.bfloat16
+I32 = mybir.dt.int32
+U32 = mybir.dt.uint32
+U16 = mybir.dt.uint16
+U8 = mybir.dt.uint8
+E4M3 = mybir.dt.float8_e4m3fn_x4
+E5M2 = mybir.dt.float8_e5m2_x4
+E2M1 = mybir.dt.float4_e2m1fn_x4
+ALU = mybir.AluOpType
+COPY = mybir.ActivationFunctionType.Copy
+
+P = 128
+PACK = 4
+HALF = 512
+PIECE = 256
+GROUPS = 8
+BLOCKS = N // P
+TILES = HALF // P
+CAST_V = 160
+WEAVE_V = 352
+
+
+def weave(copy, dst, src, j0, j1):
+    copy(
+        out=dst[:, j0:j1, :].rearrange("p (c i) t -> p c t i", i=4),
+        in_=src[:, :, j0:j1].rearrange("p t (c i) -> p c t i", i=4),
+    )
+
+
+def tile_list_embg_tgq4_mul_kernel(tc, dy, w_words, w_scales, d, wgo, offs, out):
+    nc = tc.nc
+    with ExitStack() as ctx:
+        keep = ctx.enter_context(tc.tile_pool(name="keep", bufs=1))
+        psum = ctx.enter_context(tc.psum_pool(name="psum", bufs=1))
+
+        def sb(name, shape, dtype, tag=None):
+            return keep.tile(shape, dtype, name=name, tag=tag or name, align_bytes=64)
+
+        def bank(name, index):
+            return psum.tile([P, HALF], F32, name=name, tag="bank%d" % index)
+
+        offsets = keep.tile([P, J // 16], U16, name="offsets")
+        dy_view = dy.rearrange("(p t) j -> p t j", t=PACK)
+        d_view = d.rearrange("(b p) j -> p b j", p=P)
+        raw = [sb("raw%d" % h, [P, 2, PACK, PIECE], F32) for h in range(2)]
+        for h in range(2):
+            for c in range(2):
+                j0 = h * HALF + c * PIECE
+                nc.sync.dma_start(out=raw[h][:, c, :, :], in_=dy_view[:, :, j0 : j0 + PIECE])
+        w_codes = sb("w_codes", [P, 2 * N], U8)
+        w_plane = sb("w_plane", [P, N], U8)
+        nc.vector.memset(w_plane[:].bitcast(I32), 0)
+        nc.sync.dma_start(out=w_codes[:].bitcast(I32), in_=w_words[0].bitcast(I32))
+        for q in range(4):
+            nc.sync.dma_start(
+                out=w_plane[32 * q : 32 * q + 4, :].bitcast(I32), in_=w_scales[0, 4 * q : 4 * q + 4, :].bitcast(I32)
+            )
+        gate = [sb("gate%d" % h, [P, HALF], F32) for h in range(2)]
+        d_first = sb("d_first", [P, HALF], F32, tag="slot1")
+        d_rest = sb("d_rest", [P, BLOCKS - 1, HALF], F32)
+        d_second = sb("d_second", [P, BLOCKS, HALF], F32)
+        nc.sync.dma_start(out=gate[0][:], in_=wgo[:, 0:HALF])
+        nc.sync.dma_start(out=d_first[:], in_=d_view[:, 0, 0:HALF])
+        nc.sync.dma_start(offsets[:], offs)
+        nc.sync.dma_start(out=d_rest[:], in_=d_view[:, 1:BLOCKS, 0:HALF])
+        nc.sync.dma_start(out=gate[1][:], in_=wgo[:, HALF:J])
+        nc.sync.dma_start(out=d_second[:], in_=d_view[:, :, HALF:J])
+
+        diag = sb("diag", [P, HALF + 16], BF16)
+        nc.vector.memset(diag[:], 0.0)
+        nc.gpsimd.affine_select(
+            out=diag[:], in_=diag[:], pattern=[[1, HALF + 16]], compare_op=ALU.not_equal, fill=1.0,
+            base=-3, channel_multiplier=-4,
+        )
+        eye = sb("eye", [P, P], F32)
+        nc.scalar.activation(out=eye[:], in_=diag[:, 3 : 3 + HALF : 4], func=COPY)
+        eye_in = sb("eye_in", [P, PACK, HALF], BF16)
+        for t in range(PACK):
+            nc.vector.tensor_copy(out=eye_in[:, t, :], in_=diag[:, 3 - t : 3 - t + HALF])
+        eye_codes = sb("eye_codes", [P, HALF], U32)
+        eye_plane = sb("eye_plane", [P, HALF], U8)
+        nc.vector.quantize_mx(
+            out=eye_codes[:].bitcast(E4M3), scales=eye_plane[:], in_=eye_in[:].rearrange("p t c -> p (t c)")
+        )
+
+        q_codes = [sb("q_codes%d" % h, [P, HALF], U32) for h in range(2)]
+        q_plane = [sb("q_plane%d" % h, [P, HALF], U8) for h in range(2)]
+        r_codes = [sb("r_codes%d" % h, [P, HALF], U32) for h in range(2)]
+        r_plane = [sb("r_plane%d" % h, [P, HALF], U8) for h in range(2)]
+        gate_t = [sb("gate_t%d" % h, [P, TILES, GROUPS], F32) for h in range(2)]
+
+        def quantise(codes, plane, fmt, src, j0, j1):
+            nc.vector.quantize_mx(
+                out=codes[:, j0:j1].bitcast(fmt), scales=plane[:, j0:j1], in_=src.rearrange("p j t -> p (j t)")
+            )
+
+        def decode(h, t, acc):
+            cols = slice(t * P, (t + 1) * P)
+            nc.tensor.matmul_mx(
+                out=acc[:], lhsT=eye_codes[:, cols].bitcast(E4M3), lhsT_scale=eye_plane[:, cols],
+                rhs=q_codes[h][:].bitcast(E5M2), rhs_scale=q_plane[h][:], start=True, stop=True,
+            )
+
+        def leftover(h, t, acc, rest):
+            nc.vector.tensor_tensor(
+                out=rest[:, t, :].rearrange("p (c j) -> p c j", c=2), in0=raw[h][:, :, t, :],
+                in1=acc[:].rearrange("p (c j) -> p c j", c=2), op=ALU.subtract,
+            )
+
+        def turned_pass(codes, plane, fmt, u, acc, first):
+            cols = slice(u * P, (u + 1) * P)
+            nc.tensor.matmul_mx(
+                out=acc[:], lhsT=codes[:, cols].bitcast(fmt), lhsT_scale=plane[:, cols],
+                rhs=w_codes[:].bitcast(E2M1), rhs_scale=w_plane[:], start=first, stop=not first,
+            )
+
+        def direct_pass(codes, plane, fmt, acc, first):
+            nc.tensor.matmul_mx(
+                out=acc[:], lhsT=w_codes[:, 0 : 2 * P].bitcast(E2M1), lhsT_scale=w_plane[:, 0:P],
+                rhs=codes[:].bitcast(fmt), rhs_scale=plane[:], start=first, stop=not first,
+            )
+
+        def turn_gate(h, acc):
+            for u in range(TILES):
+                nc.tensor.transpose(acc[:, u * P : (u + 1) * P], gate[h][:, u * P : (u + 1) * P], eye[:])
+            nc.scalar.copy(out=gate_t[h][:], in_=acc[:].rearrange("p (u g s) -> p u g s", u=TILES, s=16)[:, :, :, 0])
+
+        def weigh(h, u, acc, dst, b0):
+            src4 = acc[:].rearrange("p (b g s) -> p b g s", b=BLOCKS, s=16)
+            dst4 = dst[:].rearrange("p (b g s) -> p b g s", b=BLOCKS, s=16)
+            for g in range(GROUPS):
+                nc.scalar.activation(
+                    out=dst4[:, b0:, g, :], in_=src4[:, b0:, g, :], func=COPY, scale=gate_t[h][:, u, g : g + 1]
+                )
+
+        def turn(weighed, b, acc):
+            for u in range(TILES):
+                nc.tensor.transpose(acc[:, u * P : (u + 1) * P], weighed[u][:, b * P : (b + 1) * P], eye[:])
+
+        def turn_back(weighed, b, acc, dst):
+            turn(weighed, b, acc)
+            nc.scalar.copy(out=dst[:], in_=acc[:])
+
+        def clear(name, tag):
+            page = sb(name, [P, T], F32, tag=tag)
+            nc.gpsimd.memset(page[:], 0.0)
+            return page
+
+        def scatter(page, h, a, b):
+            nc.vector.tensor_tensor(
+                out=page[:].indirect(offsets[:, 32 * h : 32 * (h + 1)]), in0=a, in1=b, op=ALU.mult
+            )
+
+        for c in range(2):
+            woven = sb("woven0_%d" % c, [P, PIECE, PACK], BF16, tag="slot0" if c == 1 else None)
+            weave(nc.vector.tensor_copy, woven, raw[0][:, c], 0, CAST_V)
+            weave(nc.scalar.copy, woven, raw[0][:, c], CAST_V, PIECE)
+            quantise(q_codes[0], q_plane[0], E5M2, woven[:], c * PIECE, (c + 1) * PIECE)
+        pages = [clear("page0", "slot0")]
+        rest0 = sb("rest0", [P, PACK, HALF], BF16)
+        decoded = [bank("decoded0_%d" % t, t) for t in range(PACK)]
+        for t in range(PACK):
+            decode(0, t, decoded[t])
+        for t in range(PACK):
+            leftover(0, t, decoded[t], rest0)
+        direct = bank("direct", 0)
+        direct_pass(q_codes[0], q_plane[0], E5M2, direct, True)
+        turned = [bank("turned0_%d" % u, 4 + u) for u in range(TILES)]
+        for u in range(TILES):
+            turned_pass(q_codes[0], q_plane[0], E5M2, u, turned[u], True)
+        turn_gate(0, bank("gate_bank0", 1))
+        rest0_woven = sb("rest0_woven", [P, HALF, PACK], BF16)
+        weave(nc.vector.tensor_copy, rest0_woven, rest0, 0, WEAVE_V)
+        weave(nc.scalar.copy, rest0_woven, rest0, WEAVE_V, HALF)
+        quantise(r_codes[0], r_plane[0], E4M3, rest0_woven[:], 0, HALF)
+        direct_pass(r_codes[0], r_plane[0], E4M3, direct, False)
+        for u in range(TILES):
+            turned_pass(r_codes[0], r_plane[0], E4M3, u, turned[u], False)
+        first = sb("first", [P, HALF], F32, tag="slot2")
+        nc.vector.tensor_tensor(out=first[:], in0=direct[:], in1=d_first[:], op=ALU.mult)
+        scatter(pages[0], 0, first[:], gate[0][:])
+        pages.append(clear("page1", "slot1"))
+        pages.append(clear("page2", "slot2"))
+
+        weighed0 = [sb("weighed0_%d" % u, [P, N], F32, tag="slot6" if u == TILES - 1 else None) for u in range(TILES)]
+        for u in range(TILES):
+            weigh(0, u, turned[u], weighed0[u], 1)
+
+        woven1 = sb("woven1", [P, HALF, PACK], BF16)
+        for c in range(2):
+            for e in range(2):
+                weave(nc.scalar.copy, woven1[:, c * PIECE : (c + 1) * PIECE, :], raw[1][:, c], e * P, (e + 1) * P)
+        quantise(q_codes[1], q_plane[1], E5M2, woven1[:], 0, HALF)
+        rest1 = sb("rest1", [P, PACK, HALF], BF16, tag="slot5")
+        decoded = [bank("decoded1_%d" % t, (2, 3, 1, 2)[t]) for t in range(PACK)]
+        for t in range(PACK):
+            decode(1, t, decoded[t])
+        back01 = sb("back0_1", [P, HALF], F32, tag="slot3")
+        turn_back(weighed0, 1, bank("back_bank0_1", 4), back01)
+        for t in range(PACK):
+            leftover(1, t, decoded[t], rest1)
+        scatter(pages[1], 0, back01[:], d_rest[:, 0, :])
+        pages.append(clear("page3", "slot3"))
+        back_banks = [bank("back_bank0_%d" % b, 3 + b) for b in (2, 3)]
+        for b in (2, 3):
+            turn(weighed0, b, back_banks[b - 2])
+        rest1_woven = sb("rest1_woven", [P, HALF, PACK], BF16, tag="slot6")
+        weave(nc.scalar.copy, rest1_woven, rest1, 0, PIECE)
+        weave(nc.scalar.copy, rest1_woven, rest1, PIECE, HALF)
+        quantise(r_codes[1], r_plane[1], E4M3, rest1_woven[:], 0, HALF)
+        back02 = sb("back0_2", [P, HALF], F32, tag="slot5")
+        nc.scalar.copy(out=back02[:], in_=back_banks[0][:])
+        back03 = sb("back0_3", [P, HALF], F32)
+        nc.scalar.copy(out=back03[:], in_=back_banks[1][:])
+        turn_gate(1, bank("gate_bank1", 4))
+        turned = [bank("turned1_%d" % u, (3, 1, 0, 7)[u]) for u in range(TILES)]
+        for u in range(TILES):
+            turned_pass(q_codes[1], q_plane[1], E5M2, u, turned[u], True)
+        for u in range(TILES):
+            turned_pass(r_codes[1], r_plane[1], E4M3, u, turned[u], False)
+        scatter(pages[2], 0, back02[:], d_rest[:, 1, :])
+        scatter(pages[3], 0, back03[:], d_rest[:, 2, :])
+        weighed1 = [sb("weighed1_%d" % u, [P, N], F32) for u in range(TILES)]
+        for u in range(TILES):
+            weigh(1, u, turned[u], weighed1[u], 0)
+        for b in range(BLOCKS):
+            back = sb("back1_%d" % b, [P, HALF], F32)
+            turn_back(weighed1, b, bank("back_bank1_%d" % b, (2, 4, 5, 6)[b]), back)
+            scatter(pages[b], 1, back[:], d_second[:, b, :])
+            nc.sync.dma_start(out=out[b * P : (b + 1) * P, :], in_=pages[b][:])

@@ -25,7 +25,16 @@ GROUPS = 8
 BLOCKS = N // P
 TILES = HALF // P
 CAST_V = 160
-WEAVE_V = 352
+CAST_S = PIECE - CAST_V
+WEAVE_V = 288
+GATE_FIRST, GATE_STEP = 70, 7
+
+
+def gate_column(tile, g):
+    return min(
+        p for p in range(P)
+        if (GATE_FIRST + GATE_STEP * p) // P == g and (GATE_FIRST + GATE_STEP * p) % (J // P) == tile
+    )
 
 
 def weave(copy, dst, src, j0, j1):
@@ -39,6 +48,7 @@ def tile_list_embg_tgq4_mul_kernel(tc, dy, w_words, w_scales, d, wgo, offs, out)
     nc = tc.nc
     with ExitStack() as ctx:
         keep = ctx.enter_context(tc.tile_pool(name="keep", bufs=1))
+        lap = ctx.enter_context(tc.tile_pool(name="lap", bufs=1))
         psum = ctx.enter_context(tc.psum_pool(name="psum", bufs=1))
 
         def sb(name, shape, dtype, tag=None):
@@ -50,11 +60,21 @@ def tile_list_embg_tgq4_mul_kernel(tc, dy, w_words, w_scales, d, wgo, offs, out)
         offsets = keep.tile([P, J // 16], U16, name="offsets")
         dy_view = dy.rearrange("(p t) j -> p t j", t=PACK)
         d_view = d.rearrange("(b p) j -> p b j", p=P)
-        raw = [sb("raw%d" % h, [P, 2, PACK, PIECE], F32) for h in range(2)]
-        for h in range(2):
-            for c in range(2):
-                j0 = h * HALF + c * PIECE
-                nc.sync.dma_start(out=raw[h][:, c, :, :], in_=dy_view[:, :, j0 : j0 + PIECE])
+        raw_flat = [sb("raw%d" % h, [P, PACK * HALF], F32, tag="slot4" if h == 0 else None) for h in range(2)]
+        raw = [x[:].rearrange("p (c t j) -> p c t j", c=2, t=PACK) for x in raw_flat]
+
+        def load_dy(h, c):
+            j0 = h * HALF + c * PIECE
+            nc.sync.dma_start(out=raw[h][:, c, :, :], in_=dy_view[:, :, j0 : j0 + PIECE])
+
+        load_dy(0, 0)
+        load_dy(0, 1)
+        gate_rows = sb("gate_rows", [P, P], F32)
+        nc.sync.dma_start(
+            out=gate_rows[:],
+            in_=wgo.rearrange("r (u j) -> (r u) j", j=P)[GATE_FIRST : GATE_FIRST + GATE_STEP * (P - 1) + 1 : GATE_STEP, :],
+        )
+        load_dy(1, 0)
         w_codes = sb("w_codes", [P, 2 * N], U8)
         w_plane = sb("w_plane", [P, N], U8)
         nc.vector.memset(w_plane[:].bitcast(I32), 0)
@@ -63,39 +83,42 @@ def tile_list_embg_tgq4_mul_kernel(tc, dy, w_words, w_scales, d, wgo, offs, out)
             nc.sync.dma_start(
                 out=w_plane[32 * q : 32 * q + 4, :].bitcast(I32), in_=w_scales[0, 4 * q : 4 * q + 4, :].bitcast(I32)
             )
-        gate = [sb("gate%d" % h, [P, HALF], F32) for h in range(2)]
-        d_first = sb("d_first", [P, HALF], F32, tag="slot1")
+        load_dy(1, 1)
+        gate = sb("gate", [P, HALF], F32)
+        d_first = sb("d_first", [P, HALF], F32, tag="slot2")
         d_rest = sb("d_rest", [P, BLOCKS - 1, HALF], F32)
         d_second = sb("d_second", [P, BLOCKS, HALF], F32)
-        nc.sync.dma_start(out=gate[0][:], in_=wgo[:, 0:HALF])
+        nc.sync.dma_start(out=gate[:], in_=wgo[:, 0:HALF])
         nc.sync.dma_start(out=d_first[:], in_=d_view[:, 0, 0:HALF])
         nc.sync.dma_start(offsets[:], offs)
         nc.sync.dma_start(out=d_rest[:], in_=d_view[:, 1:BLOCKS, 0:HALF])
-        nc.sync.dma_start(out=gate[1][:], in_=wgo[:, HALF:J])
         nc.sync.dma_start(out=d_second[:], in_=d_view[:, :, HALF:J])
 
         diag = sb("diag", [P, HALF + 16], BF16)
-        nc.vector.memset(diag[:], 0.0)
+        nc.gpsimd.memset(diag[:], 0.0)
         nc.gpsimd.affine_select(
             out=diag[:], in_=diag[:], pattern=[[1, HALF + 16]], compare_op=ALU.not_equal, fill=1.0,
             base=-3, channel_multiplier=-4,
         )
         eye = sb("eye", [P, P], F32)
-        nc.scalar.activation(out=eye[:], in_=diag[:, 3 : 3 + HALF : 4], func=COPY)
-        eye_in = sb("eye_in", [P, PACK, HALF], BF16)
+        stage = sb("stage", [P, PACK * (HALF + 2 * CAST_S)], BF16, tag="slot0")
+        eye_at = PACK * CAST_S
         for t in range(PACK):
-            nc.vector.tensor_copy(out=eye_in[:, t, :], in_=diag[:, 3 - t : 3 - t + HALF])
+            nc.vector.tensor_copy(
+                out=stage[:, eye_at + t * HALF : eye_at + (t + 1) * HALF], in_=diag[:, 3 - t : 3 - t + HALF]
+            )
         eye_codes = sb("eye_codes", [P, HALF], U32)
         eye_plane = sb("eye_plane", [P, HALF], U8)
+        nc.vector.tensor_copy(out=eye[:], in_=diag[:, 3 : 3 + HALF : 4])
         nc.vector.quantize_mx(
-            out=eye_codes[:].bitcast(E4M3), scales=eye_plane[:], in_=eye_in[:].rearrange("p t c -> p (t c)")
+            out=eye_codes[:].bitcast(E4M3), scales=eye_plane[:], in_=stage[:, eye_at : eye_at + PACK * HALF]
         )
 
-        q_codes = [sb("q_codes%d" % h, [P, HALF], U32) for h in range(2)]
+        q_codes = [sb("q_codes0", [P, HALF], U32)]
         q_plane = [sb("q_plane%d" % h, [P, HALF], U8) for h in range(2)]
         r_codes = [sb("r_codes%d" % h, [P, HALF], U32) for h in range(2)]
         r_plane = [sb("r_plane%d" % h, [P, HALF], U8) for h in range(2)]
-        gate_t = [sb("gate_t%d" % h, [P, TILES, GROUPS], F32) for h in range(2)]
+        gate_t = sb("gate_t", [P, P], F32)
 
         def quantise(codes, plane, fmt, src, j0, j1):
             nc.vector.quantize_mx(
@@ -128,17 +151,13 @@ def tile_list_embg_tgq4_mul_kernel(tc, dy, w_words, w_scales, d, wgo, offs, out)
                 rhs=codes[:].bitcast(fmt), rhs_scale=plane[:], start=first, stop=not first,
             )
 
-        def turn_gate(h, acc):
-            for u in range(TILES):
-                nc.tensor.transpose(acc[:, u * P : (u + 1) * P], gate[h][:, u * P : (u + 1) * P], eye[:])
-            nc.scalar.copy(out=gate_t[h][:], in_=acc[:].rearrange("p (u g s) -> p u g s", u=TILES, s=16)[:, :, :, 0])
-
         def weigh(h, u, acc, dst, b0):
             src4 = acc[:].rearrange("p (b g s) -> p b g s", b=BLOCKS, s=16)
             dst4 = dst[:].rearrange("p (b g s) -> p b g s", b=BLOCKS, s=16)
             for g in range(GROUPS):
+                col = gate_column(h * TILES + u, g)
                 nc.scalar.activation(
-                    out=dst4[:, b0:, g, :], in_=src4[:, b0:, g, :], func=COPY, scale=gate_t[h][:, u, g : g + 1]
+                    out=dst4[:, b0:, g, :], in_=src4[:, b0:, g, :], func=COPY, scale=gate_t[:, col : col + 1]
                 )
 
         def turn(weighed, b, acc):
@@ -149,8 +168,7 @@ def tile_list_embg_tgq4_mul_kernel(tc, dy, w_words, w_scales, d, wgo, offs, out)
             turn(weighed, b, acc)
             nc.scalar.copy(out=dst[:], in_=acc[:])
 
-        def clear(name, tag):
-            page = sb(name, [P, T], F32, tag=tag)
+        def clear(page):
             nc.gpsimd.memset(page[:], 0.0)
             return page
 
@@ -159,80 +177,88 @@ def tile_list_embg_tgq4_mul_kernel(tc, dy, w_words, w_scales, d, wgo, offs, out)
                 out=page[:].indirect(offsets[:, 32 * h : 32 * (h + 1)]), in0=a, in1=b, op=ALU.mult
             )
 
+        at0 = eye_at + PACK * (HALF - CAST_V)
+        woven = stage[:, at0 : at0 + PACK * PIECE].rearrange("p (j t) -> p j t", t=PACK)
+        weave(nc.vector.tensor_copy, woven, raw[0][:, 0], 0, CAST_V)
+        weave(nc.scalar.copy, woven, raw[0][:, 0], CAST_V, PIECE)
+        quantise(q_codes[0], q_plane[0], E5M2, woven, 0, PIECE)
+        woven = stage[:, 0 : PACK * PIECE].rearrange("p (j t) -> p j t", t=PACK)
+        weave(nc.vector.tensor_copy, woven, raw[0][:, 1], CAST_S, PIECE)
+        weave(nc.scalar.copy, woven, raw[0][:, 1], 0, CAST_S)
+        quantise(q_codes[0], q_plane[0], E5M2, woven, PIECE, HALF)
+        gate_bank = bank("gate_bank", 5)
+        nc.tensor.transpose(gate_bank[:, 0:P], gate_rows[:], eye[:])
+        nc.scalar.copy(out=gate_t[:], in_=gate_bank[:, 0:P])
+        pages = [clear(sb("page0", [P, T], F32, tag="slot0"))]
+        woven1 = sb("woven1", [P, HALF, PACK], BF16)
         for c in range(2):
-            woven = sb("woven0_%d" % c, [P, PIECE, PACK], BF16, tag="slot0" if c == 1 else None)
-            weave(nc.vector.tensor_copy, woven, raw[0][:, c], 0, CAST_V)
-            weave(nc.scalar.copy, woven, raw[0][:, c], CAST_V, PIECE)
-            quantise(q_codes[0], q_plane[0], E5M2, woven[:], c * PIECE, (c + 1) * PIECE)
-        pages = [clear("page0", "slot0")]
+            weave(nc.scalar.copy, woven1[:, c * PIECE : (c + 1) * PIECE, :], raw[1][:, c], 0, PIECE)
+
         rest0 = sb("rest0", [P, PACK, HALF], BF16)
         decoded = [bank("decoded0_%d" % t, t) for t in range(PACK)]
         for t in range(PACK):
             decode(0, t, decoded[t])
         for t in range(PACK):
             leftover(0, t, decoded[t], rest0)
-        direct = bank("direct", 0)
+        q_codes.append(sb("q_codes1", [P, HALF], U32, tag="slot4"))
+        quantise(q_codes[1], q_plane[1], E5M2, woven1[:], 0, HALF)
+        direct = bank("direct", 4)
         direct_pass(q_codes[0], q_plane[0], E5M2, direct, True)
-        turned = [bank("turned0_%d" % u, 4 + u) for u in range(TILES)]
-        for u in range(TILES):
+        decoded = [bank("decoded1_%d" % t, (5, 6, 7, 3)[t]) for t in range(PACK)]
+        for t in range(PACK):
+            decode(1, t, decoded[t])
+        turned = [bank("turned0_%d" % u, u) for u in range(TILES - 1)]
+        for u in range(TILES - 1):
             turned_pass(q_codes[0], q_plane[0], E5M2, u, turned[u], True)
-        turn_gate(0, bank("gate_bank0", 1))
-        rest0_woven = sb("rest0_woven", [P, HALF, PACK], BF16)
+        rest0_woven = lap.tile([P, HALF, PACK], BF16, name="rest0_woven", offset=6144, align_bytes=64)
         weave(nc.vector.tensor_copy, rest0_woven, rest0, 0, WEAVE_V)
         weave(nc.scalar.copy, rest0_woven, rest0, WEAVE_V, HALF)
         quantise(r_codes[0], r_plane[0], E4M3, rest0_woven[:], 0, HALF)
         direct_pass(r_codes[0], r_plane[0], E4M3, direct, False)
-        for u in range(TILES):
+        for u in range(TILES - 1):
             turned_pass(r_codes[0], r_plane[0], E4M3, u, turned[u], False)
-        first = sb("first", [P, HALF], F32, tag="slot2")
+        first = sb("first", [P, HALF], F32, tag="slot3")
         nc.vector.tensor_tensor(out=first[:], in0=direct[:], in1=d_first[:], op=ALU.mult)
-        scatter(pages[0], 0, first[:], gate[0][:])
-        pages.append(clear("page1", "slot1"))
-        pages.append(clear("page2", "slot2"))
+        pages.append(clear(lap.tile([P, T], F32, name="page1", offset=0, align_bytes=64)))
+        pages.append(clear(sb("page2", [P, T], F32, tag="slot2")))
+        rest1 = lap.tile([P, PACK, HALF], BF16, name="rest1", offset=8192, align_bytes=64)
+        for t in range(PACK):
+            leftover(1, t, decoded[t], rest1)
+        turned.append(bank("turned0_3", 5))
+        turned_pass(q_codes[0], q_plane[0], E5M2, TILES - 1, turned[TILES - 1], True)
+        turned_pass(r_codes[0], r_plane[0], E4M3, TILES - 1, turned[TILES - 1], False)
+        scatter(pages[0], 0, first[:], gate[:])
+        pages.append(clear(sb("page3", [P, T], F32, tag="slot3")))
 
         weighed0 = [sb("weighed0_%d" % u, [P, N], F32, tag="slot6" if u == TILES - 1 else None) for u in range(TILES)]
         for u in range(TILES):
             weigh(0, u, turned[u], weighed0[u], 1)
-
-        woven1 = sb("woven1", [P, HALF, PACK], BF16)
-        for c in range(2):
-            for e in range(2):
-                weave(nc.scalar.copy, woven1[:, c * PIECE : (c + 1) * PIECE, :], raw[1][:, c], e * P, (e + 1) * P)
-        quantise(q_codes[1], q_plane[1], E5M2, woven1[:], 0, HALF)
-        rest1 = sb("rest1", [P, PACK, HALF], BF16, tag="slot5")
-        decoded = [bank("decoded1_%d" % t, (2, 3, 1, 2)[t]) for t in range(PACK)]
-        for t in range(PACK):
-            decode(1, t, decoded[t])
-        back01 = sb("back0_1", [P, HALF], F32, tag="slot3")
-        turn_back(weighed0, 1, bank("back_bank0_1", 4), back01)
-        for t in range(PACK):
-            leftover(1, t, decoded[t], rest1)
-        scatter(pages[1], 0, back01[:], d_rest[:, 0, :])
-        pages.append(clear("page3", "slot3"))
-        back_banks = [bank("back_bank0_%d" % b, 3 + b) for b in (2, 3)]
-        for b in (2, 3):
-            turn(weighed0, b, back_banks[b - 2])
+        back_banks = [bank("back_bank0_%d" % b, (4, 6, 7)[b - 1]) for b in (1, 2, 3)]
+        for b in (1, 2, 3):
+            turn(weighed0, b, back_banks[b - 1])
+        back0 = [sb("back0_1", [P, HALF], F32)] + [
+            lap.tile([P, HALF], F32, name="back0_%d" % b, offset=8192 + 2048 * (b - 2), align_bytes=64) for b in (2, 3)
+        ]
+        nc.scalar.copy(out=back0[0][:], in_=back_banks[0][:])
+        scatter(pages[1], 0, back0[0][:], d_rest[:, 0, :])
         rest1_woven = sb("rest1_woven", [P, HALF, PACK], BF16, tag="slot6")
         weave(nc.scalar.copy, rest1_woven, rest1, 0, PIECE)
         weave(nc.scalar.copy, rest1_woven, rest1, PIECE, HALF)
         quantise(r_codes[1], r_plane[1], E4M3, rest1_woven[:], 0, HALF)
-        back02 = sb("back0_2", [P, HALF], F32, tag="slot5")
-        nc.scalar.copy(out=back02[:], in_=back_banks[0][:])
-        back03 = sb("back0_3", [P, HALF], F32)
-        nc.scalar.copy(out=back03[:], in_=back_banks[1][:])
-        turn_gate(1, bank("gate_bank1", 4))
-        turned = [bank("turned1_%d" % u, (3, 1, 0, 7)[u]) for u in range(TILES)]
+        nc.scalar.copy(out=back0[1][:], in_=back_banks[1][:])
+        nc.scalar.copy(out=back0[2][:], in_=back_banks[2][:])
+        turned = [bank("turned1_%d" % u, 4 + u) for u in range(TILES)]
         for u in range(TILES):
             turned_pass(q_codes[1], q_plane[1], E5M2, u, turned[u], True)
         for u in range(TILES):
             turned_pass(r_codes[1], r_plane[1], E4M3, u, turned[u], False)
-        scatter(pages[2], 0, back02[:], d_rest[:, 1, :])
-        scatter(pages[3], 0, back03[:], d_rest[:, 2, :])
+        scatter(pages[2], 0, back0[1][:], d_rest[:, 1, :])
+        scatter(pages[3], 0, back0[2][:], d_rest[:, 2, :])
         weighed1 = [sb("weighed1_%d" % u, [P, N], F32) for u in range(TILES)]
         for u in range(TILES):
             weigh(1, u, turned[u], weighed1[u], 0)
         for b in range(BLOCKS):
             back = sb("back1_%d" % b, [P, HALF], F32)
-            turn_back(weighed1, b, bank("back_bank1_%d" % b, (2, 4, 5, 6)[b]), back)
+            turn_back(weighed1, b, bank("back_bank1_%d" % b, b), back)
             scatter(pages[b], 1, back[:], d_second[:, b, :])
             nc.sync.dma_start(out=out[b * P : (b + 1) * P, :], in_=pages[b][:])

@@ -69,22 +69,22 @@ def tile_list_embg_tgq4_mul_kernel(tc, dy, w_words, w_scales, d, wgo, offs, out)
 
         load_dy(0, 0)
         load_dy(0, 1)
-        gate_rows = sb("gate_rows", [P, P], F32)
-        nc.sync.dma_start(
-            out=gate_rows[:],
-            in_=wgo.rearrange("r (u j) -> (r u) j", j=P)[GATE_FIRST : GATE_FIRST + GATE_STEP * (P - 1) + 1 : GATE_STEP, :],
-        )
         load_dy(1, 0)
         w_codes = sb("w_codes", [P, 2 * N], U8)
         w_plane = sb("w_plane", [P, N], U8)
         nc.vector.memset(w_plane[:].bitcast(I32), 0)
-        nc.sync.dma_start(out=w_codes[:].bitcast(I32), in_=w_words[0].bitcast(I32))
         for q in range(4):
             nc.sync.dma_start(
                 out=w_plane[32 * q : 32 * q + 4, :].bitcast(I32), in_=w_scales[0, 4 * q : 4 * q + 4, :].bitcast(I32)
             )
         load_dy(1, 1)
-        gate = sb("gate", [P, HALF], F32)
+        nc.sync.dma_start(out=w_codes[:].bitcast(I32), in_=w_words[0].bitcast(I32))
+        gate_rows = sb("gate_rows", [P, P], F32)
+        nc.sync.dma_start(
+            out=gate_rows[:],
+            in_=wgo.rearrange("r (u j) -> (r u) j", j=P)[GATE_FIRST : GATE_FIRST + GATE_STEP * (P - 1) + 1 : GATE_STEP, :],
+        )
+        gate = sb("gate", [P, HALF], F32, tag="slot1")
         d_first = sb("d_first", [P, HALF], F32, tag="slot2")
         d_rest = sb("d_rest", [P, BLOCKS - 1, HALF], F32)
         d_second = sb("d_second", [P, BLOCKS, HALF], F32)
@@ -186,15 +186,12 @@ def tile_list_embg_tgq4_mul_kernel(tc, dy, w_words, w_scales, d, wgo, offs, out)
         weave(nc.vector.tensor_copy, woven, raw[0][:, 1], CAST_S, PIECE)
         weave(nc.scalar.copy, woven, raw[0][:, 1], 0, CAST_S)
         quantise(q_codes[0], q_plane[0], E5M2, woven, PIECE, HALF)
-        gate_bank = bank("gate_bank", 5)
-        nc.tensor.transpose(gate_bank[:, 0:P], gate_rows[:], eye[:])
-        nc.scalar.copy(out=gate_t[:], in_=gate_bank[:, 0:P])
         pages = [clear(sb("page0", [P, T], F32, tag="slot0"))]
         woven1 = sb("woven1", [P, HALF, PACK], BF16)
         for c in range(2):
             weave(nc.scalar.copy, woven1[:, c * PIECE : (c + 1) * PIECE, :], raw[1][:, c], 0, PIECE)
 
-        rest0 = sb("rest0", [P, PACK, HALF], BF16)
+        rest0 = lap.tile([P, PACK, HALF], BF16, name="rest0", offset=0, align_bytes=64)
         decoded = [bank("decoded0_%d" % t, t) for t in range(PACK)]
         for t in range(PACK):
             decode(0, t, decoded[t])
@@ -204,31 +201,35 @@ def tile_list_embg_tgq4_mul_kernel(tc, dy, w_words, w_scales, d, wgo, offs, out)
         quantise(q_codes[1], q_plane[1], E5M2, woven1[:], 0, HALF)
         direct = bank("direct", 4)
         direct_pass(q_codes[0], q_plane[0], E5M2, direct, True)
+        gate_bank = bank("gate_bank", 0)
+        nc.tensor.transpose(gate_bank[:, 0:P], gate_rows[:], eye[:])
+        nc.scalar.copy(out=gate_t[:], in_=gate_bank[:, 0:P])
         decoded = [bank("decoded1_%d" % t, (5, 6, 7, 3)[t]) for t in range(PACK)]
         for t in range(PACK):
             decode(1, t, decoded[t])
         turned = [bank("turned0_%d" % u, u) for u in range(TILES - 1)]
         for u in range(TILES - 1):
             turned_pass(q_codes[0], q_plane[0], E5M2, u, turned[u], True)
-        rest0_woven = lap.tile([P, HALF, PACK], BF16, name="rest0_woven", offset=6144, align_bytes=64)
+        rest0_woven = sb("rest0_woven", [P, HALF, PACK], BF16, tag="slot5")
         weave(nc.vector.tensor_copy, rest0_woven, rest0, 0, WEAVE_V)
         weave(nc.scalar.copy, rest0_woven, rest0, WEAVE_V, HALF)
         quantise(r_codes[0], r_plane[0], E4M3, rest0_woven[:], 0, HALF)
         direct_pass(r_codes[0], r_plane[0], E4M3, direct, False)
         for u in range(TILES - 1):
             turned_pass(r_codes[0], r_plane[0], E4M3, u, turned[u], False)
-        first = sb("first", [P, HALF], F32, tag="slot3")
-        nc.vector.tensor_tensor(out=first[:], in0=direct[:], in1=d_first[:], op=ALU.mult)
-        pages.append(clear(lap.tile([P, T], F32, name="page1", offset=0, align_bytes=64)))
+        first = sb("first", [P, HALF], F32)
+        nc.scalar.copy(out=first[:], in_=direct[:])
+        factor = sb("factor", [P, HALF], F32, tag="slot5")
+        nc.gpsimd.tensor_tensor(out=factor[:], in0=d_first[:], in1=gate[:], op=ALU.mult)
+        pages.append(clear(sb("page1", [P, T], F32, tag="slot1")))
         pages.append(clear(sb("page2", [P, T], F32, tag="slot2")))
-        rest1 = lap.tile([P, PACK, HALF], BF16, name="rest1", offset=8192, align_bytes=64)
+        rest1 = lap.tile([P, PACK, HALF], BF16, name="rest1", offset=0, align_bytes=64)
         for t in range(PACK):
             leftover(1, t, decoded[t], rest1)
         turned.append(bank("turned0_3", 5))
         turned_pass(q_codes[0], q_plane[0], E5M2, TILES - 1, turned[TILES - 1], True)
         turned_pass(r_codes[0], r_plane[0], E4M3, TILES - 1, turned[TILES - 1], False)
-        scatter(pages[0], 0, first[:], gate[:])
-        pages.append(clear(sb("page3", [P, T], F32, tag="slot3")))
+        scatter(pages[0], 0, first[:], factor[:])
 
         weighed0 = [sb("weighed0_%d" % u, [P, N], F32, tag="slot6" if u == TILES - 1 else None) for u in range(TILES)]
         for u in range(TILES):
@@ -237,7 +238,7 @@ def tile_list_embg_tgq4_mul_kernel(tc, dy, w_words, w_scales, d, wgo, offs, out)
         for b in (1, 2, 3):
             turn(weighed0, b, back_banks[b - 1])
         back0 = [sb("back0_1", [P, HALF], F32)] + [
-            lap.tile([P, HALF], F32, name="back0_%d" % b, offset=8192 + 2048 * (b - 2), align_bytes=64) for b in (2, 3)
+            lap.tile([P, HALF], F32, name="back0_%d" % b, offset=2048 * (b - 2), align_bytes=64) for b in (2, 3)
         ]
         nc.scalar.copy(out=back0[0][:], in_=back_banks[0][:])
         scatter(pages[1], 0, back0[0][:], d_rest[:, 0, :])
@@ -245,6 +246,7 @@ def tile_list_embg_tgq4_mul_kernel(tc, dy, w_words, w_scales, d, wgo, offs, out)
         weave(nc.scalar.copy, rest1_woven, rest1, 0, PIECE)
         weave(nc.scalar.copy, rest1_woven, rest1, PIECE, HALF)
         quantise(r_codes[1], r_plane[1], E4M3, rest1_woven[:], 0, HALF)
+        pages.append(clear(sb("page3", [P, T], F32, tag="slot6")))
         nc.scalar.copy(out=back0[1][:], in_=back_banks[1][:])
         nc.scalar.copy(out=back0[2][:], in_=back_banks[2][:])
         turned = [bank("turned1_%d" % u, 4 + u) for u in range(TILES)]

@@ -26,7 +26,7 @@ BLOCKS = N // P
 TILES = HALF // P
 CAST_V = 160
 CAST_S = PIECE - CAST_V
-WEAVE_V = 288
+WEAVE_V = 296
 GATE_FIRST, GATE_STEP = 70, 7
 
 
@@ -60,7 +60,7 @@ def tile_list_embg_tgq4_mul_kernel(tc, dy, w_words, w_scales, d, wgo, offs, out)
         offsets = keep.tile([P, J // 16], U16, name="offsets")
         dy_view = dy.rearrange("(p t) j -> p t j", t=PACK)
         d_view = d.rearrange("(b p) j -> p b j", p=P)
-        raw_flat = [sb("raw%d" % h, [P, PACK * HALF], F32, tag="slot4" if h == 0 else None) for h in range(2)]
+        raw_flat = [sb("raw%d" % h, [P, PACK * HALF], F32) for h in range(2)]
         raw = [x[:].rearrange("p (c t j) -> p c t j", c=2, t=PACK) for x in raw_flat]
 
         def load_dy(h, c):
@@ -79,7 +79,7 @@ def tile_list_embg_tgq4_mul_kernel(tc, dy, w_words, w_scales, d, wgo, offs, out)
             )
         load_dy(1, 1)
         nc.sync.dma_start(out=w_codes[:].bitcast(I32), in_=w_words[0].bitcast(I32))
-        gate_rows = sb("gate_rows", [P, P], F32)
+        gate_rows = sb("gate_rows", [P, P], F32, tag="slot4")
         nc.sync.dma_start(
             out=gate_rows[:],
             in_=wgo.rearrange("r (u j) -> (r u) j", j=P)[GATE_FIRST : GATE_FIRST + GATE_STEP * (P - 1) + 1 : GATE_STEP, :],
@@ -94,28 +94,29 @@ def tile_list_embg_tgq4_mul_kernel(tc, dy, w_words, w_scales, d, wgo, offs, out)
         nc.sync.dma_start(out=d_rest[:], in_=d_view[:, 1:BLOCKS, 0:HALF])
         nc.sync.dma_start(out=d_second[:], in_=d_view[:, :, HALF:J])
 
-        diag = sb("diag", [P, HALF + 16], BF16)
-        nc.gpsimd.memset(diag[:], 0.0)
-        nc.gpsimd.affine_select(
-            out=diag[:], in_=diag[:], pattern=[[1, HALF + 16]], compare_op=ALU.not_equal, fill=1.0,
-            base=-3, channel_multiplier=-4,
+        ramp = sb("ramp", [P, HALF], BF16)
+        nc.gpsimd.iota(
+            ramp[:], pattern=[[1, HALF]], base=0, channel_multiplier=-PACK, allow_small_or_imprecise_dtypes=True
         )
         eye = sb("eye", [P, P], F32)
         stage = sb("stage", [P, PACK * (HALF + 2 * CAST_S)], BF16, tag="slot0")
         eye_at = PACK * CAST_S
         for t in range(PACK):
-            nc.vector.tensor_copy(
-                out=stage[:, eye_at + t * HALF : eye_at + (t + 1) * HALF], in_=diag[:, 3 - t : 3 - t + HALF]
+            nc.vector.tensor_scalar(
+                out=stage[:, eye_at + t * HALF : eye_at + (t + 1) * HALF], in0=ramp[:], scalar1=float(t),
+                scalar2=None, op0=ALU.is_equal,
             )
         eye_codes = sb("eye_codes", [P, HALF], U32)
         eye_plane = sb("eye_plane", [P, HALF], U8)
-        nc.vector.tensor_copy(out=eye[:], in_=diag[:, 3 : 3 + HALF : 4])
+        nc.vector.tensor_scalar(
+            out=eye[:], in0=ramp[:, 0:HALF:PACK], scalar1=0.0, scalar2=None, op0=ALU.is_equal
+        )
         nc.vector.quantize_mx(
             out=eye_codes[:].bitcast(E4M3), scales=eye_plane[:], in_=stage[:, eye_at : eye_at + PACK * HALF]
         )
 
-        q_codes = [sb("q_codes0", [P, HALF], U32)]
-        q_plane = [sb("q_plane%d" % h, [P, HALF], U8) for h in range(2)]
+        q_codes = [sb("q_codes%d" % h, [P, HALF], U32) for h in range(2)]
+        q_plane = [sb("q_plane0", [P, HALF], U8)]
         r_codes = [sb("r_codes%d" % h, [P, HALF], U32) for h in range(2)]
         r_plane = [sb("r_plane%d" % h, [P, HALF], U8) for h in range(2)]
         gate_t = sb("gate_t", [P, P], F32)
@@ -197,13 +198,13 @@ def tile_list_embg_tgq4_mul_kernel(tc, dy, w_words, w_scales, d, wgo, offs, out)
             decode(0, t, decoded[t])
         for t in range(PACK):
             leftover(0, t, decoded[t], rest0)
-        q_codes.append(sb("q_codes1", [P, HALF], U32, tag="slot4"))
-        quantise(q_codes[1], q_plane[1], E5M2, woven1[:], 0, HALF)
         direct = bank("direct", 4)
         direct_pass(q_codes[0], q_plane[0], E5M2, direct, True)
         gate_bank = bank("gate_bank", 0)
         nc.tensor.transpose(gate_bank[:, 0:P], gate_rows[:], eye[:])
         nc.scalar.copy(out=gate_t[:], in_=gate_bank[:, 0:P])
+        q_plane.append(sb("q_plane1", [P, HALF], U8, tag="slot4"))
+        quantise(q_codes[1], q_plane[1], E5M2, woven1[:], 0, HALF)
         decoded = [bank("decoded1_%d" % t, (5, 6, 7, 3)[t]) for t in range(PACK)]
         for t in range(PACK):
             decode(1, t, decoded[t])

@@ -26,7 +26,7 @@ BLOCKS = N // P
 TILES = HALF // P
 CAST_V = 160
 CAST_S = PIECE - CAST_V
-WEAVE_V = 296
+WEAVE_V = 192
 GATE_FIRST, GATE_STEP = 70, 7
 
 
@@ -69,6 +69,11 @@ def tile_list_embg_tgq4_mul_kernel(tc, dy, w_words, w_scales, d, wgo, offs, out)
 
         load_dy(0, 0)
         load_dy(0, 1)
+        gate_rows = sb("gate_rows", [P, P], F32, tag="slot4")
+        nc.sync.dma_start(
+            out=gate_rows[:],
+            in_=wgo.rearrange("r (u j) -> (r u) j", j=P)[GATE_FIRST : GATE_FIRST + GATE_STEP * (P - 1) + 1 : GATE_STEP, :],
+        )
         load_dy(1, 0)
         w_codes = sb("w_codes", [P, 2 * N], U8)
         w_plane = sb("w_plane", [P, N], U8)
@@ -79,11 +84,6 @@ def tile_list_embg_tgq4_mul_kernel(tc, dy, w_words, w_scales, d, wgo, offs, out)
             )
         load_dy(1, 1)
         nc.sync.dma_start(out=w_codes[:].bitcast(I32), in_=w_words[0].bitcast(I32))
-        gate_rows = sb("gate_rows", [P, P], F32, tag="slot4")
-        nc.sync.dma_start(
-            out=gate_rows[:],
-            in_=wgo.rearrange("r (u j) -> (r u) j", j=P)[GATE_FIRST : GATE_FIRST + GATE_STEP * (P - 1) + 1 : GATE_STEP, :],
-        )
         gate = sb("gate", [P, HALF], F32, tag="slot1")
         d_first = sb("d_first", [P, HALF], F32, tag="slot2")
         d_rest = sb("d_rest", [P, BLOCKS - 1, HALF], F32)
@@ -196,25 +196,33 @@ def tile_list_embg_tgq4_mul_kernel(tc, dy, w_words, w_scales, d, wgo, offs, out)
         decoded = [bank("decoded0_%d" % t, t) for t in range(PACK)]
         for t in range(PACK):
             decode(0, t, decoded[t])
-        for t in range(PACK):
+        for t in range(2):
             leftover(0, t, decoded[t], rest0)
-        direct = bank("direct", 4)
-        direct_pass(q_codes[0], q_plane[0], E5M2, direct, True)
+        for c in range(2):
+            for t in (2, 3):
+                nc.vector.tensor_tensor(
+                    out=rest0[:, t, c * PIECE : (c + 1) * PIECE], in0=raw[0][:, c, t, :],
+                    in1=decoded[t][:, c * PIECE : (c + 1) * PIECE], op=ALU.subtract,
+                )
         gate_bank = bank("gate_bank", 0)
         nc.tensor.transpose(gate_bank[:, 0:P], gate_rows[:], eye[:])
         nc.scalar.copy(out=gate_t[:], in_=gate_bank[:, 0:P])
+        direct = bank("direct", 1)
+        direct_pass(q_codes[0], q_plane[0], E5M2, direct, True)
         q_plane.append(sb("q_plane1", [P, HALF], U8, tag="slot4"))
         quantise(q_codes[1], q_plane[1], E5M2, woven1[:], 0, HALF)
-        decoded = [bank("decoded1_%d" % t, (5, 6, 7, 3)[t]) for t in range(PACK)]
+        decoded = [bank("decoded1_%d" % t, (4, 5, 6, 7)[t]) for t in range(PACK)]
         for t in range(PACK):
             decode(1, t, decoded[t])
-        turned = [bank("turned0_%d" % u, u) for u in range(TILES - 1)]
+        turned = [bank("turned0_%d" % u, (0, 2, 3)[u]) for u in range(TILES - 1)]
         for u in range(TILES - 1):
             turned_pass(q_codes[0], q_plane[0], E5M2, u, turned[u], True)
         rest0_woven = sb("rest0_woven", [P, HALF, PACK], BF16, tag="slot5")
-        weave(nc.vector.tensor_copy, rest0_woven, rest0, 0, WEAVE_V)
-        weave(nc.scalar.copy, rest0_woven, rest0, WEAVE_V, HALF)
-        quantise(r_codes[0], r_plane[0], E4M3, rest0_woven[:], 0, HALF)
+        weave(nc.scalar.copy, rest0_woven, rest0, 0, PIECE)
+        weave(nc.vector.tensor_copy, rest0_woven, rest0, HALF - WEAVE_V, HALF)
+        weave(nc.scalar.copy, rest0_woven, rest0, PIECE, HALF - WEAVE_V)
+        for c in range(2):
+            quantise(r_codes[0], r_plane[0], E4M3, rest0_woven[:, c * PIECE : (c + 1) * PIECE, :], c * PIECE, (c + 1) * PIECE)
         direct_pass(r_codes[0], r_plane[0], E4M3, direct, False)
         for u in range(TILES - 1):
             turned_pass(r_codes[0], r_plane[0], E4M3, u, turned[u], False)
@@ -227,7 +235,7 @@ def tile_list_embg_tgq4_mul_kernel(tc, dy, w_words, w_scales, d, wgo, offs, out)
         rest1 = lap.tile([P, PACK, HALF], BF16, name="rest1", offset=0, align_bytes=64)
         for t in range(PACK):
             leftover(1, t, decoded[t], rest1)
-        turned.append(bank("turned0_3", 5))
+        turned.append(bank("turned0_3", 4))
         turned_pass(q_codes[0], q_plane[0], E5M2, TILES - 1, turned[TILES - 1], True)
         turned_pass(r_codes[0], r_plane[0], E4M3, TILES - 1, turned[TILES - 1], False)
         scatter(pages[0], 0, first[:], factor[:])
@@ -235,13 +243,18 @@ def tile_list_embg_tgq4_mul_kernel(tc, dy, w_words, w_scales, d, wgo, offs, out)
         weighed0 = [sb("weighed0_%d" % u, [P, N], F32, tag="slot6" if u == TILES - 1 else None) for u in range(TILES)]
         for u in range(TILES):
             weigh(0, u, turned[u], weighed0[u], 1)
-        back_banks = [bank("back_bank0_%d" % b, (4, 6, 7)[b - 1]) for b in (1, 2, 3)]
-        for b in (1, 2, 3):
+        back_banks = [bank("back_bank0_%d" % b, (1, 6, 7)[b - 1]) for b in (1, 2, 3)]
+        late = bank("late", 5)
+        for u in range(TILES):
+            dst = back_banks[0][:, u * P : (u + 1) * P] if u < TILES - 1 else late[:, 0:P]
+            nc.tensor.transpose(dst, weighed0[u][:, P : 2 * P], eye[:])
+        for b in (2, 3):
             turn(weighed0, b, back_banks[b - 1])
         back0 = [sb("back0_1", [P, HALF], F32)] + [
             lap.tile([P, HALF], F32, name="back0_%d" % b, offset=2048 * (b - 2), align_bytes=64) for b in (2, 3)
         ]
-        nc.scalar.copy(out=back0[0][:], in_=back_banks[0][:])
+        nc.scalar.copy(out=back0[0][:, 0 : HALF - P], in_=back_banks[0][:, 0 : HALF - P])
+        nc.scalar.copy(out=back0[0][:, HALF - P : HALF], in_=late[:, 0:P])
         scatter(pages[1], 0, back0[0][:], d_rest[:, 0, :])
         rest1_woven = sb("rest1_woven", [P, HALF, PACK], BF16, tag="slot6")
         weave(nc.scalar.copy, rest1_woven, rest1, 0, PIECE)
@@ -250,7 +263,7 @@ def tile_list_embg_tgq4_mul_kernel(tc, dy, w_words, w_scales, d, wgo, offs, out)
         pages.append(clear(sb("page3", [P, T], F32, tag="slot6")))
         nc.scalar.copy(out=back0[1][:], in_=back_banks[1][:])
         nc.scalar.copy(out=back0[2][:], in_=back_banks[2][:])
-        turned = [bank("turned1_%d" % u, 4 + u) for u in range(TILES)]
+        turned = [bank("turned1_%d" % u, (4, 1, 5, 6)[u]) for u in range(TILES)]
         for u in range(TILES):
             turned_pass(q_codes[1], q_plane[1], E5M2, u, turned[u], True)
         for u in range(TILES):
@@ -262,6 +275,6 @@ def tile_list_embg_tgq4_mul_kernel(tc, dy, w_words, w_scales, d, wgo, offs, out)
             weigh(1, u, turned[u], weighed1[u], 0)
         for b in range(BLOCKS):
             back = sb("back1_%d" % b, [P, HALF], F32)
-            turn_back(weighed1, b, bank("back_bank1_%d" % b, b), back)
+            turn_back(weighed1, b, bank("back_bank1_%d" % b, (0, 2, 3, 7)[b]), back)
             scatter(pages[b], 1, back[:], d_second[:, b, :])
             nc.sync.dma_start(out=out[b * P : (b + 1) * P, :], in_=pages[b][:])

@@ -26,7 +26,8 @@ BLOCKS = N // P
 TILES = HALF // P
 CAST_V = 160
 CAST_S = PIECE - CAST_V
-WEAVE_V = 192
+CAST_VB = 128
+CLEAR_ODD = 769
 GATE_FIRST, GATE_STEP = 70, 7
 
 
@@ -54,227 +55,314 @@ def tile_list_embg_tgq4_mul_kernel(tc, dy, w_words, w_scales, d, wgo, offs, out)
         def sb(name, shape, dtype, tag=None):
             return keep.tile(shape, dtype, name=name, tag=tag or name, align_bytes=64)
 
+        def placed(name, shape, dtype, offset):
+            return lap.tile(shape, dtype, name=name, offset=offset, align_bytes=64)
+
         def bank(name, index):
             return psum.tile([P, HALF], F32, name=name, tag="bank%d" % index)
 
         offsets = keep.tile([P, J // 16], U16, name="offsets")
         dy_view = dy.rearrange("(p t) j -> p t j", t=PACK)
         d_view = d.rearrange("(b p) j -> p b j", p=P)
-        raw_flat = [sb("raw%d" % h, [P, PACK * HALF], F32) for h in range(2)]
-        raw = [x[:].rearrange("p (c t j) -> p c t j", c=2, t=PACK) for x in raw_flat]
-
-        def load_dy(h, c):
-            j0 = h * HALF + c * PIECE
-            nc.sync.dma_start(out=raw[h][:, c, :, :], in_=dy_view[:, :, j0 : j0 + PIECE])
-
-        load_dy(0, 0)
-        load_dy(0, 1)
-        gate_rows = sb("gate_rows", [P, P], F32, tag="slot4")
+        raw = [placed("raw0", [P, PACK, PIECE], F32, 32768)] + [sb("raw%d" % c, [P, PACK, PIECE], F32) for c in (1, 2, 3)]
+        for c in range(2):
+            nc.sync.dma_start(out=raw[c][:], in_=dy_view[:, :, c * PIECE : (c + 1) * PIECE])
+        gate_rows = sb("gate_rows", [P, P], F32)
         nc.sync.dma_start(
             out=gate_rows[:],
             in_=wgo.rearrange("r (u j) -> (r u) j", j=P)[GATE_FIRST : GATE_FIRST + GATE_STEP * (P - 1) + 1 : GATE_STEP, :],
         )
-        load_dy(1, 0)
+        for c in (2, 3):
+            nc.sync.dma_start(out=raw[c][:], in_=dy_view[:, :, c * PIECE : (c + 1) * PIECE])
+        pages = [sb("page0", [P, T], F32)]
         w_codes = sb("w_codes", [P, 2 * N], U8)
-        w_plane = sb("w_plane", [P, N], U8)
-        nc.vector.memset(w_plane[:].bitcast(I32), 0)
+        w_plane_tile = sb("w_plane", [P, N + 4], U8)
+        nc.vector.memset(w_plane_tile[:].bitcast(I32), 0)
+        w_plane = w_plane_tile[:, 0:N]
+        nc.vector.memset(pages[0][:, 0:CLEAR_ODD], 0.0)
+        nc.sync.dma_start(out=w_codes[:].bitcast(I32), in_=w_words[0].bitcast(I32))
         for q in range(4):
             nc.sync.dma_start(
                 out=w_plane[32 * q : 32 * q + 4, :].bitcast(I32), in_=w_scales[0, 4 * q : 4 * q + 4, :].bitcast(I32)
             )
-        load_dy(1, 1)
-        nc.sync.dma_start(out=w_codes[:].bitcast(I32), in_=w_words[0].bitcast(I32))
-        gate = sb("gate", [P, HALF], F32, tag="slot1")
-        d_first = sb("d_first", [P, HALF], F32, tag="slot2")
-        d_rest = sb("d_rest", [P, BLOCKS - 1, HALF], F32)
-        d_second = sb("d_second", [P, BLOCKS, HALF], F32)
-        nc.sync.dma_start(out=gate[:], in_=wgo[:, 0:HALF])
-        nc.sync.dma_start(out=d_first[:], in_=d_view[:, 0, 0:HALF])
+        d_first = sb("d_first", [P, 2, PIECE], F32)
+        gate = sb("gate", [P, PIECE], F32)
+        d_next = sb("d_next", [P, 2, PIECE], F32)
+        d_second = [placed("d_second0", [P, 2, PIECE], F32, 46080), sb("d_second1", [P, 2, PIECE], F32)]
+        d_late = sb("d_late", [P, BLOCKS, HALF], F32)
+        nc.sync.dma_start(out=d_first[:], in_=d_view[:, 0:2, 0:PIECE])
+        nc.sync.dma_start(out=gate[:], in_=wgo[:, 0:PIECE])
         nc.sync.dma_start(offsets[:], offs)
-        nc.sync.dma_start(out=d_rest[:], in_=d_view[:, 1:BLOCKS, 0:HALF])
-        nc.sync.dma_start(out=d_second[:], in_=d_view[:, :, HALF:J])
+        nc.sync.dma_start(out=d_next[:], in_=d_view[:, 2:4, 0:PIECE])
+        for k in range(2):
+            nc.sync.dma_start(out=d_second[k][:], in_=d_view[:, 2 * k : 2 * k + 2, PIECE:HALF])
+        nc.sync.dma_start(out=d_late[:], in_=d_view[:, :, HALF:J])
+
+        wide_codes = sb("wide_codes", [P, 2 * HALF], U32)
+        wide_plane = sb("wide_plane", [P, 2 * HALF], U8)
+        nc.vector.memset(wide_codes[:].rearrange("p (c j) -> p c j", j=PIECE)[:, 1:4:2, :], 0)
+        nc.vector.memset(pages[0][:, CLEAR_ODD - 1 : T], 0.0)
 
         ramp = sb("ramp", [P, HALF], BF16)
         nc.gpsimd.iota(
             ramp[:], pattern=[[1, HALF]], base=0, channel_multiplier=-PACK, allow_small_or_imprecise_dtypes=True
         )
         eye = sb("eye", [P, P], F32)
-        stage = sb("stage", [P, PACK * (HALF + 2 * CAST_S)], BF16, tag="slot0")
-        eye_at = PACK * CAST_S
-        for t in range(PACK):
-            nc.vector.tensor_scalar(
-                out=stage[:, eye_at + t * HALF : eye_at + (t + 1) * HALF], in0=ramp[:], scalar1=float(t),
-                scalar2=None, op0=ALU.is_equal,
-            )
-        eye_codes = sb("eye_codes", [P, HALF], U32)
-        eye_plane = sb("eye_plane", [P, HALF], U8)
+        stage = placed("stage", [P, 2 * HALF + PACK * CAST_S], BF16, 6400)
+        eye_codes = [sb("eye_codes%d" % e, [P, 2 * P], U32) for e in range(2)]
+        eye_plane = [sb("eye_plane%d" % e, [P, 2 * P], U8) for e in range(2)]
+
+        def selectors(e, ones):
+            for u in range(2):
+                nc.vector.tensor_scalar(
+                    out=ones[:, u * HALF : (u + 1) * HALF], in0=ramp[:], scalar1=float(2 * u + e), scalar2=None,
+                    op0=ALU.is_equal,
+                )
+
+        selectors(0, stage)
         nc.vector.tensor_scalar(
             out=eye[:], in0=ramp[:, 0:HALF:PACK], scalar1=0.0, scalar2=None, op0=ALU.is_equal
         )
-        nc.vector.quantize_mx(
-            out=eye_codes[:].bitcast(E4M3), scales=eye_plane[:], in_=stage[:, eye_at : eye_at + PACK * HALF]
-        )
+        nc.vector.quantize_mx(out=eye_codes[0][:].bitcast(E4M3), scales=eye_plane[0][:], in_=stage[:, 0 : 2 * HALF])
 
-        q_codes = [sb("q_codes%d" % h, [P, HALF], U32) for h in range(2)]
-        q_plane = [sb("q_plane0", [P, HALF], U8)]
-        r_codes = [sb("r_codes%d" % h, [P, HALF], U32) for h in range(2)]
-        r_plane = [sb("r_plane%d" % h, [P, HALF], U8) for h in range(2)]
-        gate_t = sb("gate_t", [P, P], F32)
+        r_codes = [sb("r_codes%d" % c, [P, PIECE], U32) for c in range(4)]
+        r_plane = [sb("r_plane%d" % c, [P, PIECE], U8) for c in range(4)]
 
-        def quantise(codes, plane, fmt, src, j0, j1):
-            nc.vector.quantize_mx(
-                out=codes[:, j0:j1].bitcast(fmt), scales=plane[:, j0:j1], in_=src.rearrange("p j t -> p (j t)")
+        def quantise(codes, plane, fmt, src):
+            nc.vector.quantize_mx(out=codes.bitcast(fmt), scales=plane, in_=src.rearrange("p j t -> p (j t)"))
+
+        def move_codes(c):
+            src, dst = c * HALF, c * HALF + PIECE
+            code_bytes = wide_codes[:].bitcast(U8)
+            nc.vector.tensor_copy(
+                out=code_bytes[:, PACK * dst : PACK * (dst + PIECE) : 2],
+                in_=code_bytes[:, PACK * src + 1 : PACK * (src + PIECE) : 2],
             )
+            plane_words = wide_plane[:].bitcast(I32)
+            for at in ((dst,), (src, dst))[c]:
+                nc.vector.tensor_copy(out=plane_words[:, at // 4 : (at + PIECE) // 4], in_=made_plane[c].bitcast(I32))
 
-        def decode(h, t, acc):
-            cols = slice(t * P, (t + 1) * P)
+        def decode(codes, plane, t, acc):
+            cols = slice(t // 2 * P, (t // 2 + 1) * P)
             nc.tensor.matmul_mx(
-                out=acc[:], lhsT=eye_codes[:, cols].bitcast(E4M3), lhsT_scale=eye_plane[:, cols],
-                rhs=q_codes[h][:].bitcast(E5M2), rhs_scale=q_plane[h][:], start=True, stop=True,
+                out=acc[:], lhsT=eye_codes[t % 2][:, cols].bitcast(E4M3), lhsT_scale=eye_plane[t % 2][:, cols],
+                rhs=codes.bitcast(E5M2), rhs_scale=plane, start=True, stop=True,
             )
 
-        def leftover(h, t, acc, rest):
+        def leftover_pair(c, u, acc, pairs):
             nc.vector.tensor_tensor(
-                out=rest[:, t, :].rearrange("p (c j) -> p c j", c=2), in0=raw[h][:, :, t, :],
-                in1=acc[:].rearrange("p (c j) -> p c j", c=2), op=ALU.subtract,
+                out=pairs[:, u, :].rearrange("p (c i e) -> p c e i", i=4, e=2),
+                in0=raw[c][:, 2 * u : 2 * u + 2, :].rearrange("p e (c i) -> p c e i", i=4),
+                in1=acc[:].rearrange("p (e c i) -> p c e i", e=2, i=4), op=ALU.subtract,
             )
 
-        def turned_pass(codes, plane, fmt, u, acc, first):
+        def weave_pairs(dst, pairs):
+            nc.scalar.copy(
+                out=dst[:].rearrange("p j t -> p (j t)").bitcast(U32).rearrange("p (j u) -> p j u", u=2),
+                in_=pairs[:].bitcast(U32).rearrange("p u j -> p j u"),
+            )
+
+        def turned_first(codes, plane, acc):
+            nc.tensor.matmul_mx(
+                out=acc[:], lhsT=codes.bitcast(E5M2), lhsT_scale=plane,
+                rhs=w_codes[:].bitcast(E2M1), rhs_scale=w_plane, start=True, stop=False,
+            )
+
+        def turned_second(c, u, acc, n0, n1, stop):
             cols = slice(u * P, (u + 1) * P)
             nc.tensor.matmul_mx(
-                out=acc[:], lhsT=codes[:, cols].bitcast(fmt), lhsT_scale=plane[:, cols],
-                rhs=w_codes[:].bitcast(E2M1), rhs_scale=w_plane[:], start=first, stop=not first,
+                out=acc[:, n0:n1], lhsT=r_codes[c][:, cols].bitcast(E4M3), lhsT_scale=r_plane[c][:, cols],
+                rhs=w_codes[:, 2 * n0 : 2 * n1].bitcast(E2M1), rhs_scale=w_plane[:, n0:n1], start=False, stop=stop,
             )
 
-        def direct_pass(codes, plane, fmt, acc, first):
+        def direct_pass(b, codes, plane, fmt, dst, start, stop):
             nc.tensor.matmul_mx(
-                out=acc[:], lhsT=w_codes[:, 0 : 2 * P].bitcast(E2M1), lhsT_scale=w_plane[:, 0:P],
-                rhs=codes[:].bitcast(fmt), rhs_scale=plane[:], start=first, stop=not first,
+                out=dst, lhsT=w_codes[:, 2 * b * P : 2 * (b + 1) * P].bitcast(E2M1),
+                lhsT_scale=w_plane[:, b * P : (b + 1) * P], rhs=codes.bitcast(fmt), rhs_scale=plane,
+                start=start, stop=stop,
             )
 
-        def weigh(h, u, acc, dst, b0):
+        def weigh(tile, acc, dst, b0):
             src4 = acc[:].rearrange("p (b g s) -> p b g s", b=BLOCKS, s=16)
             dst4 = dst[:].rearrange("p (b g s) -> p b g s", b=BLOCKS, s=16)
             for g in range(GROUPS):
-                col = gate_column(h * TILES + u, g)
+                col = gate_column(tile, g)
                 nc.scalar.activation(
                     out=dst4[:, b0:, g, :], in_=src4[:, b0:, g, :], func=COPY, scale=gate_t[:, col : col + 1]
                 )
 
-        def turn(weighed, b, acc):
-            for u in range(TILES):
-                nc.tensor.transpose(acc[:, u * P : (u + 1) * P], weighed[u][:, b * P : (b + 1) * P], eye[:])
-
-        def turn_back(weighed, b, acc, dst):
-            turn(weighed, b, acc)
-            nc.scalar.copy(out=dst[:], in_=acc[:])
+        def turn_pair(weighed, b0, acc):
+            for b in range(2):
+                for u in range(2):
+                    at = b * PIECE + u * P
+                    nc.tensor.transpose(acc[:, at : at + P], weighed[u][:, (b0 + b) * P : (b0 + b + 1) * P], eye[:])
 
         def clear(page):
             nc.gpsimd.memset(page[:], 0.0)
             return page
 
-        def scatter(page, h, a, b):
-            nc.vector.tensor_tensor(
-                out=page[:].indirect(offsets[:, 32 * h : 32 * (h + 1)]), in0=a, in1=b, op=ALU.mult
-            )
+        def window(b, c0, c1):
+            return pages[b][:].indirect(offsets[:, 16 * c0 : 16 * c1])
 
-        at0 = eye_at + PACK * (HALF - CAST_V)
-        woven = stage[:, at0 : at0 + PACK * PIECE].rearrange("p (j t) -> p j t", t=PACK)
-        weave(nc.vector.tensor_copy, woven, raw[0][:, 0], 0, CAST_V)
-        weave(nc.scalar.copy, woven, raw[0][:, 0], CAST_V, PIECE)
-        quantise(q_codes[0], q_plane[0], E5M2, woven, 0, PIECE)
-        woven = stage[:, 0 : PACK * PIECE].rearrange("p (j t) -> p j t", t=PACK)
-        weave(nc.vector.tensor_copy, woven, raw[0][:, 1], CAST_S, PIECE)
-        weave(nc.scalar.copy, woven, raw[0][:, 1], 0, CAST_S)
-        quantise(q_codes[0], q_plane[0], E5M2, woven, PIECE, HALF)
-        pages = [clear(sb("page0", [P, T], F32, tag="slot0"))]
-        woven1 = sb("woven1", [P, HALF, PACK], BF16)
-        for c in range(2):
-            weave(nc.scalar.copy, woven1[:, c * PIECE : (c + 1) * PIECE, :], raw[1][:, c], 0, PIECE)
+        def scatter(dst, x, y):
+            nc.vector.tensor_tensor(out=dst, in0=x, in1=y, op=ALU.mult)
 
-        rest0 = lap.tile([P, PACK, HALF], BF16, name="rest0", offset=0, align_bytes=64)
-        decoded = [bank("decoded0_%d" % t, t) for t in range(PACK)]
-        for t in range(PACK):
-            decode(0, t, decoded[t])
-        for t in range(2):
-            leftover(0, t, decoded[t], rest0)
+        def place(b, c, x):
+            nc.vector.tensor_copy(out=window(b, c, c + 1), in_=x)
+
+        q_codes = [wide_codes[:, c * HALF : c * HALF + PIECE] for c in range(2)]
+        q_plane = [wide_plane[:, c * HALF : c * HALF + PIECE] for c in range(2)]
+        plane1 = placed("plane1", [P, PIECE], U8, 15360)
+        made_plane = [q_plane[0], plane1[:]]
+        woven0 = stage[:, PACK * CAST_S :].rearrange("p (j t) -> p j t", t=PACK)
+        weave(nc.vector.tensor_copy, woven0, raw[0], 0, CAST_V)
+        weave(nc.scalar.copy, woven0, raw[0], CAST_V, PIECE)
+        quantise(q_codes[0], q_plane[0], E5M2, woven0)
+        move_codes(0)
+        woven1 = placed("woven1", [P, PIECE, PACK], BF16, 8704)
+        weave(nc.vector.tensor_copy, woven1, raw[1], 0, CAST_VB)
+        weave(nc.scalar.copy, woven1, raw[1], CAST_VB, PIECE)
+        quantise(q_codes[1], made_plane[1], E5M2, woven1[:])
+        move_codes(1)
+        odd_ones = sb("odd_ones", [P, 2 * HALF], BF16)
+        selectors(1, odd_ones)
+        nc.vector.quantize_mx(out=eye_codes[1][:].bitcast(E4M3), scales=eye_plane[1][:], in_=odd_ones[:])
+        woven2 = placed("woven2", [P, PIECE, PACK], BF16, 5632)
+        weave(nc.scalar.copy, woven2, raw[2], 0, PIECE)
+        pages.append(clear(placed("page1", [P, T], F32, 15360)))
+
+        pairs = [placed("pairs0", [P, 2, HALF], BF16, 9216), sb("pairs1", [P, 2, HALF], BF16)]
         for c in range(2):
-            for t in (2, 3):
-                nc.vector.tensor_tensor(
-                    out=rest0[:, t, c * PIECE : (c + 1) * PIECE], in0=raw[0][:, c, t, :],
-                    in1=decoded[t][:, c * PIECE : (c + 1) * PIECE], op=ALU.subtract,
-                )
-        gate_bank = bank("gate_bank", 0)
+            decoded = [bank("decoded%d_%d" % (c, u), 2 * c + u) for u in range(2)]
+            win = slice(c * HALF, (c + 1) * HALF)
+            for u in range(2):
+                decode(wide_codes[:, win], wide_plane[:, win], 2 * u, decoded[u])
+            for u in range(2):
+                leftover_pair(c, u, decoded[u], pairs[c])
+        direct = [bank("direct%d" % b, 2 + b) for b in range(2)]
+        for b in range(2):
+            direct_pass(b, wide_codes[:, 0:HALF], wide_plane[:, 0:HALF], E5M2, direct[b][:], True, False)
+        turned = [bank("turned0_%d" % u, u) for u in range(2)]
+        for u in range(2):
+            turned_first(q_codes[0][:, u * P : (u + 1) * P], q_plane[0][:, u * P : (u + 1) * P], turned[u])
+        woven3 = [placed("woven3a", [P, P, PACK], BF16, 7680), placed("woven3b", [P, P, PACK], BF16, 32768)]
+        rest = [sb("rest0", [P, PIECE, PACK], BF16), placed("rest1", [P, PIECE, PACK], BF16, 34816)]
+        weave(nc.scalar.copy, woven3[0], raw[3][:, :, 0:P], 0, P)
+        weave_pairs(rest[0], pairs[0])
+        weave(nc.scalar.copy, woven3[1], raw[3][:, :, P:PIECE], 0, P)
+        weave_pairs(rest[1], pairs[1])
+        gate_bank = bank("gate_bank", 4)
+        gate_t = placed("gate_t", [P, P], F32, 10752)
         nc.tensor.transpose(gate_bank[:, 0:P], gate_rows[:], eye[:])
         nc.scalar.copy(out=gate_t[:], in_=gate_bank[:, 0:P])
-        direct = bank("direct", 1)
-        direct_pass(q_codes[0], q_plane[0], E5M2, direct, True)
-        q_plane.append(sb("q_plane1", [P, HALF], U8, tag="slot4"))
-        quantise(q_codes[1], q_plane[1], E5M2, woven1[:], 0, HALF)
-        decoded = [bank("decoded1_%d" % t, (4, 5, 6, 7)[t]) for t in range(PACK)]
+        quantise(r_codes[0][:], r_plane[0][:], E4M3, rest[0][:])
+        late_codes = placed("late_codes", [P, HALF], U32, 8704)
+        late_plane = sb("late_plane", [P, HALF], U8)
+        quantise(late_codes[:, 0:PIECE], late_plane[:, 0:PIECE], E5M2, woven2[:])
+        for k in range(2):
+            cols = slice(PIECE + k * P, PIECE + (k + 1) * P)
+            quantise(late_codes[:, cols], late_plane[:, cols], E5M2, woven3[k][:])
+        for b in range(2):
+            for u in range(2):
+                cols = slice(u * P, (u + 1) * P)
+                direct_pass(b, r_codes[0][:, cols], r_plane[0][:, cols], E4M3, direct[b][:, cols], False, u == 1)
+        for u in range(2):
+            for b in (2, 3):
+                turned_second(0, u, turned[u], b * P, (b + 1) * P, b == 3)
+        quantise(r_codes[1][:], r_plane[1][:], E4M3, rest[1][:])
+        first = sb("first", [P, 2, PIECE], F32, tag="pairs1")
+        for b in range(2):
+            nc.vector.tensor_tensor(out=first[:, b, :], in0=direct[b][:, 0:PIECE], in1=d_first[:, b, :], op=ALU.mult)
+        pages.append(clear(placed("page2", [P, T], F32, 27648)))
+        pages.append(clear(placed("page3", [P, T], F32, 35840)))
+        decoded = [bank("decoded_late%d" % t, 4 + t) for t in range(PACK)]
         for t in range(PACK):
-            decode(1, t, decoded[t])
-        turned = [bank("turned0_%d" % u, (0, 2, 3)[u]) for u in range(TILES - 1)]
-        for u in range(TILES - 1):
-            turned_pass(q_codes[0], q_plane[0], E5M2, u, turned[u], True)
-        rest0_woven = sb("rest0_woven", [P, HALF, PACK], BF16, tag="slot5")
-        weave(nc.scalar.copy, rest0_woven, rest0, 0, PIECE)
-        weave(nc.vector.tensor_copy, rest0_woven, rest0, HALF - WEAVE_V, HALF)
-        weave(nc.scalar.copy, rest0_woven, rest0, PIECE, HALF - WEAVE_V)
-        for c in range(2):
-            quantise(r_codes[0], r_plane[0], E4M3, rest0_woven[:, c * PIECE : (c + 1) * PIECE, :], c * PIECE, (c + 1) * PIECE)
-        direct_pass(r_codes[0], r_plane[0], E4M3, direct, False)
-        for u in range(TILES - 1):
-            turned_pass(r_codes[0], r_plane[0], E4M3, u, turned[u], False)
-        first = sb("first", [P, HALF], F32)
-        nc.scalar.copy(out=first[:], in_=direct[:])
-        factor = sb("factor", [P, HALF], F32, tag="slot5")
-        nc.gpsimd.tensor_tensor(out=factor[:], in0=d_first[:], in1=gate[:], op=ALU.mult)
-        pages.append(clear(sb("page1", [P, T], F32, tag="slot1")))
-        pages.append(clear(sb("page2", [P, T], F32, tag="slot2")))
-        rest1 = lap.tile([P, PACK, HALF], BF16, name="rest1", offset=0, align_bytes=64)
-        for t in range(PACK):
-            leftover(1, t, decoded[t], rest1)
-        turned.append(bank("turned0_3", 4))
-        turned_pass(q_codes[0], q_plane[0], E5M2, TILES - 1, turned[TILES - 1], True)
-        turned_pass(r_codes[0], r_plane[0], E4M3, TILES - 1, turned[TILES - 1], False)
-        scatter(pages[0], 0, first[:], factor[:])
+            decode(late_codes[:], late_plane[:], t, decoded[t])
+        for b in range(2):
+            scatter(window(b, 0, 1), first[:, b, :], gate[:])
 
-        weighed0 = [sb("weighed0_%d" % u, [P, N], F32, tag="slot6" if u == TILES - 1 else None) for u in range(TILES)]
-        for u in range(TILES):
-            weigh(0, u, turned[u], weighed0[u], 1)
-        back_banks = [bank("back_bank0_%d" % b, (1, 6, 7)[b - 1]) for b in (1, 2, 3)]
-        late = bank("late", 5)
-        for u in range(TILES):
-            dst = back_banks[0][:, u * P : (u + 1) * P] if u < TILES - 1 else late[:, 0:P]
-            nc.tensor.transpose(dst, weighed0[u][:, P : 2 * P], eye[:])
-        for b in (2, 3):
-            turn(weighed0, b, back_banks[b - 1])
-        back0 = [sb("back0_1", [P, HALF], F32)] + [
-            lap.tile([P, HALF], F32, name="back0_%d" % b, offset=2048 * (b - 2), align_bytes=64) for b in (2, 3)
-        ]
-        nc.scalar.copy(out=back0[0][:, 0 : HALF - P], in_=back_banks[0][:, 0 : HALF - P])
-        nc.scalar.copy(out=back0[0][:, HALF - P : HALF], in_=late[:, 0:P])
-        scatter(pages[1], 0, back0[0][:], d_rest[:, 0, :])
-        rest1_woven = sb("rest1_woven", [P, HALF, PACK], BF16, tag="slot6")
-        weave(nc.scalar.copy, rest1_woven, rest1, 0, PIECE)
-        weave(nc.scalar.copy, rest1_woven, rest1, PIECE, HALF)
-        quantise(r_codes[1], r_plane[1], E4M3, rest1_woven[:], 0, HALF)
-        pages.append(clear(sb("page3", [P, T], F32, tag="slot6")))
-        nc.scalar.copy(out=back0[1][:], in_=back_banks[1][:])
-        nc.scalar.copy(out=back0[2][:], in_=back_banks[2][:])
-        turned = [bank("turned1_%d" % u, (4, 1, 5, 6)[u]) for u in range(TILES)]
-        for u in range(TILES):
-            turned_pass(q_codes[1], q_plane[1], E5M2, u, turned[u], True)
-        for u in range(TILES):
-            turned_pass(r_codes[1], r_plane[1], E4M3, u, turned[u], False)
-        scatter(pages[2], 0, back0[1][:], d_rest[:, 1, :])
-        scatter(pages[3], 0, back0[2][:], d_rest[:, 2, :])
-        weighed1 = [sb("weighed1_%d" % u, [P, N], F32) for u in range(TILES)]
-        for u in range(TILES):
-            weigh(1, u, turned[u], weighed1[u], 0)
-        for b in range(BLOCKS):
-            back = sb("back1_%d" % b, [P, HALF], F32)
-            turn_back(weighed1, b, bank("back_bank1_%d" % b, (0, 2, 3, 7)[b]), back)
-            scatter(pages[b], 1, back[:], d_second[:, b, :])
+        weighed = [sb("weighed0_%d" % u, [P, N], F32) for u in range(2)]
+        for u in range(2):
+            weigh(u, turned[u], weighed[u], 2)
+        back_bank = bank("back_bank0", 0)
+        turn_pair(weighed, 2, back_bank)
+        values = sb("values0", [P, 2, PIECE], F32)
+        for b in range(2):
+            nc.vector.tensor_tensor(
+                out=values[:, b, :], in0=back_bank[:, b * PIECE : (b + 1) * PIECE], in1=d_next[:, b, :], op=ALU.mult
+            )
+        for b in range(2):
+            place(2 + b, 0, values[:, b, :])
+        known = [sb("known0", [P, PACK, PIECE], F32)]
+        for t in range(PACK):
+            nc.scalar.copy(out=known[0][:, t, :], in_=decoded[t][:, 0:PIECE])
+
+        def product(c, codes, plane, banks):
+            turned = [bank("turned%d_%d" % (c, u), banks[u]) for u in range(2)]
+            for u in range(2):
+                turned_first(codes[:, u * P : (u + 1) * P], plane[:, u * P : (u + 1) * P], turned[u])
+            for u in range(2):
+                turned_second(c, u, turned[u], 0, N, True)
+            weighed = [sb("weighed%d_%d" % (c, u), [P, N], F32) for u in range(2)]
+            for u in range(2):
+                weigh(2 * c + u, turned[u], weighed[u], 0)
+            accs = [bank("back_bank%d_%d" % (c, k), banks[2 + k]) for k in range(2)]
+            for k in range(2):
+                turn_pair(weighed, 2 * k, accs[k])
+            return accs
+
+        def late_leftover(c, k, dst):
+            cols = slice(k * P, (k + 1) * P)
+            nc.gpsimd.tensor_tensor(
+                out=dst.rearrange("p (c i) t -> p c t i", i=4),
+                in0=raw[2 + c][:, :, cols].rearrange("p t (c i) -> p c t i", i=4),
+                in1=known[c][:, :, cols].rearrange("p t (c i) -> p c t i", i=4), op=ALU.subtract,
+            )
+
+        accs = product(1, q_codes[1], q_plane[1], (2, 3, 1, 0))
+        backs = [placed("back1_0", [P, HALF], F32, 49152), sb("back1_1", [P, HALF], F32)]
+        for k in range(2):
+            nc.scalar.copy(out=backs[k][:], in_=accs[k][:])
+        known.append(sb("known1", [P, PACK, PIECE], F32, tag="weighed1_1"))
+        for t in range(PACK):
+            nc.scalar.copy(out=known[1][:, t, :], in_=decoded[t][:, PIECE:HALF])
+        late = [placed("late0", [P, P, PACK], BF16, 48128)]
+        late_leftover(0, 0, late[0][:])
+        values = sb("values1_0", [P, 2, PIECE], F32)
+        nc.gpsimd.tensor_tensor(
+            out=values[:], in0=backs[0][:].rearrange("p (b j) -> p b j", b=2), in1=d_second[0][:], op=ALU.mult
+        )
+        quantise(r_codes[2][:, 0:P], r_plane[2][:, 0:P], E4M3, late[0][:])
+        late.append(placed("late1", [P, P, PACK], BF16, 48640))
+        late_leftover(0, 1, late[1][:])
+        for b in range(2):
+            place(b, 1, values[:, b, :])
+        quantise(r_codes[2][:, P:PIECE], r_plane[2][:, P:PIECE], E4M3, late[1][:])
+        values = placed("values1_1", [P, 2, PIECE], F32, 46592)
+        nc.gpsimd.tensor_tensor(
+            out=values[:], in0=backs[1][:].rearrange("p (b j) -> p b j", b=2), in1=d_second[1][:], op=ALU.mult
+        )
+        for b in range(2):
+            place(2 + b, 1, values[:, b, :])
+        late = placed("late2", [P, PIECE, PACK], BF16, 48640)
+        for k in range(2):
+            late_leftover(1, k, late[:, k * P : (k + 1) * P, :])
+        quantise(r_codes[3][:], r_plane[3][:], E4M3, late[:])
+
+        accs = product(2, late_codes[:, 0:PIECE], late_plane[:, 0:PIECE], (1, 0, 2, 3))
+        third = sb("third", [P, 5, PIECE], F32, tag="weighed1_1")
+        for b in range(2):
+            nc.scalar.copy(out=third[:, b, :], in_=accs[0][:, b * PIECE : (b + 1) * PIECE])
+        nc.scalar.copy(out=third[:, 2:4, :], in_=accs[1][:].rearrange("p (b j) -> p b j", b=2))
+        for b in range(3):
+            scatter(window(b, 2, 3), third[:, b, :], d_late[:, b, 0:PIECE])
+        accs = product(3, late_codes[:, PIECE:HALF], late_plane[:, PIECE:HALF], (4, 5, 6, 7))
+        fourth = sb("fourth", [P, 3, PIECE], F32)
+        nc.scalar.copy(out=fourth[:, 0:2, :], in_=accs[0][:].rearrange("p (b j) -> p b j", b=2))
+        nc.scalar.copy(out=fourth[:, 2, :], in_=accs[1][:, 0:PIECE])
+        nc.scalar.copy(out=third[:, 4, :], in_=accs[1][:, PIECE:HALF])
+        for b in range(3):
+            scatter(window(b, 3, 4), fourth[:, b, :], d_late[:, b, PIECE:HALF])
             nc.sync.dma_start(out=out[b * P : (b + 1) * P, :], in_=pages[b][:])
+        scatter(window(3, 2, 4), third[:, 3:5, :].rearrange("p c j -> p (c j)"), d_late[:, 3, :])
+        nc.sync.dma_start(out=out[3 * P : 4 * P, :], in_=pages[3][:])

@@ -88,20 +88,17 @@ def tile_list_embg_tgq4_mul_kernel(tc, dy, w_words, w_scales, d, wgo, offs, out)
         d_first = sb("d_first", [P, 2, PIECE], F32)
         gate = sb("gate", [P, PIECE], F32)
         d_next = sb("d_next", [P, 2, PIECE], F32)
-        d_second = [placed("d_second0", [P, 2, PIECE], F32, 46080), sb("d_second1", [P, 2, PIECE], F32)]
+        d_second = sb("d_second", [P, BLOCKS, PIECE], F32)
         d_late = sb("d_late", [P, BLOCKS, HALF], F32)
         nc.sync.dma_start(out=d_first[:], in_=d_view[:, 0:2, 0:PIECE])
         nc.sync.dma_start(out=gate[:], in_=wgo[:, 0:PIECE])
         nc.sync.dma_start(offsets[:], offs)
         nc.sync.dma_start(out=d_next[:], in_=d_view[:, 2:4, 0:PIECE])
-        for k in range(2):
-            nc.sync.dma_start(out=d_second[k][:], in_=d_view[:, 2 * k : 2 * k + 2, PIECE:HALF])
+        nc.sync.dma_start(out=d_second[:], in_=d_view[:, :, PIECE:HALF])
         nc.sync.dma_start(out=d_late[:], in_=d_view[:, :, HALF:J])
 
         wide_codes = sb("wide_codes", [P, 2 * HALF], U32)
         wide_plane = sb("wide_plane", [P, 2 * HALF], U8)
-        nc.vector.memset(wide_codes[:].rearrange("p (c j) -> p c j", j=PIECE)[:, 1:4:2, :], 0)
-        nc.vector.memset(pages[0][:, CLEAR_ODD - 1 : T], 0.0)
 
         ramp = sb("ramp", [P, HALF], BF16)
         nc.gpsimd.iota(
@@ -119,10 +116,8 @@ def tile_list_embg_tgq4_mul_kernel(tc, dy, w_words, w_scales, d, wgo, offs, out)
                     op0=ALU.is_equal,
                 )
 
+        nc.vector.memset(pages[0][:, CLEAR_ODD - 1 : T], 0.0)
         selectors(0, stage)
-        nc.vector.tensor_scalar(
-            out=eye[:], in0=ramp[:, 0:HALF:PACK], scalar1=0.0, scalar2=None, op0=ALU.is_equal
-        )
         nc.vector.quantize_mx(out=eye_codes[0][:].bitcast(E4M3), scales=eye_plane[0][:], in_=stage[:, 0 : 2 * HALF])
 
         r_codes = [sb("r_codes%d" % c, [P, PIECE], U32) for c in range(4)]
@@ -133,14 +128,14 @@ def tile_list_embg_tgq4_mul_kernel(tc, dy, w_words, w_scales, d, wgo, offs, out)
 
         def move_codes(c):
             src, dst = c * HALF, c * HALF + PIECE
+            plane_words = wide_plane[:].bitcast(I32)
+            for at in ((dst,), (src, dst))[c]:
+                nc.vector.tensor_copy(out=plane_words[:, at // 4 : (at + PIECE) // 4], in_=made_plane[c].bitcast(I32))
             code_bytes = wide_codes[:].bitcast(U8)
             nc.vector.tensor_copy(
                 out=code_bytes[:, PACK * dst : PACK * (dst + PIECE) : 2],
                 in_=code_bytes[:, PACK * src + 1 : PACK * (src + PIECE) : 2],
             )
-            plane_words = wide_plane[:].bitcast(I32)
-            for at in ((dst,), (src, dst))[c]:
-                nc.vector.tensor_copy(out=plane_words[:, at // 4 : (at + PIECE) // 4], in_=made_plane[c].bitcast(I32))
 
         def decode(codes, plane, t, acc):
             cols = slice(t // 2 * P, (t // 2 + 1) * P)
@@ -151,9 +146,9 @@ def tile_list_embg_tgq4_mul_kernel(tc, dy, w_words, w_scales, d, wgo, offs, out)
 
         def leftover_pair(c, u, acc, pairs):
             nc.vector.tensor_tensor(
-                out=pairs[:, u, :].rearrange("p (c i e) -> p c e i", i=4, e=2),
-                in0=raw[c][:, 2 * u : 2 * u + 2, :].rearrange("p e (c i) -> p c e i", i=4),
-                in1=acc[:].rearrange("p (e c i) -> p c e i", e=2, i=4), op=ALU.subtract,
+                out=pairs[:, u, :].rearrange("p (j e) -> p j e", e=2),
+                in0=raw[c][:, 2 * u : 2 * u + 2, :].rearrange("p e j -> p j e"),
+                in1=acc[:].rearrange("p (e j) -> p j e", e=2), op=ALU.subtract,
             )
 
         def weave_pairs(dst, pairs):
@@ -215,8 +210,15 @@ def tile_list_embg_tgq4_mul_kernel(tc, dy, w_words, w_scales, d, wgo, offs, out)
         plane1 = placed("plane1", [P, PIECE], U8, 15360)
         made_plane = [q_plane[0], plane1[:]]
         woven0 = stage[:, PACK * CAST_S :].rearrange("p (j t) -> p j t", t=PACK)
+        nc.vector.memset(wide_codes[:].rearrange("p (c j) -> p c j", j=PIECE)[:, 1:4:2, :], 0)
+        odd_ones = placed("odd_ones", [P, 2 * HALF], BF16, 9216)
+        selectors(1, odd_ones)
+        nc.vector.tensor_scalar(
+            out=eye[:], in0=ramp[:, 0:HALF:PACK], scalar1=0.0, scalar2=None, op0=ALU.is_equal
+        )
         weave(nc.vector.tensor_copy, woven0, raw[0], 0, CAST_V)
         weave(nc.scalar.copy, woven0, raw[0], CAST_V, PIECE)
+        nc.vector.quantize_mx(out=eye_codes[1][:].bitcast(E4M3), scales=eye_plane[1][:], in_=odd_ones[:])
         quantise(q_codes[0], q_plane[0], E5M2, woven0)
         move_codes(0)
         woven1 = placed("woven1", [P, PIECE, PACK], BF16, 8704)
@@ -224,9 +226,6 @@ def tile_list_embg_tgq4_mul_kernel(tc, dy, w_words, w_scales, d, wgo, offs, out)
         weave(nc.scalar.copy, woven1, raw[1], CAST_VB, PIECE)
         quantise(q_codes[1], made_plane[1], E5M2, woven1[:])
         move_codes(1)
-        odd_ones = sb("odd_ones", [P, 2 * HALF], BF16)
-        selectors(1, odd_ones)
-        nc.vector.quantize_mx(out=eye_codes[1][:].bitcast(E4M3), scales=eye_plane[1][:], in_=odd_ones[:])
         woven2 = placed("woven2", [P, PIECE, PACK], BF16, 5632)
         weave(nc.scalar.copy, woven2, raw[2], 0, PIECE)
         pages.append(clear(placed("page1", [P, T], F32, 15360)))
@@ -275,7 +274,7 @@ def tile_list_embg_tgq4_mul_kernel(tc, dy, w_words, w_scales, d, wgo, offs, out)
             nc.vector.tensor_tensor(out=first[:, b, :], in0=direct[b][:, 0:PIECE], in1=d_first[:, b, :], op=ALU.mult)
         pages.append(clear(placed("page2", [P, T], F32, 27648)))
         pages.append(clear(placed("page3", [P, T], F32, 35840)))
-        decoded = [bank("decoded_late%d" % t, 4 + t) for t in range(PACK)]
+        decoded = [bank("decoded_late%d" % t, (5, 6, 7, 2)[t]) for t in range(PACK)]
         for t in range(PACK):
             decode(late_codes[:], late_plane[:], t, decoded[t])
         for b in range(2):
@@ -293,6 +292,7 @@ def tile_list_embg_tgq4_mul_kernel(tc, dy, w_words, w_scales, d, wgo, offs, out)
             )
         for b in range(2):
             place(2 + b, 0, values[:, b, :])
+
         known = [sb("known0", [P, PACK, PIECE], F32)]
         for t in range(PACK):
             nc.scalar.copy(out=known[0][:, t, :], in_=decoded[t][:, 0:PIECE])
@@ -319,44 +319,43 @@ def tile_list_embg_tgq4_mul_kernel(tc, dy, w_words, w_scales, d, wgo, offs, out)
                 in1=known[c][:, :, cols].rearrange("p t (c i) -> p c t i", i=4), op=ALU.subtract,
             )
 
-        accs = product(1, q_codes[1], q_plane[1], (2, 3, 1, 0))
-        backs = [placed("back1_0", [P, HALF], F32, 49152), sb("back1_1", [P, HALF], F32)]
+        accs = product(1, q_codes[1], q_plane[1], (4, 3, 1, 0))
+        backs = sb("backs", [P, BLOCKS, PIECE], F32)
         for k in range(2):
-            nc.scalar.copy(out=backs[k][:], in_=accs[k][:])
+            nc.scalar.copy(out=backs[:, 2 * k : 2 * k + 2, :], in_=accs[k][:].rearrange("p (b j) -> p b j", b=2))
         known.append(sb("known1", [P, PACK, PIECE], F32, tag="weighed1_1"))
         for t in range(PACK):
             nc.scalar.copy(out=known[1][:, t, :], in_=decoded[t][:, PIECE:HALF])
-        late = [placed("late0", [P, P, PACK], BF16, 48128)]
-        late_leftover(0, 0, late[0][:])
+
+        def times_d(dst, b):
+            nc.gpsimd.tensor_tensor(out=dst, in0=backs[:, b, :], in1=d_second[:, b, :], op=ALU.mult)
+
         values = sb("values1_0", [P, 2, PIECE], F32)
-        nc.gpsimd.tensor_tensor(
-            out=values[:], in0=backs[0][:].rearrange("p (b j) -> p b j", b=2), in1=d_second[0][:], op=ALU.mult
-        )
-        quantise(r_codes[2][:, 0:P], r_plane[2][:, 0:P], E4M3, late[0][:])
-        late.append(placed("late1", [P, P, PACK], BF16, 48640))
-        late_leftover(0, 1, late[1][:])
+        late = placed("late0", [P, PIECE, PACK], BF16, 47104)
+        times_d(values[:, 0, :], 0)
+        place(0, 1, values[:, 0, :])
+        for k in range(2):
+            late_leftover(0, k, late[:, k * P : (k + 1) * P, :])
+        quantise(r_codes[2][:], r_plane[2][:], E4M3, late[:])
+        times_d(values[:, 1, :], 1)
+        place(1, 1, values[:, 1, :])
+        values = placed("values1_1", [P, 2, PIECE], F32, 46080)
         for b in range(2):
-            place(b, 1, values[:, b, :])
-        quantise(r_codes[2][:, P:PIECE], r_plane[2][:, P:PIECE], E4M3, late[1][:])
-        values = placed("values1_1", [P, 2, PIECE], F32, 46592)
-        nc.gpsimd.tensor_tensor(
-            out=values[:], in0=backs[1][:].rearrange("p (b j) -> p b j", b=2), in1=d_second[1][:], op=ALU.mult
-        )
-        for b in range(2):
+            times_d(values[:, b, :], 2 + b)
             place(2 + b, 1, values[:, b, :])
-        late = placed("late2", [P, PIECE, PACK], BF16, 48640)
+        late = placed("late1", [P, PIECE, PACK], BF16, 48128)
         for k in range(2):
             late_leftover(1, k, late[:, k * P : (k + 1) * P, :])
         quantise(r_codes[3][:], r_plane[3][:], E4M3, late[:])
 
-        accs = product(2, late_codes[:, 0:PIECE], late_plane[:, 0:PIECE], (1, 0, 2, 3))
+        accs = product(2, late_codes[:, 0:PIECE], late_plane[:, 0:PIECE], (1, 0, 4, 3))
         third = sb("third", [P, 5, PIECE], F32, tag="weighed1_1")
         for b in range(2):
             nc.scalar.copy(out=third[:, b, :], in_=accs[0][:, b * PIECE : (b + 1) * PIECE])
         nc.scalar.copy(out=third[:, 2:4, :], in_=accs[1][:].rearrange("p (b j) -> p b j", b=2))
         for b in range(3):
             scatter(window(b, 2, 3), third[:, b, :], d_late[:, b, 0:PIECE])
-        accs = product(3, late_codes[:, PIECE:HALF], late_plane[:, PIECE:HALF], (4, 5, 6, 7))
+        accs = product(3, late_codes[:, PIECE:HALF], late_plane[:, PIECE:HALF], (5, 6, 7, 2))
         fourth = sb("fourth", [P, 3, PIECE], F32)
         nc.scalar.copy(out=fourth[:, 0:2, :], in_=accs[0][:].rearrange("p (b j) -> p b j", b=2))
         nc.scalar.copy(out=fourth[:, 2, :], in_=accs[1][:, 0:PIECE])

@@ -26,8 +26,9 @@ BLOCKS = N // P
 TILES = HALF // P
 CAST_V = 160
 CAST_S = PIECE - CAST_V
-CAST_VB = 128
+CAST_VB = 96
 CLEAR_ODD = 769
+CLEAR_WAIT = 400
 GATE_FIRST, GATE_STEP = 70, 7
 
 
@@ -67,11 +68,6 @@ def tile_list_embg_tgq4_mul_kernel(tc, dy, w_words, w_scales, d, wgo, offs, out)
         raw = [placed("raw0", [P, PACK, PIECE], F32, 32768)] + [sb("raw%d" % c, [P, PACK, PIECE], F32) for c in (1, 2, 3)]
         for c in range(2):
             nc.sync.dma_start(out=raw[c][:], in_=dy_view[:, :, c * PIECE : (c + 1) * PIECE])
-        gate_rows = sb("gate_rows", [P, P], F32)
-        nc.sync.dma_start(
-            out=gate_rows[:],
-            in_=wgo.rearrange("r (u j) -> (r u) j", j=P)[GATE_FIRST : GATE_FIRST + GATE_STEP * (P - 1) + 1 : GATE_STEP, :],
-        )
         for c in (2, 3):
             nc.sync.dma_start(out=raw[c][:], in_=dy_view[:, :, c * PIECE : (c + 1) * PIECE])
         pages = [sb("page0", [P, T], F32)]
@@ -85,6 +81,11 @@ def tile_list_embg_tgq4_mul_kernel(tc, dy, w_words, w_scales, d, wgo, offs, out)
             nc.sync.dma_start(
                 out=w_plane[32 * q : 32 * q + 4, :].bitcast(I32), in_=w_scales[0, 4 * q : 4 * q + 4, :].bitcast(I32)
             )
+        gate_rows = sb("gate_rows", [P, P], F32)
+        nc.sync.dma_start(
+            out=gate_rows[:],
+            in_=wgo.rearrange("r (u j) -> (r u) j", j=P)[GATE_FIRST : GATE_FIRST + GATE_STEP * (P - 1) + 1 : GATE_STEP, :],
+        )
         d_first = sb("d_first", [P, 2, PIECE], F32)
         gate = sb("gate", [P, PIECE], F32)
         d_next = sb("d_next", [P, 2, PIECE], F32)
@@ -105,8 +106,8 @@ def tile_list_embg_tgq4_mul_kernel(tc, dy, w_words, w_scales, d, wgo, offs, out)
             ramp[:], pattern=[[1, HALF]], base=0, channel_multiplier=-PACK, allow_small_or_imprecise_dtypes=True
         )
         eye = sb("eye", [P, P], F32)
-        stage = placed("stage", [P, 2 * HALF + PACK * CAST_S], BF16, 6400)
-        eye_codes = [sb("eye_codes%d" % e, [P, 2 * P], U32) for e in range(2)]
+        even_ones = placed("even_ones", [P, 2 * HALF], BF16, 1536)
+        eye_codes = [sb("eye_codes0", [P, 2 * P], U32)]
         eye_plane = [sb("eye_plane%d" % e, [P, 2 * P], U8) for e in range(2)]
 
         def selectors(e, ones):
@@ -116,9 +117,11 @@ def tile_list_embg_tgq4_mul_kernel(tc, dy, w_words, w_scales, d, wgo, offs, out)
                     op0=ALU.is_equal,
                 )
 
-        nc.vector.memset(pages[0][:, CLEAR_ODD - 1 : T], 0.0)
-        selectors(0, stage)
-        nc.vector.quantize_mx(out=eye_codes[0][:].bitcast(E4M3), scales=eye_plane[0][:], in_=stage[:, 0 : 2 * HALF])
+        nc.vector.memset(pages[0][:, CLEAR_ODD - 1 : T - 2 * CLEAR_WAIT], 0.0)
+        selectors(0, even_ones)
+        nc.scalar.copy(out=eye[:], in_=even_ones[:, 0:HALF:PACK])
+        nc.vector.memset(wide_codes[:, PIECE:HALF], 0)
+        nc.vector.quantize_mx(out=eye_codes[0][:].bitcast(E4M3), scales=eye_plane[0][:], in_=even_ones[:])
 
         r_codes = [sb("r_codes%d" % c, [P, PIECE], U32) for c in range(4)]
         r_plane = [sb("r_plane%d" % c, [P, PIECE], U8) for c in range(4)]
@@ -209,28 +212,29 @@ def tile_list_embg_tgq4_mul_kernel(tc, dy, w_words, w_scales, d, wgo, offs, out)
         q_plane = [wide_plane[:, c * HALF : c * HALF + PIECE] for c in range(2)]
         plane1 = placed("plane1", [P, PIECE], U8, 15360)
         made_plane = [q_plane[0], plane1[:]]
-        woven0 = stage[:, PACK * CAST_S :].rearrange("p (j t) -> p j t", t=PACK)
-        nc.vector.memset(wide_codes[:].rearrange("p (c j) -> p c j", j=PIECE)[:, 1:4:2, :], 0)
-        odd_ones = placed("odd_ones", [P, 2 * HALF], BF16, 9216)
-        selectors(1, odd_ones)
-        nc.vector.tensor_scalar(
-            out=eye[:], in0=ramp[:, 0:HALF:PACK], scalar1=0.0, scalar2=None, op0=ALU.is_equal
-        )
+        stage = placed("stage", [P, PACK * (2 * PIECE - CAST_VB)], BF16, 2560)
+        woven0 = stage[:, 0 : PACK * PIECE].rearrange("p (j t) -> p j t", t=PACK)
+        nc.vector.memset(wide_codes[:, HALF + PIECE : 2 * HALF], 0)
         weave(nc.vector.tensor_copy, woven0, raw[0], 0, CAST_V)
         weave(nc.scalar.copy, woven0, raw[0], CAST_V, PIECE)
-        nc.vector.quantize_mx(out=eye_codes[1][:].bitcast(E4M3), scales=eye_plane[1][:], in_=odd_ones[:])
+        odd_ones = placed("odd_ones", [P, 2 * HALF], BF16, 512)
+        selectors(1, odd_ones)
         quantise(q_codes[0], q_plane[0], E5M2, woven0)
+        eye_codes.append(sb("eye_codes1", [P, 2 * P], U32))
+        nc.vector.quantize_mx(out=eye_codes[1][:].bitcast(E4M3), scales=eye_plane[1][:], in_=odd_ones[:])
         move_codes(0)
-        woven1 = placed("woven1", [P, PIECE, PACK], BF16, 8704)
+        woven1 = stage[:, PACK * (PIECE - CAST_VB) :].rearrange("p (j t) -> p j t", t=PACK)
         weave(nc.vector.tensor_copy, woven1, raw[1], 0, CAST_VB)
         weave(nc.scalar.copy, woven1, raw[1], CAST_VB, PIECE)
-        quantise(q_codes[1], made_plane[1], E5M2, woven1[:])
+        nc.vector.memset(pages[0][:, T - 2 * CLEAR_WAIT : T - CLEAR_WAIT], 0.0)
+        quantise(q_codes[1], made_plane[1], E5M2, woven1)
+        nc.vector.memset(pages[0][:, T - CLEAR_WAIT : T], 0.0)
         move_codes(1)
-        woven2 = placed("woven2", [P, PIECE, PACK], BF16, 5632)
+        woven2 = placed("woven2", [P, PIECE, PACK], BF16, 2560)
         weave(nc.scalar.copy, woven2, raw[2], 0, PIECE)
         pages.append(clear(placed("page1", [P, T], F32, 15360)))
 
-        pairs = [placed("pairs0", [P, 2, HALF], BF16, 9216), sb("pairs1", [P, 2, HALF], BF16)]
+        pairs = [placed("pairs0", [P, 2, HALF], BF16, 5632), sb("pairs1", [P, 2, HALF], BF16)]
         for c in range(2):
             decoded = [bank("decoded%d_%d" % (c, u), 2 * c + u) for u in range(2)]
             win = slice(c * HALF, (c + 1) * HALF)
@@ -241,21 +245,22 @@ def tile_list_embg_tgq4_mul_kernel(tc, dy, w_words, w_scales, d, wgo, offs, out)
         direct = [bank("direct%d" % b, 2 + b) for b in range(2)]
         for b in range(2):
             direct_pass(b, wide_codes[:, 0:HALF], wide_plane[:, 0:HALF], E5M2, direct[b][:], True, False)
-        turned = [bank("turned0_%d" % u, u) for u in range(2)]
-        for u in range(2):
-            turned_first(q_codes[0][:, u * P : (u + 1) * P], q_plane[0][:, u * P : (u + 1) * P], turned[u])
-        woven3 = [placed("woven3a", [P, P, PACK], BF16, 7680), placed("woven3b", [P, P, PACK], BF16, 32768)]
+        turned = [bank("turned0_0", 0)]
+        turned_first(q_codes[0][:, 0:P], q_plane[0][:, 0:P], turned[0])
+        woven3 = [placed("woven3a", [P, P, PACK], BF16, 4608), placed("woven3b", [P, P, PACK], BF16, 32768)]
         rest = [sb("rest0", [P, PIECE, PACK], BF16), placed("rest1", [P, PIECE, PACK], BF16, 34816)]
         weave(nc.scalar.copy, woven3[0], raw[3][:, :, 0:P], 0, P)
         weave_pairs(rest[0], pairs[0])
         weave(nc.scalar.copy, woven3[1], raw[3][:, :, P:PIECE], 0, P)
         weave_pairs(rest[1], pairs[1])
-        gate_bank = bank("gate_bank", 4)
-        gate_t = placed("gate_t", [P, P], F32, 10752)
+        gate_bank = bank("gate_bank", 1)
+        gate_t = placed("gate_t", [P, P], F32, 5632)
         nc.tensor.transpose(gate_bank[:, 0:P], gate_rows[:], eye[:])
         nc.scalar.copy(out=gate_t[:], in_=gate_bank[:, 0:P])
+        turned.append(bank("turned0_1", 1))
+        turned_first(q_codes[0][:, P:PIECE], q_plane[0][:, P:PIECE], turned[1])
         quantise(r_codes[0][:], r_plane[0][:], E4M3, rest[0][:])
-        late_codes = placed("late_codes", [P, HALF], U32, 8704)
+        late_codes = placed("late_codes", [P, HALF], U32, 6144)
         late_plane = sb("late_plane", [P, HALF], U8)
         quantise(late_codes[:, 0:PIECE], late_plane[:, 0:PIECE], E5M2, woven2[:])
         for k in range(2):
@@ -274,7 +279,7 @@ def tile_list_embg_tgq4_mul_kernel(tc, dy, w_words, w_scales, d, wgo, offs, out)
             nc.vector.tensor_tensor(out=first[:, b, :], in0=direct[b][:, 0:PIECE], in1=d_first[:, b, :], op=ALU.mult)
         pages.append(clear(placed("page2", [P, T], F32, 27648)))
         pages.append(clear(placed("page3", [P, T], F32, 35840)))
-        decoded = [bank("decoded_late%d" % t, (5, 6, 7, 2)[t]) for t in range(PACK)]
+        decoded = [bank("decoded_late%d" % t, 4 + t) for t in range(PACK)]
         for t in range(PACK):
             decode(late_codes[:], late_plane[:], t, decoded[t])
         for b in range(2):
@@ -319,7 +324,7 @@ def tile_list_embg_tgq4_mul_kernel(tc, dy, w_words, w_scales, d, wgo, offs, out)
                 in1=known[c][:, :, cols].rearrange("p t (c i) -> p c t i", i=4), op=ALU.subtract,
             )
 
-        accs = product(1, q_codes[1], q_plane[1], (4, 3, 1, 0))
+        accs = product(1, q_codes[1], q_plane[1], (2, 3, 1, 0))
         backs = sb("backs", [P, BLOCKS, PIECE], F32)
         for k in range(2):
             nc.scalar.copy(out=backs[:, 2 * k : 2 * k + 2, :], in_=accs[k][:].rearrange("p (b j) -> p b j", b=2))
@@ -348,14 +353,14 @@ def tile_list_embg_tgq4_mul_kernel(tc, dy, w_words, w_scales, d, wgo, offs, out)
             late_leftover(1, k, late[:, k * P : (k + 1) * P, :])
         quantise(r_codes[3][:], r_plane[3][:], E4M3, late[:])
 
-        accs = product(2, late_codes[:, 0:PIECE], late_plane[:, 0:PIECE], (1, 0, 4, 3))
+        accs = product(2, late_codes[:, 0:PIECE], late_plane[:, 0:PIECE], (1, 0, 2, 3))
         third = sb("third", [P, 5, PIECE], F32, tag="weighed1_1")
         for b in range(2):
             nc.scalar.copy(out=third[:, b, :], in_=accs[0][:, b * PIECE : (b + 1) * PIECE])
         nc.scalar.copy(out=third[:, 2:4, :], in_=accs[1][:].rearrange("p (b j) -> p b j", b=2))
         for b in range(3):
             scatter(window(b, 2, 3), third[:, b, :], d_late[:, b, 0:PIECE])
-        accs = product(3, late_codes[:, PIECE:HALF], late_plane[:, PIECE:HALF], (5, 6, 7, 2))
+        accs = product(3, late_codes[:, PIECE:HALF], late_plane[:, PIECE:HALF], (4, 5, 6, 7))
         fourth = sb("fourth", [P, 3, PIECE], F32)
         nc.scalar.copy(out=fourth[:, 0:2, :], in_=accs[0][:].rearrange("p (b j) -> p b j", b=2))
         nc.scalar.copy(out=fourth[:, 2, :], in_=accs[1][:, 0:PIECE])

@@ -68,6 +68,7 @@ def tile_list_embg_tgq4_mul_kernel(tc, dy, w_words, w_scales, d, wgo, offs, out)
         raw = [placed("raw0", [P, PACK, PIECE], F32, 32768)] + [sb("raw%d" % c, [P, PACK, PIECE], F32) for c in (1, 2, 3)]
         for c in range(2):
             nc.sync.dma_start(out=raw[c][:], in_=dy_view[:, :, c * PIECE : (c + 1) * PIECE])
+        nc.sync.dma_start(offsets[:], offs)
         for c in (2, 3):
             nc.sync.dma_start(out=raw[c][:], in_=dy_view[:, :, c * PIECE : (c + 1) * PIECE])
         pages = [sb("page0", [P, T], F32)]
@@ -93,7 +94,6 @@ def tile_list_embg_tgq4_mul_kernel(tc, dy, w_words, w_scales, d, wgo, offs, out)
         d_late = sb("d_late", [P, BLOCKS, HALF], F32)
         nc.sync.dma_start(out=d_first[:], in_=d_view[:, 0:2, 0:PIECE])
         nc.sync.dma_start(out=gate[:], in_=wgo[:, 0:PIECE])
-        nc.sync.dma_start(offsets[:], offs)
         nc.sync.dma_start(out=d_next[:], in_=d_view[:, 2:4, 0:PIECE])
         nc.sync.dma_start(out=d_second[:], in_=d_view[:, :, PIECE:HALF])
         nc.sync.dma_start(out=d_late[:], in_=d_view[:, :, HALF:J])
@@ -106,7 +106,7 @@ def tile_list_embg_tgq4_mul_kernel(tc, dy, w_words, w_scales, d, wgo, offs, out)
             ramp[:], pattern=[[1, HALF]], base=0, channel_multiplier=-PACK, allow_small_or_imprecise_dtypes=True
         )
         eye = sb("eye", [P, P], F32)
-        even_ones = placed("even_ones", [P, 2 * HALF], BF16, 1536)
+        even_ones = placed("even_ones", [P, 2 * HALF], BF16, 2560)
         eye_codes = [sb("eye_codes0", [P, 2 * P], U32)]
         eye_plane = [sb("eye_plane%d" % e, [P, 2 * P], U8) for e in range(2)]
 
@@ -160,17 +160,17 @@ def tile_list_embg_tgq4_mul_kernel(tc, dy, w_words, w_scales, d, wgo, offs, out)
                 in_=pairs[:].bitcast(U32).rearrange("p u j -> p j u"),
             )
 
-        def turned_first(codes, plane, acc):
+        def turned_first(codes, plane, acc, start=True):
             nc.tensor.matmul_mx(
                 out=acc[:], lhsT=codes.bitcast(E5M2), lhsT_scale=plane,
-                rhs=w_codes[:].bitcast(E2M1), rhs_scale=w_plane, start=True, stop=False,
+                rhs=w_codes[:].bitcast(E2M1), rhs_scale=w_plane, start=start, stop=not start,
             )
 
-        def turned_second(c, u, acc, n0, n1, stop):
+        def turned_second(c, u, acc, n0, n1, stop, start=False):
             cols = slice(u * P, (u + 1) * P)
             nc.tensor.matmul_mx(
                 out=acc[:, n0:n1], lhsT=r_codes[c][:, cols].bitcast(E4M3), lhsT_scale=r_plane[c][:, cols],
-                rhs=w_codes[:, 2 * n0 : 2 * n1].bitcast(E2M1), rhs_scale=w_plane[:, n0:n1], start=False, stop=stop,
+                rhs=w_codes[:, 2 * n0 : 2 * n1].bitcast(E2M1), rhs_scale=w_plane[:, n0:n1], start=start, stop=stop,
             )
 
         def direct_pass(b, codes, plane, fmt, dst, start, stop):
@@ -212,12 +212,12 @@ def tile_list_embg_tgq4_mul_kernel(tc, dy, w_words, w_scales, d, wgo, offs, out)
         q_plane = [wide_plane[:, c * HALF : c * HALF + PIECE] for c in range(2)]
         plane1 = placed("plane1", [P, PIECE], U8, 15360)
         made_plane = [q_plane[0], plane1[:]]
-        stage = placed("stage", [P, PACK * (2 * PIECE - CAST_VB)], BF16, 2560)
+        stage = placed("stage", [P, PACK * (2 * PIECE - CAST_VB)], BF16, 3584)
         woven0 = stage[:, 0 : PACK * PIECE].rearrange("p (j t) -> p j t", t=PACK)
         nc.vector.memset(wide_codes[:, HALF + PIECE : 2 * HALF], 0)
         weave(nc.vector.tensor_copy, woven0, raw[0], 0, CAST_V)
         weave(nc.scalar.copy, woven0, raw[0], CAST_V, PIECE)
-        odd_ones = placed("odd_ones", [P, 2 * HALF], BF16, 512)
+        odd_ones = placed("odd_ones", [P, 2 * HALF], BF16, 1536)
         selectors(1, odd_ones)
         quantise(q_codes[0], q_plane[0], E5M2, woven0)
         eye_codes.append(sb("eye_codes1", [P, 2 * P], U32))
@@ -230,11 +230,11 @@ def tile_list_embg_tgq4_mul_kernel(tc, dy, w_words, w_scales, d, wgo, offs, out)
         quantise(q_codes[1], made_plane[1], E5M2, woven1)
         nc.vector.memset(pages[0][:, T - CLEAR_WAIT : T], 0.0)
         move_codes(1)
-        woven2 = placed("woven2", [P, PIECE, PACK], BF16, 2560)
+        woven2 = placed("woven2", [P, PIECE, PACK], BF16, 0)
         weave(nc.scalar.copy, woven2, raw[2], 0, PIECE)
         pages.append(clear(placed("page1", [P, T], F32, 15360)))
 
-        pairs = [placed("pairs0", [P, 2, HALF], BF16, 5632), sb("pairs1", [P, 2, HALF], BF16)]
+        pairs = [placed("pairs0", [P, 2, HALF], BF16, 6656), sb("pairs1", [P, 2, HALF], BF16)]
         for c in range(2):
             decoded = [bank("decoded%d_%d" % (c, u), 2 * c + u) for u in range(2)]
             win = slice(c * HALF, (c + 1) * HALF)
@@ -247,20 +247,20 @@ def tile_list_embg_tgq4_mul_kernel(tc, dy, w_words, w_scales, d, wgo, offs, out)
             direct_pass(b, wide_codes[:, 0:HALF], wide_plane[:, 0:HALF], E5M2, direct[b][:], True, False)
         turned = [bank("turned0_0", 0)]
         turned_first(q_codes[0][:, 0:P], q_plane[0][:, 0:P], turned[0])
-        woven3 = [placed("woven3a", [P, P, PACK], BF16, 4608), placed("woven3b", [P, P, PACK], BF16, 32768)]
+        woven3 = [placed("woven3a", [P, P, PACK], BF16, 5632), placed("woven3b", [P, P, PACK], BF16, 32768)]
         rest = [sb("rest0", [P, PIECE, PACK], BF16), placed("rest1", [P, PIECE, PACK], BF16, 34816)]
         weave(nc.scalar.copy, woven3[0], raw[3][:, :, 0:P], 0, P)
         weave_pairs(rest[0], pairs[0])
         weave(nc.scalar.copy, woven3[1], raw[3][:, :, P:PIECE], 0, P)
         weave_pairs(rest[1], pairs[1])
         gate_bank = bank("gate_bank", 1)
-        gate_t = placed("gate_t", [P, P], F32, 5632)
+        gate_t = placed("gate_t", [P, P], F32, 6656)
         nc.tensor.transpose(gate_bank[:, 0:P], gate_rows[:], eye[:])
         nc.scalar.copy(out=gate_t[:], in_=gate_bank[:, 0:P])
         turned.append(bank("turned0_1", 1))
         turned_first(q_codes[0][:, P:PIECE], q_plane[0][:, P:PIECE], turned[1])
         quantise(r_codes[0][:], r_plane[0][:], E4M3, rest[0][:])
-        late_codes = placed("late_codes", [P, HALF], U32, 6144)
+        late_codes = placed("late_codes", [P, HALF], U32, 7168)
         late_plane = sb("late_plane", [P, HALF], U8)
         quantise(late_codes[:, 0:PIECE], late_plane[:, 0:PIECE], E5M2, woven2[:])
         for k in range(2):
@@ -279,11 +279,18 @@ def tile_list_embg_tgq4_mul_kernel(tc, dy, w_words, w_scales, d, wgo, offs, out)
             nc.vector.tensor_tensor(out=first[:, b, :], in0=direct[b][:, 0:PIECE], in1=d_first[:, b, :], op=ALU.mult)
         pages.append(clear(placed("page2", [P, T], F32, 27648)))
         pages.append(clear(placed("page3", [P, T], F32, 35840)))
-        decoded = [bank("decoded_late%d" % t, 4 + t) for t in range(PACK)]
-        for t in range(PACK):
-            decode(late_codes[:], late_plane[:], t, decoded[t])
         for b in range(2):
             scatter(window(b, 0, 1), first[:, b, :], gate[:])
+
+        late_banks = (4, 5, 2, 3)
+        decoded = [bank("decoded_late%d" % t, late_banks[t]) for t in range(2)]
+        for t in range(2):
+            decode(late_codes[:], late_plane[:], t, decoded[t])
+        turned1 = [bank("turned1_%d" % u, 6 + u) for u in range(2)]
+        for u in range(2):
+            cols = slice(u * P, (u + 1) * P)
+            turned_second(1, u, turned1[u], 0, N, False, True)
+            turned_first(q_codes[1][:, cols], q_plane[1][:, cols], turned1[u], False)
 
         weighed = [sb("weighed0_%d" % u, [P, N], F32) for u in range(2)]
         for u in range(2):
@@ -297,10 +304,19 @@ def tile_list_embg_tgq4_mul_kernel(tc, dy, w_words, w_scales, d, wgo, offs, out)
             )
         for b in range(2):
             place(2 + b, 0, values[:, b, :])
-
+        for t in (2, 3):
+            decoded.append(bank("decoded_late%d" % t, late_banks[t]))
+            decode(late_codes[:], late_plane[:], t, decoded[t])
         known = [sb("known0", [P, PACK, PIECE], F32)]
-        for t in range(PACK):
-            nc.scalar.copy(out=known[0][:, t, :], in_=decoded[t][:, 0:PIECE])
+
+        def turn_back(c, turned, banks):
+            weighed = [sb("weighed%d_%d" % (c, u), [P, N], F32) for u in range(2)]
+            for u in range(2):
+                weigh(2 * c + u, turned[u], weighed[u], 0)
+            accs = [bank("back_bank%d_%d" % (c, k), banks[k]) for k in range(2)]
+            for k in range(2):
+                turn_pair(weighed, 2 * k, accs[k])
+            return accs
 
         def product(c, codes, plane, banks):
             turned = [bank("turned%d_%d" % (c, u), banks[u]) for u in range(2)]
@@ -308,23 +324,18 @@ def tile_list_embg_tgq4_mul_kernel(tc, dy, w_words, w_scales, d, wgo, offs, out)
                 turned_first(codes[:, u * P : (u + 1) * P], plane[:, u * P : (u + 1) * P], turned[u])
             for u in range(2):
                 turned_second(c, u, turned[u], 0, N, True)
-            weighed = [sb("weighed%d_%d" % (c, u), [P, N], F32) for u in range(2)]
-            for u in range(2):
-                weigh(2 * c + u, turned[u], weighed[u], 0)
-            accs = [bank("back_bank%d_%d" % (c, k), banks[2 + k]) for k in range(2)]
-            for k in range(2):
-                turn_pair(weighed, 2 * k, accs[k])
-            return accs
+            return turn_back(c, turned, banks[2:])
 
-        def late_leftover(c, k, dst):
-            cols = slice(k * P, (k + 1) * P)
+        def late_leftover(c, cols, dst):
             nc.gpsimd.tensor_tensor(
-                out=dst.rearrange("p (c i) t -> p c t i", i=4),
+                out=dst[:, cols, :].rearrange("p (c i) t -> p c t i", i=4),
                 in0=raw[2 + c][:, :, cols].rearrange("p t (c i) -> p c t i", i=4),
                 in1=known[c][:, :, cols].rearrange("p t (c i) -> p c t i", i=4), op=ALU.subtract,
             )
 
-        accs = product(1, q_codes[1], q_plane[1], (2, 3, 1, 0))
+        accs = turn_back(1, turned1, (1, 6))
+        for t in range(PACK):
+            nc.scalar.copy(out=known[0][:, t, :], in_=decoded[t][:, 0:PIECE])
         backs = sb("backs", [P, BLOCKS, PIECE], F32)
         for k in range(2):
             nc.scalar.copy(out=backs[:, 2 * k : 2 * k + 2, :], in_=accs[k][:].rearrange("p (b j) -> p b j", b=2))
@@ -337,10 +348,10 @@ def tile_list_embg_tgq4_mul_kernel(tc, dy, w_words, w_scales, d, wgo, offs, out)
 
         values = sb("values1_0", [P, 2, PIECE], F32)
         late = placed("late0", [P, PIECE, PACK], BF16, 47104)
+        late_leftover(0, slice(0, P), late)
         times_d(values[:, 0, :], 0)
         place(0, 1, values[:, 0, :])
-        for k in range(2):
-            late_leftover(0, k, late[:, k * P : (k + 1) * P, :])
+        late_leftover(0, slice(P, PIECE), late)
         quantise(r_codes[2][:], r_plane[2][:], E4M3, late[:])
         times_d(values[:, 1, :], 1)
         place(1, 1, values[:, 1, :])
@@ -349,18 +360,17 @@ def tile_list_embg_tgq4_mul_kernel(tc, dy, w_words, w_scales, d, wgo, offs, out)
             times_d(values[:, b, :], 2 + b)
             place(2 + b, 1, values[:, b, :])
         late = placed("late1", [P, PIECE, PACK], BF16, 48128)
-        for k in range(2):
-            late_leftover(1, k, late[:, k * P : (k + 1) * P, :])
+        late_leftover(1, slice(0, PIECE), late)
         quantise(r_codes[3][:], r_plane[3][:], E4M3, late[:])
 
-        accs = product(2, late_codes[:, 0:PIECE], late_plane[:, 0:PIECE], (1, 0, 2, 3))
+        accs = product(2, late_codes[:, 0:PIECE], late_plane[:, 0:PIECE], (1, 6, 0, 7))
         third = sb("third", [P, 5, PIECE], F32, tag="weighed1_1")
         for b in range(2):
             nc.scalar.copy(out=third[:, b, :], in_=accs[0][:, b * PIECE : (b + 1) * PIECE])
         nc.scalar.copy(out=third[:, 2:4, :], in_=accs[1][:].rearrange("p (b j) -> p b j", b=2))
         for b in range(3):
             scatter(window(b, 2, 3), third[:, b, :], d_late[:, b, 0:PIECE])
-        accs = product(3, late_codes[:, PIECE:HALF], late_plane[:, PIECE:HALF], (4, 5, 6, 7))
+        accs = product(3, late_codes[:, PIECE:HALF], late_plane[:, PIECE:HALF], (4, 5, 2, 3))
         fourth = sb("fourth", [P, 3, PIECE], F32)
         nc.scalar.copy(out=fourth[:, 0:2, :], in_=accs[0][:].rearrange("p (b j) -> p b j", b=2))
         nc.scalar.copy(out=fourth[:, 2, :], in_=accs[1][:, 0:PIECE])

@@ -23,12 +23,8 @@ HALF = 512
 PIECE = 256
 GROUPS = 8
 BLOCKS = N // P
-TILES = HALF // P
-CAST_V = 160
-CAST_S = PIECE - CAST_V
-CAST_VB = 96
 CLEAR_ODD = 769
-CLEAR_WAIT = 400
+CLEAR_CUT = 1152
 GATE_FIRST, GATE_STEP = 70, 7
 
 
@@ -65,12 +61,13 @@ def tile_list_embg_tgq4_mul_kernel(tc, dy, w_words, w_scales, d, wgo, offs, out)
         offsets = keep.tile([P, J // 16], U16, name="offsets")
         dy_view = dy.rearrange("(p t) j -> p t j", t=PACK)
         d_view = d.rearrange("(b p) j -> p b j", p=P)
-        raw = [placed("raw0", [P, PACK, PIECE], F32, 32768)] + [sb("raw%d" % c, [P, PACK, PIECE], F32) for c in (1, 2, 3)]
-        for c in range(2):
-            nc.sync.dma_start(out=raw[c][:], in_=dy_view[:, :, c * PIECE : (c + 1) * PIECE])
-        nc.sync.dma_start(offsets[:], offs)
-        for c in (2, 3):
-            nc.sync.dma_start(out=raw[c][:], in_=dy_view[:, :, c * PIECE : (c + 1) * PIECE])
+        raw_a = sb("raw_a", [P, PACK, P], F32)
+        raw_b = sb("raw_b", [P, PACK, P], F32)
+        raw_c = placed("raw_c", [P, PACK, PIECE], F32, 36864)
+        raw_d = [sb("raw_d%d" % c, [P, PACK, PIECE], F32) for c in range(2)]
+        nc.sync.dma_start(out=raw_a[:], in_=dy_view[:, :, 0:P])
+        nc.sync.dma_start(out=raw_b[:], in_=dy_view[:, :, P:PIECE])
+        nc.sync.dma_start(out=raw_c[:], in_=dy_view[:, :, PIECE:HALF])
         pages = [sb("page0", [P, T], F32)]
         w_codes = sb("w_codes", [P, 2 * N], U8)
         w_plane_tile = sb("w_plane", [P, N + 4], U8)
@@ -78,305 +75,305 @@ def tile_list_embg_tgq4_mul_kernel(tc, dy, w_words, w_scales, d, wgo, offs, out)
         w_plane = w_plane_tile[:, 0:N]
         nc.vector.memset(pages[0][:, 0:CLEAR_ODD], 0.0)
         nc.sync.dma_start(out=w_codes[:].bitcast(I32), in_=w_words[0].bitcast(I32))
+        nc.sync.dma_start(offsets[:], offs)
         for q in range(4):
             nc.sync.dma_start(
                 out=w_plane[32 * q : 32 * q + 4, :].bitcast(I32), in_=w_scales[0, 4 * q : 4 * q + 4, :].bitcast(I32)
             )
+        d_first = [sb("d_first%d" % u, [P, 2, P], F32) for u in range(2)]
+        gate = [sb("gate%d" % u, [P, P], F32) for u in range(2)]
+        d_next = sb("d_next", [P, 2, PIECE], F32)
+        d_second = sb("d_second", [P, BLOCKS, PIECE], F32)
+        d_late = sb("d_late", [P, BLOCKS, HALF], F32)
         gate_rows = sb("gate_rows", [P, P], F32)
+        nc.sync.dma_start(out=raw_d[0][:], in_=dy_view[:, :, HALF : HALF + PIECE])
+        nc.sync.dma_start(out=d_first[0][:], in_=d_view[:, 0:2, 0:P])
+        nc.sync.dma_start(out=gate[0][:], in_=wgo[:, 0:P])
         nc.sync.dma_start(
             out=gate_rows[:],
             in_=wgo.rearrange("r (u j) -> (r u) j", j=P)[GATE_FIRST : GATE_FIRST + GATE_STEP * (P - 1) + 1 : GATE_STEP, :],
         )
-        d_first = sb("d_first", [P, 2, PIECE], F32)
-        gate = sb("gate", [P, PIECE], F32)
-        d_next = sb("d_next", [P, 2, PIECE], F32)
-        d_second = sb("d_second", [P, BLOCKS, PIECE], F32)
-        d_late = sb("d_late", [P, BLOCKS, HALF], F32)
-        nc.sync.dma_start(out=d_first[:], in_=d_view[:, 0:2, 0:PIECE])
-        nc.sync.dma_start(out=gate[:], in_=wgo[:, 0:PIECE])
+        nc.sync.dma_start(out=d_first[1][:], in_=d_view[:, 0:2, P:PIECE])
+        nc.sync.dma_start(out=gate[1][:], in_=wgo[:, P:PIECE])
+        nc.sync.dma_start(out=raw_d[1][:], in_=dy_view[:, :, HALF + PIECE : J])
         nc.sync.dma_start(out=d_next[:], in_=d_view[:, 2:4, 0:PIECE])
         nc.sync.dma_start(out=d_second[:], in_=d_view[:, :, PIECE:HALF])
         nc.sync.dma_start(out=d_late[:], in_=d_view[:, :, HALF:J])
-
-        wide_codes = sb("wide_codes", [P, 2 * HALF], U32)
-        wide_plane = sb("wide_plane", [P, 2 * HALF], U8)
 
         ramp = sb("ramp", [P, HALF], BF16)
         nc.gpsimd.iota(
             ramp[:], pattern=[[1, HALF]], base=0, channel_multiplier=-PACK, allow_small_or_imprecise_dtypes=True
         )
         eye = sb("eye", [P, P], F32)
-        even_ones = placed("even_ones", [P, 2 * HALF], BF16, 2560)
-        eye_codes = [sb("eye_codes0", [P, 2 * P], U32)]
-        eye_plane = [sb("eye_plane%d" % e, [P, 2 * P], U8) for e in range(2)]
+        ones = [placed("ones0", [P, 2 * HALF], BF16, 50176), sb("ones1", [P, 2 * HALF], BF16)]
+        eye_codes = sb("eye_codes", [P, PACK * P], U32)
+        eye_plane = sb("eye_plane", [P, PACK * P], U8)
+        for t in range(PACK):
+            nc.vector.tensor_scalar(
+                out=ones[t // 2][:, t % 2 * HALF : (t % 2 + 1) * HALF], in0=ramp[:], scalar1=float(t), scalar2=None, op0=ALU.is_equal
+            )
+        nc.vector.memset(pages[0][:, CLEAR_ODD - 1 : T], 0.0)
+        for h in range(2):
+            part = slice(h * PIECE, (h + 1) * PIECE)
+            nc.vector.quantize_mx(out=eye_codes[:, part].bitcast(E4M3), scales=eye_plane[:, part], in_=ones[h][:])
 
-        def selectors(e, ones):
-            for u in range(2):
-                nc.vector.tensor_scalar(
-                    out=ones[:, u * HALF : (u + 1) * HALF], in0=ramp[:], scalar1=float(2 * u + e), scalar2=None,
-                    op0=ALU.is_equal,
-                )
+        early_codes = placed("early_codes", [P, PIECE], U32, 50176)
+        q_plane = sb("q_plane", [P, J], U8)
+        r_codes = sb("r_codes", [P, J], U32)
+        r_plane = sb("r_plane", [P, J], U8)
 
-        nc.vector.memset(pages[0][:, CLEAR_ODD - 1 : T - 2 * CLEAR_WAIT], 0.0)
-        selectors(0, even_ones)
-        nc.scalar.copy(out=eye[:], in_=even_ones[:, 0:HALF:PACK])
-        nc.vector.memset(wide_codes[:, PIECE:HALF], 0)
-        nc.vector.quantize_mx(out=eye_codes[0][:].bitcast(E4M3), scales=eye_plane[0][:], in_=even_ones[:])
-
-        r_codes = [sb("r_codes%d" % c, [P, PIECE], U32) for c in range(4)]
-        r_plane = [sb("r_plane%d" % c, [P, PIECE], U8) for c in range(4)]
+        def cols(u0, u1):
+            return slice(u0 * P, u1 * P)
 
         def quantise(codes, plane, fmt, src):
             nc.vector.quantize_mx(out=codes.bitcast(fmt), scales=plane, in_=src.rearrange("p j t -> p (j t)"))
 
-        def move_codes(c):
-            src, dst = c * HALF, c * HALF + PIECE
-            plane_words = wide_plane[:].bitcast(I32)
-            for at in ((dst,), (src, dst))[c]:
-                nc.vector.tensor_copy(out=plane_words[:, at // 4 : (at + PIECE) // 4], in_=made_plane[c].bitcast(I32))
-            code_bytes = wide_codes[:].bitcast(U8)
-            nc.vector.tensor_copy(
-                out=code_bytes[:, PACK * dst : PACK * (dst + PIECE) : 2],
-                in_=code_bytes[:, PACK * src + 1 : PACK * (src + PIECE) : 2],
+        def decode(u, codes, acc):
+            for t in range(PACK):
+                nc.tensor.matmul_mx(
+                    out=acc[:, cols(t, t + 1)], lhsT=eye_codes[:, cols(t, t + 1)].bitcast(E4M3),
+                    lhsT_scale=eye_plane[:, cols(t, t + 1)], rhs=codes.bitcast(E5M2), rhs_scale=q_plane[:, cols(u, u + 1)],
+                    start=True, stop=True,
+                )
+
+        def leftover(engine, dst, src, known, i):
+            engine.tensor_tensor(
+                out=dst.rearrange("p (c i) t -> p c t i", i=i), in0=src.rearrange("p t (c i) -> p c t i", i=i),
+                in1=known.rearrange("p t (c i) -> p c t i", i=i), op=ALU.subtract,
             )
 
-        def decode(codes, plane, t, acc):
-            cols = slice(t // 2 * P, (t // 2 + 1) * P)
+        def turned_pass(codes, plane, fmt, acc, n0, start, stop):
             nc.tensor.matmul_mx(
-                out=acc[:], lhsT=eye_codes[t % 2][:, cols].bitcast(E4M3), lhsT_scale=eye_plane[t % 2][:, cols],
-                rhs=codes.bitcast(E5M2), rhs_scale=plane, start=True, stop=True,
-            )
-
-        def leftover_pair(c, u, acc, pairs):
-            nc.vector.tensor_tensor(
-                out=pairs[:, u, :].rearrange("p (j e) -> p j e", e=2),
-                in0=raw[c][:, 2 * u : 2 * u + 2, :].rearrange("p e j -> p j e"),
-                in1=acc[:].rearrange("p (e j) -> p j e", e=2), op=ALU.subtract,
-            )
-
-        def weave_pairs(dst, pairs):
-            nc.scalar.copy(
-                out=dst[:].rearrange("p j t -> p (j t)").bitcast(U32).rearrange("p (j u) -> p j u", u=2),
-                in_=pairs[:].bitcast(U32).rearrange("p u j -> p j u"),
-            )
-
-        def turned_first(codes, plane, acc, start=True):
-            nc.tensor.matmul_mx(
-                out=acc[:], lhsT=codes.bitcast(E5M2), lhsT_scale=plane,
-                rhs=w_codes[:].bitcast(E2M1), rhs_scale=w_plane, start=start, stop=not start,
-            )
-
-        def turned_second(c, u, acc, n0, n1, stop, start=False):
-            cols = slice(u * P, (u + 1) * P)
-            nc.tensor.matmul_mx(
-                out=acc[:, n0:n1], lhsT=r_codes[c][:, cols].bitcast(E4M3), lhsT_scale=r_plane[c][:, cols],
-                rhs=w_codes[:, 2 * n0 : 2 * n1].bitcast(E2M1), rhs_scale=w_plane[:, n0:n1], start=start, stop=stop,
+                out=acc[:, n0:N], lhsT=codes.bitcast(fmt), lhsT_scale=plane,
+                rhs=w_codes[:, 2 * n0 : 2 * N].bitcast(E2M1), rhs_scale=w_plane[:, n0:N], start=start, stop=stop,
             )
 
         def direct_pass(b, codes, plane, fmt, dst, start, stop):
             nc.tensor.matmul_mx(
                 out=dst, lhsT=w_codes[:, 2 * b * P : 2 * (b + 1) * P].bitcast(E2M1),
-                lhsT_scale=w_plane[:, b * P : (b + 1) * P], rhs=codes.bitcast(fmt), rhs_scale=plane,
-                start=start, stop=stop,
+                lhsT_scale=w_plane[:, cols(b, b + 1)], rhs=codes.bitcast(fmt), rhs_scale=plane, start=start, stop=stop,
             )
 
-        def weigh(tile, acc, dst, b0):
-            src4 = acc[:].rearrange("p (b g s) -> p b g s", b=BLOCKS, s=16)
-            dst4 = dst[:].rearrange("p (b g s) -> p b g s", b=BLOCKS, s=16)
+        def weigh(u, acc, dst, b0):
+            src4 = acc[:, b0 * P : (b0 + 2) * P].rearrange("p (b g s) -> p b g s", b=2, s=16)
+            dst4 = dst[:].rearrange("p (b g s) -> p b g s", b=2, s=16)
             for g in range(GROUPS):
-                col = gate_column(tile, g)
+                col = gate_column(u, g)
                 nc.scalar.activation(
-                    out=dst4[:, b0:, g, :], in_=src4[:, b0:, g, :], func=COPY, scale=gate_t[:, col : col + 1]
+                    out=dst4[:, :, g, :], in_=src4[:, :, g, :], func=COPY, scale=gate_t[:, col : col + 1]
                 )
+            return dst
 
-        def turn_pair(weighed, b0, acc):
-            for b in range(2):
-                for u in range(2):
+        def turn_pair(weighed, acc):
+            for u in range(2):
+                for b in range(2):
                     at = b * PIECE + u * P
-                    nc.tensor.transpose(acc[:, at : at + P], weighed[u][:, (b0 + b) * P : (b0 + b + 1) * P], eye[:])
+                    nc.tensor.transpose(acc[:, at : at + P], weighed[u][:, cols(b, b + 1)], eye[:])
+
+        def turn_back(u0, turned, b0, acc, offsets=(None, None)):
+            tiles = [
+                sb("weighed%d_%d" % (u0 + k, b0), [P, PIECE], F32) if offsets[k] is None
+                else placed("weighed%d_%d" % (u0 + k, b0), [P, PIECE], F32, offsets[k])
+                for k in range(2)
+            ]
+            turn_pair([weigh(u0 + k, turned[k], tiles[k], b0) for k in range(2)], acc)
 
         def clear(page):
             nc.gpsimd.memset(page[:], 0.0)
             return page
 
-        def window(b, c0, c1):
-            return pages[b][:].indirect(offsets[:, 16 * c0 : 16 * c1])
+        def window(b, u0, u1):
+            return pages[b][:].indirect(offsets[:, 8 * u0 : 8 * u1])
 
         def scatter(dst, x, y):
             nc.vector.tensor_tensor(out=dst, in0=x, in1=y, op=ALU.mult)
 
-        def place(b, c, x):
-            nc.vector.tensor_copy(out=window(b, c, c + 1), in_=x)
+        def place(dst, x):
+            nc.vector.tensor_copy(out=dst, in_=x)
 
-        q_codes = [wide_codes[:, c * HALF : c * HALF + PIECE] for c in range(2)]
-        q_plane = [wide_plane[:, c * HALF : c * HALF + PIECE] for c in range(2)]
-        plane1 = placed("plane1", [P, PIECE], U8, 15360)
-        made_plane = [q_plane[0], plane1[:]]
-        stage = placed("stage", [P, PACK * (2 * PIECE - CAST_VB)], BF16, 3584)
-        woven0 = stage[:, 0 : PACK * PIECE].rearrange("p (j t) -> p j t", t=PACK)
-        nc.vector.memset(wide_codes[:, HALF + PIECE : 2 * HALF], 0)
-        weave(nc.vector.tensor_copy, woven0, raw[0], 0, CAST_V)
-        weave(nc.scalar.copy, woven0, raw[0], CAST_V, PIECE)
-        odd_ones = placed("odd_ones", [P, 2 * HALF], BF16, 1536)
-        selectors(1, odd_ones)
-        quantise(q_codes[0], q_plane[0], E5M2, woven0)
-        eye_codes.append(sb("eye_codes1", [P, 2 * P], U32))
-        nc.vector.quantize_mx(out=eye_codes[1][:].bitcast(E4M3), scales=eye_plane[1][:], in_=odd_ones[:])
-        move_codes(0)
-        woven1 = stage[:, PACK * (PIECE - CAST_VB) :].rearrange("p (j t) -> p j t", t=PACK)
-        weave(nc.vector.tensor_copy, woven1, raw[1], 0, CAST_VB)
-        weave(nc.scalar.copy, woven1, raw[1], CAST_VB, PIECE)
-        nc.vector.memset(pages[0][:, T - 2 * CLEAR_WAIT : T - CLEAR_WAIT], 0.0)
-        quantise(q_codes[1], made_plane[1], E5M2, woven1)
-        nc.vector.memset(pages[0][:, T - CLEAR_WAIT : T], 0.0)
-        move_codes(1)
-        woven2 = placed("woven2", [P, PIECE, PACK], BF16, 0)
-        weave(nc.scalar.copy, woven2, raw[2], 0, PIECE)
-        pages.append(clear(placed("page1", [P, T], F32, 15360)))
+        def first_tier(u0, u1, codes, woven):
+            quantise(codes, q_plane[:, cols(u0, u1)], E5M2, woven)
 
-        pairs = [placed("pairs0", [P, 2, HALF], BF16, 6656), sb("pairs1", [P, 2, HALF], BF16)]
-        for c in range(2):
-            decoded = [bank("decoded%d_%d" % (c, u), 2 * c + u) for u in range(2)]
-            win = slice(c * HALF, (c + 1) * HALF)
-            for u in range(2):
-                decode(wide_codes[:, win], wide_plane[:, win], 2 * u, decoded[u])
-            for u in range(2):
-                leftover_pair(c, u, decoded[u], pairs[c])
-        direct = [bank("direct%d" % b, 2 + b) for b in range(2)]
+        def second_tier(u0, u1, rest):
+            quantise(r_codes[:, cols(u0, u1)], r_plane[:, cols(u0, u1)], E4M3, rest)
+
+        def planes(acc):
+            return acc[:].rearrange("p (t j) -> p t j", t=PACK)
+
+        woven_a = sb("woven_a", [P, P, PACK], BF16)
+        woven_b = placed("woven_b", [P, P, PACK], BF16, 8192)
+        woven_c = placed("woven_c", [P, PIECE, PACK], BF16, 9216)
+        weave(nc.scalar.copy, woven_a, raw_a, 0, P)
+        q_codes = [early_codes[:, cols(u, u + 1)] for u in range(2)]
+        first_tier(0, 1, q_codes[0], woven_a[:])
+        pages.append(placed("page1", [P, T], F32, 51200))
+        nc.vector.memset(pages[1][:, 0:CLEAR_CUT], 0.0)
+        weave(nc.scalar.copy, woven_b, raw_b, 0, P)
+        first_tier(1, 2, q_codes[1], woven_b[:])
+        nc.vector.memset(pages[1][:, CLEAR_CUT:T], 0.0)
+        weave(nc.scalar.copy, woven_c, raw_c, 0, PIECE)
+        nc.scalar.copy(out=eye[:], in_=ones[1][:, 2:HALF:PACK])
+        decoded = [bank("decoded%d" % u, u) for u in range(2)]
+        rest = [
+            placed("rest_a", [P, 4 * HALF], BF16, 24576)[:, 0:HALF].rearrange("p (j t) -> p j t", t=PACK),
+            placed("rest_b", [P, P, PACK], BF16, 12288)[:],
+        ]
+        for u in range(2):
+            decode(u, q_codes[u], decoded[u])
+
+        def q_of(u):
+            return q_codes[u], q_plane[:, cols(u, u + 1)], E5M2
+
+        def r_of(u):
+            return r_codes[:, cols(u, u + 1)], r_plane[:, cols(u, u + 1)], E4M3
+
+        leftover(nc.vector, rest[0], raw_a[:], planes(decoded[0]), 2)
+        second_tier(0, 1, rest[0])
+        direct_a = [bank("direct_a0", 0), bank("direct_a1", 5)]
+        direct_pass(0, *q_of(0), direct_a[0][:, 0:P], True, False)
+        direct_pass(0, *r_of(0), direct_a[0][:, 0:P], False, True)
+        direct_pass(1, *r_of(0), direct_a[1][:, 0:P], True, False)
+        direct_pass(1, *q_of(0), direct_a[1][:, 0:P], False, True)
+        first_a = [sb("first_a%d" % b, [P, P], F32) for b in range(2)]
         for b in range(2):
-            direct_pass(b, wide_codes[:, 0:HALF], wide_plane[:, 0:HALF], E5M2, direct[b][:], True, False)
-        turned = [bank("turned0_0", 0)]
-        turned_first(q_codes[0][:, 0:P], q_plane[0][:, 0:P], turned[0])
-        woven3 = [placed("woven3a", [P, P, PACK], BF16, 5632), placed("woven3b", [P, P, PACK], BF16, 32768)]
-        rest = [sb("rest0", [P, PIECE, PACK], BF16), placed("rest1", [P, PIECE, PACK], BF16, 34816)]
-        weave(nc.scalar.copy, woven3[0], raw[3][:, :, 0:P], 0, P)
-        weave_pairs(rest[0], pairs[0])
-        weave(nc.scalar.copy, woven3[1], raw[3][:, :, P:PIECE], 0, P)
-        weave_pairs(rest[1], pairs[1])
+            nc.vector.tensor_tensor(out=first_a[b][:], in0=direct_a[b][:, 0:P], in1=d_first[0][:, b, :], op=ALU.mult)
+        for h in range(2):
+            part = slice(h * P // 2, (h + 1) * P // 2)
+            leftover(nc.vector, rest[1][:, part, :], raw_b[:, :, part], planes(decoded[1])[:, :, part], 2)
+        second_tier(1, 2, rest[1][:])
+        codes_c = placed("codes_c", [P, PIECE], U32, 25600)
+        first_tier(2, 4, codes_c[:], woven_c[:])
+        q_codes.extend(codes_c[:, cols(k, k + 1)] for k in range(2))
+        decoded_c = [bank("decoded_c%d" % k, 5 * k) for k in range(2)]
+        for k in range(2):
+            decode(2 + k, q_codes[2 + k], decoded_c[k])
+        woven_d = [placed("woven_d%d" % c, [P, PIECE, PACK], BF16, (26624, 0)[c]) for c in range(2)]
+
+        def cast_late(c):
+            for k in range(2):
+                weave(nc.scalar.copy, woven_d[c][:, cols(k, k + 1), :], raw_d[c][:, :, cols(k, k + 1)], 0, P)
+
+        cast_late(0)
         gate_bank = bank("gate_bank", 1)
-        gate_t = placed("gate_t", [P, P], F32, 6656)
+        gate_t = sb("gate_t", [P, P], F32)
         nc.tensor.transpose(gate_bank[:, 0:P], gate_rows[:], eye[:])
         nc.scalar.copy(out=gate_t[:], in_=gate_bank[:, 0:P])
-        turned.append(bank("turned0_1", 1))
-        turned_first(q_codes[0][:, P:PIECE], q_plane[0][:, P:PIECE], turned[1])
-        quantise(r_codes[0][:], r_plane[0][:], E4M3, rest[0][:])
-        late_codes = placed("late_codes", [P, HALF], U32, 7168)
-        late_plane = sb("late_plane", [P, HALF], U8)
-        quantise(late_codes[:, 0:PIECE], late_plane[:, 0:PIECE], E5M2, woven2[:])
+        direct_b = bank("direct_b", 1)
+        for b in range(2):
+            direct_pass(b, *q_of(1), direct_b[:, cols(b, b + 1)], b == 0, False)
+            direct_pass(b, *r_of(1), direct_b[:, cols(b, b + 1)], False, b == 1)
+        turned = [bank("turned%d" % u, 2 + u) for u in range(2)]
+        for u in range(2):
+            turned_pass(*r_of(u), turned[u], PIECE, True, False)
+            turned_pass(*q_of(u), turned[u], PIECE, False, True)
+        pages.append(clear(placed("page2", [P, T], F32, 8192)))
+        for b in range(2):
+            scatter(window(b, 0, 1), first_a[b][:], gate[0][:])
+        back_ab = bank("back_ab", 4)
+        turn_back(0, turned, 2, back_ab, (0, None))
+        cast_late(1)
+
+        rest_c = placed("rest_c", [P, PIECE, PACK], BF16, 28672)
         for k in range(2):
-            cols = slice(PIECE + k * P, PIECE + (k + 1) * P)
-            quantise(late_codes[:, cols], late_plane[:, cols], E5M2, woven3[k][:])
-        for b in range(2):
-            for u in range(2):
-                cols = slice(u * P, (u + 1) * P)
-                direct_pass(b, r_codes[0][:, cols], r_plane[0][:, cols], E4M3, direct[b][:, cols], False, u == 1)
-        for u in range(2):
-            for b in (2, 3):
-                turned_second(0, u, turned[u], b * P, (b + 1) * P, b == 3)
-        quantise(r_codes[1][:], r_plane[1][:], E4M3, rest[1][:])
-        first = sb("first", [P, 2, PIECE], F32, tag="pairs1")
-        for b in range(2):
-            nc.vector.tensor_tensor(out=first[:, b, :], in0=direct[b][:, 0:PIECE], in1=d_first[:, b, :], op=ALU.mult)
-        pages.append(clear(placed("page2", [P, T], F32, 27648)))
-        pages.append(clear(placed("page3", [P, T], F32, 35840)))
-        for b in range(2):
-            scatter(window(b, 0, 1), first[:, b, :], gate[:])
+            leftover(nc.vector, rest_c[:, cols(k, k + 1), :], raw_c[:, :, cols(k, k + 1)], planes(decoded_c[k]), 2)
+        first_b = sb("first_b", [P, 2, P], F32)
+        nc.vector.tensor_tensor(
+            out=first_b[:], in0=direct_b[:, 0:PIECE].rearrange("p (b j) -> p b j", b=2), in1=d_first[1][:],
+            op=ALU.mult,
+        )
+        codes_d0 = placed("codes_d0", [P, PIECE], U32, 36864 + 1024)
+        first_tier(4, 6, codes_d0[:], woven_d[0][:])
+        q_codes.extend(codes_d0[:, cols(k, k + 1)] for k in range(2))
+        second_tier(2, 4, rest_c[:])
+        known = []
 
-        late_banks = (4, 5, 2, 3)
-        decoded = [bank("decoded_late%d" % t, late_banks[t]) for t in range(2)]
-        for t in range(2):
-            decode(late_codes[:], late_plane[:], t, decoded[t])
-        turned1 = [bank("turned1_%d" % u, 6 + u) for u in range(2)]
-        for u in range(2):
-            cols = slice(u * P, (u + 1) * P)
-            turned_second(1, u, turned1[u], 0, N, False, True)
-            turned_first(q_codes[1][:, cols], q_plane[1][:, cols], turned1[u], False)
+        def learn(u, index, offset):
+            acc = bank("decoded_d%d" % u, index)
+            decode(u, q_codes[u], acc)
+            known.append(placed("known%d" % u, [P, HALF], F32, offset))
+            nc.scalar.copy(out=known[u - 4][:], in_=acc[:])
 
-        weighed = [sb("weighed0_%d" % u, [P, N], F32) for u in range(2)]
-        for u in range(2):
-            weigh(u, turned[u], weighed[u], 2)
-        back_bank = bank("back_bank0", 0)
-        turn_pair(weighed, 2, back_bank)
-        values = sb("values0", [P, 2, PIECE], F32)
+        learn(4, 6, 40960)
+        turned_c = [bank("turned_c%d" % k, 5 * k) for k in range(2)]
+        for k in range(2):
+            turned_pass(*q_of(2 + k), turned_c[k], 0, True, False)
+        for k in range(2):
+            turned_pass(*r_of(2 + k), turned_c[k], 0, False, True)
+        scatter(window(0, 1, 2), first_b[:, 0, :], gate[1][:])
+        values_ab = placed("values_ab", [P, 2, PIECE], F32, 36864 + 2048)
+        scatter(window(1, 1, 2), first_b[:, 1, :], gate[1][:])
         for b in range(2):
             nc.vector.tensor_tensor(
-                out=values[:, b, :], in0=back_bank[:, b * PIECE : (b + 1) * PIECE], in1=d_next[:, b, :], op=ALU.mult
+                out=values_ab[:, b, :], in0=back_ab[:, b * PIECE : (b + 1) * PIECE], in1=d_next[:, b, :], op=ALU.mult
             )
+        pages.append(clear(placed("page3", [P, T], F32, 26624)))
         for b in range(2):
-            place(2 + b, 0, values[:, b, :])
-        for t in (2, 3):
-            decoded.append(bank("decoded_late%d" % t, late_banks[t]))
-            decode(late_codes[:], late_plane[:], t, decoded[t])
-        known = [sb("known0", [P, PACK, PIECE], F32)]
-
-        def turn_back(c, turned, banks):
-            weighed = [sb("weighed%d_%d" % (c, u), [P, N], F32) for u in range(2)]
-            for u in range(2):
-                weigh(2 * c + u, turned[u], weighed[u], 0)
-            accs = [bank("back_bank%d_%d" % (c, k), banks[k]) for k in range(2)]
-            for k in range(2):
-                turn_pair(weighed, 2 * k, accs[k])
-            return accs
-
-        def product(c, codes, plane, banks):
-            turned = [bank("turned%d_%d" % (c, u), banks[u]) for u in range(2)]
-            for u in range(2):
-                turned_first(codes[:, u * P : (u + 1) * P], plane[:, u * P : (u + 1) * P], turned[u])
-            for u in range(2):
-                turned_second(c, u, turned[u], 0, N, True)
-            return turn_back(c, turned, banks[2:])
-
-        def late_leftover(c, cols, dst):
-            nc.gpsimd.tensor_tensor(
-                out=dst[:, cols, :].rearrange("p (c i) t -> p c t i", i=4),
-                in0=raw[2 + c][:, :, cols].rearrange("p t (c i) -> p c t i", i=4),
-                in1=known[c][:, :, cols].rearrange("p t (c i) -> p c t i", i=4), op=ALU.subtract,
-            )
-
-        accs = turn_back(1, turned1, (1, 6))
-        for t in range(PACK):
-            nc.scalar.copy(out=known[0][:, t, :], in_=decoded[t][:, 0:PIECE])
+            place(window(2 + b, 0, 2), values_ab[:, b, :])
+        back_c = [bank("back_c%d" % k, 2 + k) for k in range(2)]
+        turn_back(2, turned_c, 0, back_c[0], (None, 43008))
         backs = sb("backs", [P, BLOCKS, PIECE], F32)
-        for k in range(2):
-            nc.scalar.copy(out=backs[:, 2 * k : 2 * k + 2, :], in_=accs[k][:].rearrange("p (b j) -> p b j", b=2))
-        known.append(sb("known1", [P, PACK, PIECE], F32, tag="weighed1_1"))
-        for t in range(PACK):
-            nc.scalar.copy(out=known[1][:, t, :], in_=decoded[t][:, PIECE:HALF])
+        nc.scalar.copy(out=backs[:, 0, :], in_=back_c[0][:, 0:PIECE])
+        learn(5, 7, 43008)
+        nc.scalar.copy(out=backs[:, 1, :], in_=back_c[0][:, PIECE:HALF])
+        turn_back(2, turned_c, 2, back_c[1])
+        nc.scalar.copy(out=backs[:, 2:4, :], in_=back_c[1][:].rearrange("p (b j) -> p b j", b=2))
 
         def times_d(dst, b):
             nc.gpsimd.tensor_tensor(out=dst, in0=backs[:, b, :], in1=d_second[:, b, :], op=ALU.mult)
+            place(window(b, 2, 4), dst)
 
-        values = sb("values1_0", [P, 2, PIECE], F32)
-        late = placed("late0", [P, PIECE, PACK], BF16, 47104)
-        late_leftover(0, slice(0, P), late)
-        times_d(values[:, 0, :], 0)
-        place(0, 1, values[:, 0, :])
-        late_leftover(0, slice(P, PIECE), late)
-        quantise(r_codes[2][:], r_plane[2][:], E4M3, late[:])
-        times_d(values[:, 1, :], 1)
-        place(1, 1, values[:, 1, :])
-        values = placed("values1_1", [P, 2, PIECE], F32, 46080)
-        for b in range(2):
-            times_d(values[:, b, :], 2 + b)
-            place(2 + b, 1, values[:, b, :])
-        late = placed("late1", [P, PIECE, PACK], BF16, 48128)
-        late_leftover(1, slice(0, PIECE), late)
-        quantise(r_codes[3][:], r_plane[3][:], E4M3, late[:])
+        def late_leftover(k, late):
+            leftover(nc.gpsimd, late[:, cols(k % 2, k % 2 + 1), :], raw_d[k // 2][:, :, cols(k % 2, k % 2 + 1)], planes(known[k]), 4)
 
-        accs = product(2, late_codes[:, 0:PIECE], late_plane[:, 0:PIECE], (1, 6, 0, 7))
-        third = sb("third", [P, 5, PIECE], F32, tag="weighed1_1")
-        for b in range(2):
-            nc.scalar.copy(out=third[:, b, :], in_=accs[0][:, b * PIECE : (b + 1) * PIECE])
-        nc.scalar.copy(out=third[:, 2:4, :], in_=accs[1][:].rearrange("p (b j) -> p b j", b=2))
+        def open_product(c, banks):
+            turned = [bank("turned_d%d_%d" % (c, k), banks[k]) for k in range(2)]
+            for k in range(2):
+                turned_pass(*q_of(4 + 2 * c + k), turned[k], 0, True, False)
+            return turned
+
+        def close_product(c, turned):
+            for k in range(2):
+                turned_pass(*r_of(4 + 2 * c + k), turned[k], 0, False, True)
+
+        def product(c, turned, banks):
+            accs = [bank("back_d%d_%d" % (c, k), banks[k]) for k in range(2)]
+            for k in range(2):
+                turn_back(4 + 2 * c, turned, 2 * k, accs[k])
+                if c == 1 or k == 1:
+                    for b in range(2 * k * c, 2 * k + 2):
+                        nc.scalar.copy(
+                            out=values_d[:, b, cols(2 * c, 2 * c + 2)], in_=accs[b // 2][:, b % 2 * PIECE : (b % 2 + 1) * PIECE]
+                        )
+
+        turned_d = [open_product(0, (1, 4))]
+        late = placed("late0", [P, PIECE, PACK], BF16, 45056)
+        late_leftover(0, late)
+        times_d(placed("values_c0", [P, PIECE], F32, 40960)[:], 0)
+        late_leftover(1, late)
+        codes_d1 = placed("codes_d1", [P, PIECE], U32, 43008 + 1024)
+        first_tier(6, 8, codes_d1[:], woven_d[1][:])
+        second_tier(4, 6, late[:])
+        q_codes.extend(codes_d1[:, cols(k, k + 1)] for k in range(2))
+        times_d(placed("values_c1", [P, PIECE], F32, 43008)[:], 1)
+        for u in (6, 7):
+            learn(u, u, 47104 + 2048 * (u % 2))
+        close_product(0, turned_d[0])
+        turned_d.append(open_product(1, (0, 5)))
+        for b in (2, 3):
+            times_d(placed("values_c%d" % b, [P, PIECE], F32, 45056 + 1024 * (b - 2))[:], b)
+        late = sb("late1", [P, PIECE, PACK], BF16)
+        for k in range(2, 4):
+            late_leftover(k, late)
+        second_tier(6, 8, late[:])
+        close_product(1, turned_d[1])
+
+        values_d = sb("values_d", [P, BLOCKS, HALF], F32)
+        product(0, turned_d[0], (2, 3))
         for b in range(3):
-            scatter(window(b, 2, 3), third[:, b, :], d_late[:, b, 0:PIECE])
-        accs = product(3, late_codes[:, PIECE:HALF], late_plane[:, PIECE:HALF], (4, 5, 2, 3))
-        fourth = sb("fourth", [P, 3, PIECE], F32)
-        nc.scalar.copy(out=fourth[:, 0:2, :], in_=accs[0][:].rearrange("p (b j) -> p b j", b=2))
-        nc.scalar.copy(out=fourth[:, 2, :], in_=accs[1][:, 0:PIECE])
-        nc.scalar.copy(out=third[:, 4, :], in_=accs[1][:, PIECE:HALF])
+            scatter(window(b, 4, 6), values_d[:, b, 0:PIECE], d_late[:, b, 0:PIECE])
+        product(1, turned_d[1], (1, 4))
         for b in range(3):
-            scatter(window(b, 3, 4), fourth[:, b, :], d_late[:, b, PIECE:HALF])
+            scatter(window(b, 6, 8), values_d[:, b, PIECE:HALF], d_late[:, b, PIECE:HALF])
             nc.sync.dma_start(out=out[b * P : (b + 1) * P, :], in_=pages[b][:])
-        scatter(window(3, 2, 4), third[:, 3:5, :].rearrange("p c j -> p (c j)"), d_late[:, 3, :])
+        scatter(window(3, 4, 8), values_d[:, 3, :], d_late[:, 3, :])
         nc.sync.dma_start(out=out[3 * P : 4 * P, :], in_=pages[3][:])

@@ -67,32 +67,32 @@ def tile_list_embg_tgq4_mul_kernel(tc, dy, w_words, w_scales, d, wgo, offs, out)
         raw_d = [sb("raw_d%d" % c, [P, PACK, PIECE], F32) for c in range(2)]
         nc.sync.dma_start(out=raw_a[:], in_=dy_view[:, :, 0:P])
         nc.sync.dma_start(out=raw_b[:], in_=dy_view[:, :, P:PIECE])
-        nc.sync.dma_start(out=raw_c[:], in_=dy_view[:, :, PIECE:HALF])
         pages = [sb("page0", [P, T], F32)]
         w_codes = sb("w_codes", [P, 2 * N], U8)
         w_plane_tile = sb("w_plane", [P, N + 4], U8)
         nc.vector.memset(w_plane_tile[:].bitcast(I32), 0)
         w_plane = w_plane_tile[:, 0:N]
         nc.vector.memset(pages[0][:, 0:CLEAR_ODD], 0.0)
-        nc.sync.dma_start(out=w_codes[:].bitcast(I32), in_=w_words[0].bitcast(I32))
-        nc.sync.dma_start(offsets[:], offs)
         for q in range(4):
             nc.sync.dma_start(
                 out=w_plane[32 * q : 32 * q + 4, :].bitcast(I32), in_=w_scales[0, 4 * q : 4 * q + 4, :].bitcast(I32)
             )
+        nc.sync.dma_start(out=raw_c[:], in_=dy_view[:, :, PIECE:HALF])
+        nc.sync.dma_start(out=w_codes[:].bitcast(I32), in_=w_words[0].bitcast(I32))
         d_first = [sb("d_first%d" % u, [P, 2, P], F32) for u in range(2)]
         gate = [sb("gate%d" % u, [P, P], F32) for u in range(2)]
         d_next = sb("d_next", [P, 2, PIECE], F32)
         d_second = sb("d_second", [P, BLOCKS, PIECE], F32)
         d_late = sb("d_late", [P, BLOCKS, HALF], F32)
         gate_rows = sb("gate_rows", [P, P], F32)
-        nc.sync.dma_start(out=raw_d[0][:], in_=dy_view[:, :, HALF : HALF + PIECE])
         nc.sync.dma_start(out=d_first[0][:], in_=d_view[:, 0:2, 0:P])
         nc.sync.dma_start(out=gate[0][:], in_=wgo[:, 0:P])
         nc.sync.dma_start(
             out=gate_rows[:],
             in_=wgo.rearrange("r (u j) -> (r u) j", j=P)[GATE_FIRST : GATE_FIRST + GATE_STEP * (P - 1) + 1 : GATE_STEP, :],
         )
+        nc.sync.dma_start(offsets[:], offs)
+        nc.sync.dma_start(out=raw_d[0][:], in_=dy_view[:, :, HALF : HALF + PIECE])
         nc.sync.dma_start(out=d_first[1][:], in_=d_view[:, 0:2, P:PIECE])
         nc.sync.dma_start(out=gate[1][:], in_=wgo[:, P:PIECE])
         nc.sync.dma_start(out=raw_d[1][:], in_=dy_view[:, :, HALF + PIECE : J])

@@ -291,7 +291,9 @@ def tile_list_embg_tgq4_mul_kernel(tc, dy, w_words, w_scales, d, wgo, offs, out)
             acc = bank("decoded_d%d" % u, index)
             decode(u, q_codes[u], acc)
             known.append(placed("known%d" % u, [P, HALF], F32, offset))
-            nc.scalar.copy(out=known[u - 4][:], in_=acc[:])
+            nc.scalar.copy(
+                out=known[u - 4][:].rearrange("p (j t) -> p j t", t=PACK), in_=planes(acc).rearrange("p t j -> p j t")
+            )
 
         learn(4, 6, 40960)
         turned_c = [bank("turned_c%d" % k, 5 * k) for k in range(2)]
@@ -323,7 +325,11 @@ def tile_list_embg_tgq4_mul_kernel(tc, dy, w_words, w_scales, d, wgo, offs, out)
             place(window(b, 2, 4), dst)
 
         def late_leftover(k, late):
-            leftover(nc.gpsimd, late[:, cols(k % 2, k % 2 + 1), :], raw_d[k // 2][:, :, cols(k % 2, k % 2 + 1)], planes(known[k]), 4)
+            part = cols(k % 2, k % 2 + 1)
+            nc.gpsimd.tensor_tensor(
+                out=late[:, part, :], in0=raw_d[k // 2][:, :, part].rearrange("p t j -> p j t"),
+                in1=known[k][:].rearrange("p (j t) -> p j t", t=PACK), op=ALU.subtract,
+            )
 
         def open_product(c, banks):
             turned = [bank("turned_d%d_%d" % (c, k), banks[k]) for k in range(2)]

@@ -170,10 +170,10 @@ def tile_list_embg_tgq4_mul_kernel(tc, dy, w_words, w_scales, d, wgo, offs, out)
                     at = b * PIECE + u * P
                     nc.tensor.transpose(acc[:, at : at + P], weighed[u][:, cols(b, b + 1)], eye[:])
 
-        def turn_back(u0, turned, b0, acc, offsets=(None, None)):
+        def turn_back(u0, turned, b0, acc, offsets=(None, None), room=PIECE):
             tiles = [
                 sb("weighed%d_%d" % (u0 + k, b0), [P, PIECE], F32) if offsets[k] is None
-                else placed("weighed%d_%d" % (u0 + k, b0), [P, PIECE], F32, offsets[k])
+                else placed("weighed%d_%d" % (u0 + k, b0), [P, room], F32, offsets[k])[:, 0:PIECE]
                 for k in range(2)
             ]
             turn_pair([weigh(u0 + k, turned[k], tiles[k], b0) for k in range(2)], acc)
@@ -247,7 +247,7 @@ def tile_list_embg_tgq4_mul_kernel(tc, dy, w_words, w_scales, d, wgo, offs, out)
         decoded_c = [bank("decoded_c%d" % k, 5 * k) for k in range(2)]
         for k in range(2):
             decode(2 + k, q_codes[2 + k], decoded_c[k])
-        woven_d = [placed("woven_d%d" % c, [P, PIECE, PACK], BF16, (26624, 0)[c]) for c in range(2)]
+        woven_d = [placed("woven_d%d" % c, [P, PIECE, PACK], BF16, (26624, 36864 - 1024)[c]) for c in range(2)]
 
         def cast_late(c):
             for k in range(2):
@@ -270,12 +270,12 @@ def tile_list_embg_tgq4_mul_kernel(tc, dy, w_words, w_scales, d, wgo, offs, out)
         for b in range(2):
             scatter(window(b, 0, 1), first_a[b][:], gate[0][:])
         back_ab = bank("back_ab", 4)
-        turn_back(0, turned, 2, back_ab, (0, None))
-        cast_late(1)
+        turn_back(0, turned, 2, back_ab)
 
         rest_c = placed("rest_c", [P, PIECE, PACK], BF16, 28672)
         for k in range(2):
             leftover(nc.vector, rest_c[:, cols(k, k + 1), :], raw_c[:, :, cols(k, k + 1)], planes(decoded_c[k]), 2)
+        cast_late(1)
         first_b = sb("first_b", [P, 2, P], F32)
         nc.vector.tensor_tensor(
             out=first_b[:], in0=direct_b[:, 0:PIECE].rearrange("p (b j) -> p b j", b=2), in1=d_first[1][:],
@@ -312,12 +312,12 @@ def tile_list_embg_tgq4_mul_kernel(tc, dy, w_words, w_scales, d, wgo, offs, out)
         for b in range(2):
             place(window(2 + b, 0, 2), values_ab[:, b, :])
         back_c = [bank("back_c%d" % k, 2 + k) for k in range(2)]
-        turn_back(2, turned_c, 0, back_c[0], (None, 43008))
+        turn_back(2, turned_c, 0, back_c[0], (None, 63488), 4 * PIECE)
         backs = sb("backs", [P, BLOCKS, PIECE], F32)
         nc.scalar.copy(out=backs[:, 0, :], in_=back_c[0][:, 0:PIECE])
-        learn(5, 7, 43008)
+        learn(5, 7, 63488)
         nc.scalar.copy(out=backs[:, 1, :], in_=back_c[0][:, PIECE:HALF])
-        turn_back(2, turned_c, 2, back_c[1])
+        turn_back(2, turned_c, 2, back_c[1], (65536, 66560))
         nc.scalar.copy(out=backs[:, 2:4, :], in_=back_c[1][:].rearrange("p (b j) -> p b j", b=2))
 
         def times_d(dst, b):
@@ -344,25 +344,25 @@ def tile_list_embg_tgq4_mul_kernel(tc, dy, w_words, w_scales, d, wgo, offs, out)
         def product(c, turned, banks):
             accs = [bank("back_d%d_%d" % (c, k), banks[k]) for k in range(2)]
             for k in range(2):
-                turn_back(4 + 2 * c, turned, 2 * k, accs[k])
+                turn_back(4 + 2 * c, turned, 2 * k, accs[k], (((None, None),) * 2, ((None, 69632), (69632 - 512, 69632 + 512)))[c][k])
                 if c == 1 or k == 1:
                     for b in range(2 * k * c, 2 * k + 2):
                         nc.scalar.copy(
                             out=values_d[:, b, cols(2 * c, 2 * c + 2)], in_=accs[b // 2][:, b % 2 * PIECE : (b % 2 + 1) * PIECE]
                         )
 
-        turned_d = [open_product(0, (1, 4))]
+        turned_d = [open_product(0, (1, 6))]
         late = placed("late0", [P, PIECE, PACK], BF16, 45056)
         late_leftover(0, late)
         times_d(placed("values_c0", [P, PIECE], F32, 40960)[:], 0)
         late_leftover(1, late)
-        codes_d1 = placed("codes_d1", [P, PIECE], U32, 43008 + 1024)
+        codes_d1 = placed("codes_d1", [P, PIECE], U32, 63488 + 1024)
         first_tier(6, 8, codes_d1[:], woven_d[1][:])
         second_tier(4, 6, late[:])
         q_codes.extend(codes_d1[:, cols(k, k + 1)] for k in range(2))
-        times_d(placed("values_c1", [P, PIECE], F32, 43008)[:], 1)
+        times_d(placed("values_c1", [P, PIECE], F32, 63488)[:], 1)
         for u in (6, 7):
-            learn(u, u, 47104 + 2048 * (u % 2))
+            learn(u, 4 + 3 * (u % 2), 47104 + 2048 * (u % 2))
         close_product(0, turned_d[0])
         turned_d.append(open_product(1, (0, 5)))
         for b in (2, 3):

@@ -142,11 +142,14 @@ def tile_list_embg_tgq4_mul_kernel(tc, dy, w_words, w_scales, d, wgo, offs, out)
                 in1=known.rearrange("p t (c i) -> p c t i", i=i), op=ALU.subtract,
             )
 
-        def turned_pass(codes, plane, fmt, acc, n0, start, stop):
-            nc.tensor.matmul_mx(
-                out=acc[:, n0:N], lhsT=codes.bitcast(fmt), lhsT_scale=plane,
-                rhs=w_codes[:, 2 * n0 : 2 * N].bitcast(E2M1), rhs_scale=w_plane[:, n0:N], start=start, stop=stop,
-            )
+        def turned_passes(tier, u0, b0, acc, start):
+            for k in range(2):
+                codes, plane, fmt = tier(u0 + k)
+                nc.tensor.matmul_mx(
+                    out=acc[:, k * PIECE : (k + 1) * PIECE], lhsT=codes.bitcast(fmt), lhsT_scale=plane,
+                    rhs=w_codes[:, 2 * b0 * P : 2 * (b0 + 2) * P].bitcast(E2M1), rhs_scale=w_plane[:, cols(b0, b0 + 2)],
+                    start=start and k == 0, stop=not start and k == 1,
+                )
 
         def direct_pass(b, codes, plane, fmt, dst, start, stop):
             nc.tensor.matmul_mx(
@@ -154,8 +157,8 @@ def tile_list_embg_tgq4_mul_kernel(tc, dy, w_words, w_scales, d, wgo, offs, out)
                 lhsT_scale=w_plane[:, cols(b, b + 1)], rhs=codes.bitcast(fmt), rhs_scale=plane, start=start, stop=stop,
             )
 
-        def weigh(u, acc, dst, b0):
-            src4 = acc[:, b0 * P : (b0 + 2) * P].rearrange("p (b g s) -> p b g s", b=2, s=16)
+        def weigh(u, acc, dst):
+            src4 = acc[:, u % 2 * PIECE : (u % 2 + 1) * PIECE].rearrange("p (b g s) -> p b g s", b=2, s=16)
             dst4 = dst[:].rearrange("p (b g s) -> p b g s", b=2, s=16)
             for g in range(GROUPS):
                 col = gate_column(u, g)
@@ -170,13 +173,13 @@ def tile_list_embg_tgq4_mul_kernel(tc, dy, w_words, w_scales, d, wgo, offs, out)
                     at = b * PIECE + u * P
                     nc.tensor.transpose(acc[:, at : at + P], weighed[u][:, cols(b, b + 1)], eye[:])
 
-        def turn_back(u0, turned, b0, acc, offsets=(None, None), room=PIECE):
+        def turn_back(u0, turned, b0, acc, offsets=(None, None)):
             tiles = [
                 sb("weighed%d_%d" % (u0 + k, b0), [P, PIECE], F32) if offsets[k] is None
-                else placed("weighed%d_%d" % (u0 + k, b0), [P, room], F32, offsets[k])[:, 0:PIECE]
+                else placed("weighed%d_%d" % (u0 + k, b0), [P, PIECE], F32, offsets[k])
                 for k in range(2)
             ]
-            turn_pair([weigh(u0 + k, turned[k], tiles[k], b0) for k in range(2)], acc)
+            turn_pair([weigh(u0 + k, turned, tiles[k]) for k in range(2)], acc)
 
         def clear(page):
             nc.gpsimd.memset(page[:], 0.0)
@@ -262,10 +265,9 @@ def tile_list_embg_tgq4_mul_kernel(tc, dy, w_words, w_scales, d, wgo, offs, out)
         for b in range(2):
             direct_pass(b, *q_of(1), direct_b[:, cols(b, b + 1)], b == 0, False)
             direct_pass(b, *r_of(1), direct_b[:, cols(b, b + 1)], False, b == 1)
-        turned = [bank("turned%d" % u, 2 + u) for u in range(2)]
-        for u in range(2):
-            turned_pass(*r_of(u), turned[u], PIECE, True, False)
-            turned_pass(*q_of(u), turned[u], PIECE, False, True)
+        turned = bank("turned_ab", 2)
+        turned_passes(r_of, 0, 2, turned, True)
+        turned_passes(q_of, 0, 2, turned, False)
         pages.append(clear(placed("page2", [P, T], F32, 8192)))
         for b in range(2):
             scatter(window(b, 0, 1), first_a[b][:], gate[0][:])
@@ -295,12 +297,10 @@ def tile_list_embg_tgq4_mul_kernel(tc, dy, w_words, w_scales, d, wgo, offs, out)
                 out=known[u - 4][:].rearrange("p (j t) -> p j t", t=PACK), in_=planes(acc).rearrange("p t j -> p j t")
             )
 
-        learn(4, 6, 40960)
-        turned_c = [bank("turned_c%d" % k, 5 * k) for k in range(2)]
-        for k in range(2):
-            turned_pass(*q_of(2 + k), turned_c[k], 0, True, False)
-        for k in range(2):
-            turned_pass(*r_of(2 + k), turned_c[k], 0, False, True)
+        turned = bank("turned_c0", 0)
+        turned_passes(q_of, 2, 0, turned, True)
+        learn(4, 5, 40960)
+        turned_passes(r_of, 2, 0, turned, False)
         scatter(window(0, 1, 2), first_b[:, 0, :], gate[1][:])
         values_ab = placed("values_ab", [P, 2, PIECE], F32, 36864 + 2048)
         scatter(window(1, 1, 2), first_b[:, 1, :], gate[1][:])
@@ -312,12 +312,15 @@ def tile_list_embg_tgq4_mul_kernel(tc, dy, w_words, w_scales, d, wgo, offs, out)
         for b in range(2):
             place(window(2 + b, 0, 2), values_ab[:, b, :])
         back_c = [bank("back_c%d" % k, 2 + k) for k in range(2)]
-        turn_back(2, turned_c, 0, back_c[0], (None, 63488), 4 * PIECE)
+        turn_back(2, turned, 0, back_c[0], (None, 63488))
         backs = sb("backs", [P, BLOCKS, PIECE], F32)
         nc.scalar.copy(out=backs[:, 0, :], in_=back_c[0][:, 0:PIECE])
-        learn(5, 7, 63488)
+        learn(5, 5, 63488)
         nc.scalar.copy(out=backs[:, 1, :], in_=back_c[0][:, PIECE:HALF])
-        turn_back(2, turned_c, 2, back_c[1], (65536, 66560))
+        turned = bank("turned_c1", 0)
+        turned_passes(q_of, 2, 2, turned, True)
+        turned_passes(r_of, 2, 2, turned, False)
+        turn_back(2, turned, 2, back_c[1])
         nc.scalar.copy(out=backs[:, 2:4, :], in_=back_c[1][:].rearrange("p (b j) -> p b j", b=2))
 
         def times_d(dst, b):
@@ -331,27 +334,8 @@ def tile_list_embg_tgq4_mul_kernel(tc, dy, w_words, w_scales, d, wgo, offs, out)
                 in1=known[k][:].rearrange("p (j t) -> p j t", t=PACK), op=ALU.subtract,
             )
 
-        def open_product(c, banks):
-            turned = [bank("turned_d%d_%d" % (c, k), banks[k]) for k in range(2)]
-            for k in range(2):
-                turned_pass(*q_of(4 + 2 * c + k), turned[k], 0, True, False)
-            return turned
-
-        def close_product(c, turned):
-            for k in range(2):
-                turned_pass(*r_of(4 + 2 * c + k), turned[k], 0, False, True)
-
-        def product(c, turned, banks):
-            accs = [bank("back_d%d_%d" % (c, k), banks[k]) for k in range(2)]
-            for k in range(2):
-                turn_back(4 + 2 * c, turned, 2 * k, accs[k], (((None, None),) * 2, ((None, 69632), (69632 - 512, 69632 + 512)))[c][k])
-                if c == 1 or k == 1:
-                    for b in range(2 * k * c, 2 * k + 2):
-                        nc.scalar.copy(
-                            out=values_d[:, b, cols(2 * c, 2 * c + 2)], in_=accs[b // 2][:, b % 2 * PIECE : (b % 2 + 1) * PIECE]
-                        )
-
-        turned_d = [open_product(0, (1, 6))]
+        low = [bank("turned_d0", 5)]
+        turned_passes(q_of, 4, 0, low[0], True)
         late = placed("late0", [P, PIECE, PACK], BF16, 45056)
         late_leftover(0, late)
         times_d(placed("values_c0", [P, PIECE], F32, 40960)[:], 0)
@@ -362,22 +346,42 @@ def tile_list_embg_tgq4_mul_kernel(tc, dy, w_words, w_scales, d, wgo, offs, out)
         q_codes.extend(codes_d1[:, cols(k, k + 1)] for k in range(2))
         times_d(placed("values_c1", [P, PIECE], F32, 63488)[:], 1)
         for u in (6, 7):
-            learn(u, 4 + 3 * (u % 2), 47104 + 2048 * (u % 2))
-        close_product(0, turned_d[0])
-        turned_d.append(open_product(1, (0, 5)))
+            learn(u, u, 47104 + 2048 * (u % 2))
+        turned_passes(r_of, 4, 0, low[0], False)
         for b in (2, 3):
             times_d(placed("values_c%d" % b, [P, PIECE], F32, 45056 + 1024 * (b - 2))[:], b)
         late = sb("late1", [P, PIECE, PACK], BF16)
         for k in range(2, 4):
             late_leftover(k, late)
         second_tier(6, 8, late[:])
-        close_product(1, turned_d[1])
 
         values_d = sb("values_d", [P, BLOCKS, HALF], F32)
-        product(0, turned_d[0], (2, 3))
+
+        def turn(c, b0, turned, index):
+            acc = bank("back_d%d_%d" % (c, b0), index)
+            turn_back(4 + 2 * c, turned, b0, acc)
+            return acc
+
+        def bring(c, b0, acc):
+            for b in range(2):
+                nc.scalar.copy(out=values_d[:, b0 + b, cols(2 * c, 2 * c + 2)], in_=acc[:, b * PIECE : (b + 1) * PIECE])
+
+        def upper(c, index):
+            turned = bank("turned_high%d" % c, index)
+            turned_passes(r_of, 4 + 2 * c, 2, turned, True)
+            turned_passes(q_of, 4 + 2 * c, 2, turned, False)
+            return turned
+
+        accs = [turn(0, 0, low[0], 1), turn(0, 2, upper(0, 6), 4)]
+        for k in range(2):
+            bring(0, 2 * k, accs[k])
+        low.append(bank("turned_d1", 7))
+        turned_passes(q_of, 6, 0, low[1], True)
+        turned_passes(r_of, 6, 0, low[1], False)
         for b in range(3):
             scatter(window(b, 4, 6), values_d[:, b, 0:PIECE], d_late[:, b, 0:PIECE])
-        product(1, turned_d[1], (1, 4))
+        bring(1, 0, turn(1, 0, low[1], 2))
+        bring(1, 2, turn(1, 2, upper(1, 7), 3))
         for b in range(3):
             scatter(window(b, 6, 8), values_d[:, b, PIECE:HALF], d_late[:, b, PIECE:HALF])
             nc.sync.dma_start(out=out[b * P : (b + 1) * P, :], in_=pages[b][:])

@@ -142,14 +142,17 @@ def tile_list_embg_tgq4_mul_kernel(tc, dy, w_words, w_scales, d, wgo, offs, out)
                 in1=known.rearrange("p t (c i) -> p c t i", i=i), op=ALU.subtract,
             )
 
+        def turned_pass(tier, u, b0, acc, start, stop):
+            codes, plane, fmt = tier(u)
+            nc.tensor.matmul_mx(
+                out=acc[:, u % 2 * PIECE : (u % 2 + 1) * PIECE], lhsT=codes.bitcast(fmt), lhsT_scale=plane,
+                rhs=w_codes[:, 2 * b0 * P : 2 * (b0 + 2) * P].bitcast(E2M1), rhs_scale=w_plane[:, cols(b0, b0 + 2)],
+                start=start, stop=stop,
+            )
+
         def turned_passes(tier, u0, b0, acc, start):
             for k in range(2):
-                codes, plane, fmt = tier(u0 + k)
-                nc.tensor.matmul_mx(
-                    out=acc[:, k * PIECE : (k + 1) * PIECE], lhsT=codes.bitcast(fmt), lhsT_scale=plane,
-                    rhs=w_codes[:, 2 * b0 * P : 2 * (b0 + 2) * P].bitcast(E2M1), rhs_scale=w_plane[:, cols(b0, b0 + 2)],
-                    start=start and k == 0, stop=not start and k == 1,
-                )
+                turned_pass(tier, u0 + k, b0, acc, start and k == 0, not start and k == 1)
 
         def direct_pass(b, codes, plane, fmt, dst, start, stop):
             nc.tensor.matmul_mx(
@@ -157,9 +160,10 @@ def tile_list_embg_tgq4_mul_kernel(tc, dy, w_words, w_scales, d, wgo, offs, out)
                 lhsT_scale=w_plane[:, cols(b, b + 1)], rhs=codes.bitcast(fmt), rhs_scale=plane, start=start, stop=stop,
             )
 
-        def weigh(u, acc, dst):
-            src4 = acc[:, u % 2 * PIECE : (u % 2 + 1) * PIECE].rearrange("p (b g s) -> p b g s", b=2, s=16)
-            dst4 = dst[:].rearrange("p (b g s) -> p b g s", b=2, s=16)
+        def weigh(u, acc, dst, b0=0, count=2):
+            at = u % 2 * PIECE + b0 * P
+            src4 = acc[:, at : at + count * P].rearrange("p (b g s) -> p b g s", b=count, s=16)
+            dst4 = dst[:].rearrange("p (b g s) -> p b g s", b=count, s=16)
             for g in range(GROUPS):
                 col = gate_column(u, g)
                 nc.scalar.activation(
@@ -266,8 +270,10 @@ def tile_list_embg_tgq4_mul_kernel(tc, dy, w_words, w_scales, d, wgo, offs, out)
             direct_pass(b, *q_of(1), direct_b[:, cols(b, b + 1)], b == 0, False)
             direct_pass(b, *r_of(1), direct_b[:, cols(b, b + 1)], False, b == 1)
         turned = bank("turned_ab", 2)
-        turned_passes(r_of, 0, 2, turned, True)
-        turned_passes(q_of, 0, 2, turned, False)
+        turned_pass(r_of, 0, 2, turned, True, False)
+        turned_pass(q_of, 0, 2, turned, False, False)
+        turned_pass(q_of, 1, 2, turned, False, False)
+        turned_pass(r_of, 1, 2, turned, False, True)
         pages.append(clear(placed("page2", [P, T], F32, 8192)))
         for b in range(2):
             scatter(window(b, 0, 1), first_a[b][:], gate[0][:])
@@ -355,16 +361,17 @@ def tile_list_embg_tgq4_mul_kernel(tc, dy, w_words, w_scales, d, wgo, offs, out)
             late_leftover(k, late)
         second_tier(6, 8, late[:])
 
-        values_d = sb("values_d", [P, BLOCKS, HALF], F32)
+        values_lo = sb("values_lo", [P, 2, HALF], F32)
+        values_hi = placed("values_hi", [P, 2, HALF], F32, 69632 - 4096 + 256)
 
-        def turn(c, b0, turned, index):
+        def turn(c, b0, turned, index, offsets=(None, None)):
             acc = bank("back_d%d_%d" % (c, b0), index)
-            turn_back(4 + 2 * c, turned, b0, acc)
+            turn_back(4 + 2 * c, turned, b0, acc, offsets)
             return acc
 
         def bring(c, b0, acc):
             for b in range(2):
-                nc.scalar.copy(out=values_d[:, b0 + b, cols(2 * c, 2 * c + 2)], in_=acc[:, b * PIECE : (b + 1) * PIECE])
+                nc.scalar.copy(out=(values_lo, values_hi)[b0 // 2][:, b, cols(2 * c, 2 * c + 2)], in_=acc[:, b * PIECE : (b + 1) * PIECE])
 
         def upper(c, index):
             turned = bank("turned_high%d" % c, index)
@@ -373,17 +380,26 @@ def tile_list_embg_tgq4_mul_kernel(tc, dy, w_words, w_scales, d, wgo, offs, out)
             return turned
 
         accs = [turn(0, 0, low[0], 1), turn(0, 2, upper(0, 6), 4)]
-        for k in range(2):
-            bring(0, 2 * k, accs[k])
+        bring(0, 0, accs[0])
         low.append(bank("turned_d1", 7))
         turned_passes(q_of, 6, 0, low[1], True)
         turned_passes(r_of, 6, 0, low[1], False)
-        for b in range(3):
-            scatter(window(b, 4, 6), values_d[:, b, 0:PIECE], d_late[:, b, 0:PIECE])
-        bring(1, 0, turn(1, 0, low[1], 2))
-        bring(1, 2, turn(1, 2, upper(1, 7), 3))
-        for b in range(3):
-            scatter(window(b, 6, 8), values_d[:, b, PIECE:HALF], d_late[:, b, PIECE:HALF])
+        for b in range(2):
+            scatter(window(b, 4, 6), values_lo[:, b, 0:PIECE], d_late[:, b, 0:PIECE])
+        ends = [bank("back_last%d" % b, (2, 5)[b]) for b in range(2)]
+        for b in range(2):
+            acc = ends[b]
+            for k in range(2):
+                single = placed("single%d_%d" % (b, k), [P, P], F32, 69632 + 1024 * b + 512 * k)
+                nc.tensor.transpose(acc[:, cols(k, k + 1)], weigh(6 + k, low[1], single, b, 1)[:], eye[:])
+        for b in range(2):
+            nc.scalar.copy(out=values_lo[:, b, PIECE:HALF], in_=ends[b][:, 0:PIECE])
+        last = turn(1, 2, upper(1, 0), 3, (71424 - 1024, 71424))
+        bring(0, 2, accs[1])
+        bring(1, 2, last)
+        for b in range(2):
+            scatter(window(b, 6, 8), values_lo[:, b, PIECE:HALF], d_late[:, b, PIECE:HALF])
             nc.sync.dma_start(out=out[b * P : (b + 1) * P, :], in_=pages[b][:])
-        scatter(window(3, 4, 8), values_d[:, 3, :], d_late[:, 3, :])
-        nc.sync.dma_start(out=out[3 * P : 4 * P, :], in_=pages[3][:])
+        for b in (2, 3):
+            scatter(window(b, 4, 8), values_hi[:, b - 2, :], d_late[:, b, :])
+            nc.sync.dma_start(out=out[b * P : (b + 1) * P, :], in_=pages[b][:])

from contextlib import ExitStack

import concourse.mybir as mybir

K, N, T, J = 512, 512, 2048, 1024
FLOPS = 3 * 2 * K * N * J

F32 = mybir.dt.float32
BF16 = mybir.dt.bfloat16
I32 = mybir.dt.int32
U32 = mybir.dt.uint32
U16 = mybir.dt.uint16
U8 = mybir.dt.uint8
E4M3 = mybir.dt.float8_e4m3fn_x4
E5M2 = mybir.dt.float8_e5m2_x4
E2M1 = mybir.dt.float4_e2m1fn_x4
ALU = mybir.AluOpType
COPY = mybir.ActivationFunctionType.Copy

P = 128
PACK = 4
HALF = 512
PIECE = 256
GROUPS = 8
BLOCKS = N // P
CLEAR_ODD = 769
CLEAR_CUT = 1152
GATE_FIRST, GATE_STEP = 70, 7


def gate_column(tile, g):
    return min(
        p for p in range(P)
        if (GATE_FIRST + GATE_STEP * p) // P == g and (GATE_FIRST + GATE_STEP * p) % (J // P) == tile
    )


def weave(copy, dst, src, j0, j1):
    copy(
        out=dst[:, j0:j1, :].rearrange("p (c i) t -> p c t i", i=4),
        in_=src[:, :, j0:j1].rearrange("p t (c i) -> p c t i", i=4),
    )


def tile_list_embg_tgq4_mul_kernel(tc, dy, w_words, w_scales, d, wgo, offs, out):
    nc = tc.nc
    with ExitStack() as ctx:
        keep = ctx.enter_context(tc.tile_pool(name="keep", bufs=1))
        lap = ctx.enter_context(tc.tile_pool(name="lap", bufs=1))
        psum = ctx.enter_context(tc.psum_pool(name="psum", bufs=1))

        def sb(name, shape, dtype, tag=None):
            return keep.tile(shape, dtype, name=name, tag=tag or name, align_bytes=64)

        def placed(name, shape, dtype, offset):
            return lap.tile(shape, dtype, name=name, offset=offset, align_bytes=64)

        def bank(name, index):
            return psum.tile([P, HALF], F32, name=name, tag="bank%d" % index)

        offsets = keep.tile([P, J // 16], U16, name="offsets")
        dy_view = dy.rearrange("(p t) j -> p t j", t=PACK)
        d_view = d.rearrange("(b p) j -> p b j", p=P)
        raw_a = sb("raw_a", [P, PACK, P], F32)
        raw_b = sb("raw_b", [P, PACK, P], F32)
        raw_c = placed("raw_c", [P, PACK, PIECE], F32, 36864)
        raw_d = [sb("raw_d%d" % c, [P, PACK, PIECE], F32) for c in range(2)]
        nc.sync.dma_start(out=raw_a[:], in_=dy_view[:, :, 0:P])
        nc.sync.dma_start(out=raw_b[:], in_=dy_view[:, :, P:PIECE])
        pages = [sb("page0", [P, T], F32)]
        w_codes = sb("w_codes", [P, 2 * N], U8)
        w_plane_tile = sb("w_plane", [P, N + 4], U8)
        nc.vector.memset(w_plane_tile[:].bitcast(I32), 0)
        w_plane = w_plane_tile[:, 0:N]
        nc.vector.memset(pages[0][:, 0:CLEAR_ODD], 0.0)
        for q in range(4):
            nc.sync.dma_start(
                out=w_plane[32 * q : 32 * q + 4, :].bitcast(I32), in_=w_scales[0, 4 * q : 4 * q + 4, :].bitcast(I32)
            )
        nc.sync.dma_start(out=raw_c[:], in_=dy_view[:, :, PIECE:HALF])
        nc.sync.dma_start(out=w_codes[:].bitcast(I32), in_=w_words[0].bitcast(I32))
        d_first = [sb("d_first%d" % u, [P, 2, P], F32) for u in range(2)]
        gate = [sb("gate%d" % u, [P, P], F32) for u in range(2)]
        d_next = sb("d_next", [P, 2, PIECE], F32)
        d_second = sb("d_second", [P, BLOCKS, PIECE], F32)
        d_late = sb("d_late", [P, BLOCKS, HALF], F32)
        gate_rows = sb("gate_rows", [P, P], F32)
        nc.sync.dma_start(out=d_first[0][:], in_=d_view[:, 0:2, 0:P])
        nc.sync.dma_start(out=gate[0][:], in_=wgo[:, 0:P])
        nc.sync.dma_start(
            out=gate_rows[:],
            in_=wgo.rearrange("r (u j) -> (r u) j", j=P)[GATE_FIRST : GATE_FIRST + GATE_STEP * (P - 1) + 1 : GATE_STEP, :],
        )
        nc.sync.dma_start(offsets[:], offs)
        nc.sync.dma_start(out=raw_d[0][:], in_=dy_view[:, :, HALF : HALF + PIECE])
        nc.sync.dma_start(out=d_first[1][:], in_=d_view[:, 0:2, P:PIECE])
        nc.sync.dma_start(out=gate[1][:], in_=wgo[:, P:PIECE])
        nc.sync.dma_start(out=raw_d[1][:], in_=dy_view[:, :, HALF + PIECE : J])
        nc.sync.dma_start(out=d_next[:], in_=d_view[:, 2:4, 0:PIECE])
        nc.sync.dma_start(out=d_second[:], in_=d_view[:, :, PIECE:HALF])
        nc.sync.dma_start(out=d_late[:], in_=d_view[:, :, HALF:J])

        ramp = sb("ramp", [P, HALF], BF16)
        nc.gpsimd.iota(
            ramp[:], pattern=[[1, HALF]], base=0, channel_multiplier=-PACK, allow_small_or_imprecise_dtypes=True
        )
        eye = sb("eye", [P, P], F32)
        ones = [placed("ones0", [P, 2 * HALF], BF16, 50176), sb("ones1", [P, 2 * HALF], BF16)]
        eye_codes = sb("eye_codes", [P, PACK * P], U32)
        eye_plane = sb("eye_plane", [P, PACK * P], U8)
        for t in range(PACK):
            nc.vector.tensor_scalar(
                out=ones[t // 2][:, t % 2 * HALF : (t % 2 + 1) * HALF], in0=ramp[:], scalar1=float(t), scalar2=None, op0=ALU.is_equal
            )
        nc.vector.memset(pages[0][:, CLEAR_ODD - 1 : T], 0.0)
        for h in range(2):
            part = slice(h * PIECE, (h + 1) * PIECE)
            nc.vector.quantize_mx(out=eye_codes[:, part].bitcast(E4M3), scales=eye_plane[:, part], in_=ones[h][:])

        early_codes = placed("early_codes", [P, PIECE], U32, 50176)
        q_plane = sb("q_plane", [P, J], U8)
        r_codes = sb("r_codes", [P, J], U32)
        r_plane = sb("r_plane", [P, J], U8)

        def cols(u0, u1):
            return slice(u0 * P, u1 * P)

        def quantise(codes, plane, fmt, src):
            nc.vector.quantize_mx(out=codes.bitcast(fmt), scales=plane, in_=src.rearrange("p j t -> p (j t)"))

        def decode(u, codes, acc):
            for t in range(PACK):
                nc.tensor.matmul_mx(
                    out=acc[:, cols(t, t + 1)], lhsT=eye_codes[:, cols(t, t + 1)].bitcast(E4M3),
                    lhsT_scale=eye_plane[:, cols(t, t + 1)], rhs=codes.bitcast(E5M2), rhs_scale=q_plane[:, cols(u, u + 1)],
                    start=True, stop=True,
                )

        def leftover(engine, dst, src, known, i):
            engine.tensor_tensor(
                out=dst.rearrange("p (c i) t -> p c t i", i=i), in0=src.rearrange("p t (c i) -> p c t i", i=i),
                in1=known.rearrange("p t (c i) -> p c t i", i=i), op=ALU.subtract,
            )

        def turned_pass(tier, u, b0, acc, start, stop):
            codes, plane, fmt = tier(u)
            nc.tensor.matmul_mx(
                out=acc[:, u % 2 * PIECE : (u % 2 + 1) * PIECE], lhsT=codes.bitcast(fmt), lhsT_scale=plane,
                rhs=w_codes[:, 2 * b0 * P : 2 * (b0 + 2) * P].bitcast(E2M1), rhs_scale=w_plane[:, cols(b0, b0 + 2)],
                start=start, stop=stop,
            )

        def turned_passes(tier, u0, b0, acc, start):
            for k in range(2):
                turned_pass(tier, u0 + k, b0, acc, start and k == 0, not start and k == 1)

        def direct_pass(b, codes, plane, fmt, dst, start, stop):
            nc.tensor.matmul_mx(
                out=dst, lhsT=w_codes[:, 2 * b * P : 2 * (b + 1) * P].bitcast(E2M1),
                lhsT_scale=w_plane[:, cols(b, b + 1)], rhs=codes.bitcast(fmt), rhs_scale=plane, start=start, stop=stop,
            )

        def weigh(u, acc, dst, b0=0, count=2):
            at = u % 2 * PIECE + b0 * P
            src4 = acc[:, at : at + count * P].rearrange("p (b g s) -> p b g s", b=count, s=16)
            dst4 = dst[:].rearrange("p (b g s) -> p b g s", b=count, s=16)
            for g in range(GROUPS):
                col = gate_column(u, g)
                nc.scalar.activation(
                    out=dst4[:, :, g, :], in_=src4[:, :, g, :], func=COPY, scale=gate_t[:, col : col + 1]
                )
            return dst

        def turn_pair(weighed, acc):
            for u in range(2):
                for b in range(2):
                    at = b * PIECE + u * P
                    nc.tensor.transpose(acc[:, at : at + P], weighed[u][:, cols(b, b + 1)], eye[:])

        def turn_back(u0, turned, b0, acc, offsets=(None, None)):
            tiles = [
                sb("weighed%d_%d" % (u0 + k, b0), [P, PIECE], F32) if offsets[k] is None
                else placed("weighed%d_%d" % (u0 + k, b0), [P, PIECE], F32, offsets[k])
                for k in range(2)
            ]
            turn_pair([weigh(u0 + k, turned, tiles[k]) for k in range(2)], acc)

        def clear(page):
            nc.gpsimd.memset(page[:], 0.0)
            return page

        def window(b, u0, u1):
            return pages[b][:].indirect(offsets[:, 8 * u0 : 8 * u1])

        def scatter(dst, x, y):
            nc.vector.tensor_tensor(out=dst, in0=x, in1=y, op=ALU.mult)

        def place(dst, x):
            nc.vector.tensor_copy(out=dst, in_=x)

        def first_tier(u0, u1, codes, woven):
            quantise(codes, q_plane[:, cols(u0, u1)], E5M2, woven)

        def second_tier(u0, u1, rest):
            quantise(r_codes[:, cols(u0, u1)], r_plane[:, cols(u0, u1)], E4M3, rest)

        def planes(acc):
            return acc[:].rearrange("p (t j) -> p t j", t=PACK)

        woven_a = sb("woven_a", [P, P, PACK], BF16)
        woven_b = placed("woven_b", [P, P, PACK], BF16, 8192)
        woven_c = placed("woven_c", [P, PIECE, PACK], BF16, 9216)
        weave(nc.scalar.copy, woven_a, raw_a, 0, P)
        q_codes = [early_codes[:, cols(u, u + 1)] for u in range(2)]
        first_tier(0, 1, q_codes[0], woven_a[:])
        pages.append(placed("page1", [P, T], F32, 51200))
        nc.vector.memset(pages[1][:, 0:CLEAR_CUT], 0.0)
        weave(nc.scalar.copy, woven_b, raw_b, 0, P)
        first_tier(1, 2, q_codes[1], woven_b[:])
        nc.vector.memset(pages[1][:, CLEAR_CUT:T], 0.0)
        weave(nc.scalar.copy, woven_c, raw_c, 0, PIECE)
        nc.scalar.copy(out=eye[:], in_=ones[1][:, 2:HALF:PACK])
        decoded = [bank("decoded%d" % u, u) for u in range(2)]
        rest = [
            placed("rest_a", [P, 4 * HALF], BF16, 24576)[:, 0:HALF].rearrange("p (j t) -> p j t", t=PACK),
            placed("rest_b", [P, P, PACK], BF16, 12288)[:],
        ]
        for u in range(2):
            decode(u, q_codes[u], decoded[u])

        def q_of(u):
            return q_codes[u], q_plane[:, cols(u, u + 1)], E5M2

        def r_of(u):
            return r_codes[:, cols(u, u + 1)], r_plane[:, cols(u, u + 1)], E4M3

        leftover(nc.vector, rest[0], raw_a[:], planes(decoded[0]), 2)
        second_tier(0, 1, rest[0])
        direct_a = [bank("direct_a0", 0), bank("direct_a1", 5)]
        direct_pass(0, *q_of(0), direct_a[0][:, 0:P], True, False)
        direct_pass(0, *r_of(0), direct_a[0][:, 0:P], False, True)
        direct_pass(1, *r_of(0), direct_a[1][:, 0:P], True, False)
        direct_pass(1, *q_of(0), direct_a[1][:, 0:P], False, True)
        first_a = [sb("first_a%d" % b, [P, P], F32) for b in range(2)]
        for b in range(2):
            nc.vector.tensor_tensor(out=first_a[b][:], in0=direct_a[b][:, 0:P], in1=d_first[0][:, b, :], op=ALU.mult)
        for h in range(2):
            part = slice(h * P // 2, (h + 1) * P // 2)
            leftover(nc.vector, rest[1][:, part, :], raw_b[:, :, part], planes(decoded[1])[:, :, part], 2)
        second_tier(1, 2, rest[1][:])
        codes_c = placed("codes_c", [P, PIECE], U32, 25600)
        first_tier(2, 4, codes_c[:], woven_c[:])
        q_codes.extend(codes_c[:, cols(k, k + 1)] for k in range(2))
        decoded_c = [bank("decoded_c%d" % k, 5 * k) for k in range(2)]
        for k in range(2):
            decode(2 + k, q_codes[2 + k], decoded_c[k])
        woven_d = [placed("woven_d%d" % c, [P, PIECE, PACK], BF16, (26624, 36864 - 1024)[c]) for c in range(2)]

        def cast_late(c):
            for k in range(2):
                weave(nc.scalar.copy, woven_d[c][:, cols(k, k + 1), :], raw_d[c][:, :, cols(k, k + 1)], 0, P)

        cast_late(0)
        gate_bank = bank("gate_bank", 1)
        gate_t = sb("gate_t", [P, P], F32)
        nc.tensor.transpose(gate_bank[:, 0:P], gate_rows[:], eye[:])
        nc.scalar.copy(out=gate_t[:], in_=gate_bank[:, 0:P])
        direct_b = bank("direct_b", 1)
        for b in range(2):
            direct_pass(b, *q_of(1), direct_b[:, cols(b, b + 1)], b == 0, False)
            direct_pass(b, *r_of(1), direct_b[:, cols(b, b + 1)], False, b == 1)
        turned = bank("turned_ab", 2)
        turned_pass(r_of, 0, 2, turned, True, False)
        turned_pass(q_of, 0, 2, turned, False, False)
        turned_pass(q_of, 1, 2, turned, False, False)
        turned_pass(r_of, 1, 2, turned, False, True)
        pages.append(clear(placed("page2", [P, T], F32, 8192)))
        for b in range(2):
            scatter(window(b, 0, 1), first_a[b][:], gate[0][:])
        back_ab = bank("back_ab", 4)
        turn_back(0, turned, 2, back_ab)

        rest_c = placed("rest_c", [P, PIECE, PACK], BF16, 28672)
        for k in range(2):
            leftover(nc.vector, rest_c[:, cols(k, k + 1), :], raw_c[:, :, cols(k, k + 1)], planes(decoded_c[k]), 2)
        cast_late(1)
        first_b = sb("first_b", [P, 2, P], F32)
        nc.vector.tensor_tensor(
            out=first_b[:], in0=direct_b[:, 0:PIECE].rearrange("p (b j) -> p b j", b=2), in1=d_first[1][:],
            op=ALU.mult,
        )
        codes_d0 = placed("codes_d0", [P, PIECE], U32, 36864 + 1024)
        first_tier(4, 6, codes_d0[:], woven_d[0][:])
        q_codes.extend(codes_d0[:, cols(k, k + 1)] for k in range(2))
        second_tier(2, 4, rest_c[:])
        known = []

        def learn(u, index, offset):
            acc = bank("decoded_d%d" % u, index)
            decode(u, q_codes[u], acc)
            known.append(placed("known%d" % u, [P, HALF], F32, offset))
            nc.scalar.copy(
                out=known[u - 4][:].rearrange("p (j t) -> p j t", t=PACK), in_=planes(acc).rearrange("p t j -> p j t")
            )

        turned = bank("turned_c0", 0)
        turned_passes(q_of, 2, 0, turned, True)
        learn(4, 5, 40960)
        turned_passes(r_of, 2, 0, turned, False)
        scatter(window(0, 1, 2), first_b[:, 0, :], gate[1][:])
        values_ab = placed("values_ab", [P, 2, PIECE], F32, 36864 + 2048)
        scatter(window(1, 1, 2), first_b[:, 1, :], gate[1][:])
        for b in range(2):
            nc.vector.tensor_tensor(
                out=values_ab[:, b, :], in0=back_ab[:, b * PIECE : (b + 1) * PIECE], in1=d_next[:, b, :], op=ALU.mult
            )
        pages.append(clear(placed("page3", [P, T], F32, 26624)))
        for b in range(2):
            place(window(2 + b, 0, 2), values_ab[:, b, :])
        back_c = [bank("back_c%d" % k, 2 + k) for k in range(2)]
        turn_back(2, turned, 0, back_c[0], (None, 63488))
        backs = sb("backs", [P, BLOCKS, PIECE], F32)
        nc.scalar.copy(out=backs[:, 0, :], in_=back_c[0][:, 0:PIECE])
        learn(5, 5, 63488)
        nc.scalar.copy(out=backs[:, 1, :], in_=back_c[0][:, PIECE:HALF])
        turned = bank("turned_c1", 0)
        turned_passes(q_of, 2, 2, turned, True)
        turned_passes(r_of, 2, 2, turned, False)
        turn_back(2, turned, 2, back_c[1])
        nc.scalar.copy(out=backs[:, 2:4, :], in_=back_c[1][:].rearrange("p (b j) -> p b j", b=2))

        def times_d(dst, b):
            nc.gpsimd.tensor_tensor(out=dst, in0=backs[:, b, :], in1=d_second[:, b, :], op=ALU.mult)
            place(window(b, 2, 4), dst)

        def late_leftover(k, late):
            part = cols(k % 2, k % 2 + 1)
            nc.gpsimd.tensor_tensor(
                out=late[:, part, :], in0=raw_d[k // 2][:, :, part].rearrange("p t j -> p j t"),
                in1=known[k][:].rearrange("p (j t) -> p j t", t=PACK), op=ALU.subtract,
            )

        low = [bank("turned_d0", 5)]
        turned_passes(q_of, 4, 0, low[0], True)
        late = placed("late0", [P, PIECE, PACK], BF16, 45056)
        late_leftover(0, late)
        times_d(placed("values_c0", [P, PIECE], F32, 40960)[:], 0)
        late_leftover(1, late)
        codes_d1 = placed("codes_d1", [P, PIECE], U32, 63488 + 1024)
        first_tier(6, 8, codes_d1[:], woven_d[1][:])
        second_tier(4, 6, late[:])
        q_codes.extend(codes_d1[:, cols(k, k + 1)] for k in range(2))
        times_d(placed("values_c1", [P, PIECE], F32, 63488)[:], 1)
        for u in (6, 7):
            learn(u, u, 47104 + 2048 * (u % 2))
        turned_passes(r_of, 4, 0, low[0], False)
        for b in (2, 3):
            times_d(placed("values_c%d" % b, [P, PIECE], F32, 45056 + 1024 * (b - 2))[:], b)
        late = sb("late1", [P, PIECE, PACK], BF16)
        for k in range(2, 4):
            late_leftover(k, late)
        second_tier(6, 8, late[:])

        values_lo = sb("values_lo", [P, 2, HALF], F32)
        values_hi = placed("values_hi", [P, 2, HALF], F32, 69632 - 4096 + 256)

        def turn(c, b0, turned, index, offsets=(None, None)):
            acc = bank("back_d%d_%d" % (c, b0), index)
            turn_back(4 + 2 * c, turned, b0, acc, offsets)
            return acc

        def bring(c, b0, acc):
            for b in range(2):
                nc.scalar.copy(out=(values_lo, values_hi)[b0 // 2][:, b, cols(2 * c, 2 * c + 2)], in_=acc[:, b * PIECE : (b + 1) * PIECE])

        def upper(c, index):
            turned = bank("turned_high%d" % c, index)
            turned_passes(r_of, 4 + 2 * c, 2, turned, True)
            turned_passes(q_of, 4 + 2 * c, 2, turned, False)
            return turned

        accs = [turn(0, 0, low[0], 1), turn(0, 2, upper(0, 6), 4)]
        bring(0, 0, accs[0])
        low.append(bank("turned_d1", 7))
        turned_passes(q_of, 6, 0, low[1], True)
        turned_passes(r_of, 6, 0, low[1], False)
        for b in range(2):
            scatter(window(b, 4, 6), values_lo[:, b, 0:PIECE], d_late[:, b, 0:PIECE])
        ends = [bank("back_last%d" % b, (2, 5)[b]) for b in range(2)]
        for b in range(2):
            acc = ends[b]
            for k in range(2):
                single = placed("single%d_%d" % (b, k), [P, P], F32, 69632 + 1024 * b + 512 * k)
                nc.tensor.transpose(acc[:, cols(k, k + 1)], weigh(6 + k, low[1], single, b, 1)[:], eye[:])
        for b in range(2):
            nc.scalar.copy(out=values_lo[:, b, PIECE:HALF], in_=ends[b][:, 0:PIECE])
        last = turn(1, 2, upper(1, 0), 3, (71424 - 1024, 71424))
        bring(0, 2, accs[1])
        bring(1, 2, last)
        for b in range(2):
            scatter(window(b, 6, 8), values_lo[:, b, PIECE:HALF], d_late[:, b, PIECE:HALF])
            nc.sync.dma_start(out=out[b * P : (b + 1) * P, :], in_=pages[b][:])
        for b in (2, 3):
            scatter(window(b, 4, 8), values_hi[:, b - 2, :], d_late[:, b, :])
            nc.sync.dma_start(out=out[b * P : (b + 1) * P, :], in_=pages[b][:])
